import numpy as np
import ml_dtypes


def mxq(x, axis, fmt="e4m3"):
    dtype, down = {"e4m3": (ml_dtypes.float8_e4m3fn, 7), "e5m2": (ml_dtypes.float8_e5m2, 14)}[fmt]
    v = np.moveaxis(np.asarray(x, np.float32).astype(ml_dtypes.bfloat16).astype(np.float64), axis, -1)
    blocks = v.reshape(v.shape[:-1] + (-1, 32))
    amax = np.abs(blocks).max(-1, keepdims=True)
    byte = np.maximum(np.where(amax > 0, np.frexp(amax)[1] - 1 + 127, 0) - down, 1)
    scale = np.exp2(byte - 127.0)
    codes = (blocks / scale).astype(np.float32).astype(dtype).astype(np.float64)
    return np.moveaxis((codes * scale).reshape(v.shape), -1, axis)


WIDE = False


def mx_kscale(k):
    if not WIDE:
        return np.ones(k)
    levels = np.array([10, -10, 5, -5, 0])
    if k % 512:
        return np.exp2(np.random.permutation(np.resize(levels, k // 32))).repeat(32)
    a = np.empty((k // 512, 16))
    for p in range(k // 512):
        a[p, :8] = np.random.permutation(np.resize(levels, 8))
        for g in range(8):
            far = levels[np.abs(levels - a[p, g]) >= 10]
            a[p, g + 8] = far[np.random.randint(len(far))]
    return np.exp2(a.ravel()).repeat(32)


BF16 = ml_dtypes.bfloat16


def bf(x):
    return np.asarray(x, np.float32).astype(BF16)


def f64(x):
    return np.asarray(x).astype(np.float64)


E2M1 = np.array([0.0, 0.5, 1.0, 1.5, 2.0, 3.0, 4.0, 6.0, -0.0, -0.5, -1.0, -1.5, -2.0, -3.0, -4.0, -6.0])


def pack_weight(w, fmt):
    k, n = w.shape
    w = f64(bf(w)).reshape(k // 32, 32, n)
    amax = np.abs(w).max(1)
    if fmt == "e4m3":
        byte = np.frexp(amax)[1] - 1 + 127 - 7
    else:
        mant, ex = np.frexp(amax / 6.0)
        byte = np.where(mant > 0.5, ex, ex - 1) + 127
    byte = np.clip(np.where(amax > 0, byte, 1), 1, 254)
    scaled = (w * np.exp2(127.0 - byte)[:, None, :]).reshape(k, n).astype(np.float32)
    by_word = np.ascontiguousarray(scaled.reshape(k // 512, 128, 4, n).transpose(0, 1, 3, 2))
    if fmt == "e4m3":
        words = by_word.astype(ml_dtypes.float8_e4m3fn).view(np.uint8)
    else:
        c = by_word.astype(ml_dtypes.float4_e2m1fn).view(np.uint8) & 0xF
        words = c[..., 0::2] | (c[..., 1::2] << 4)
    return np.ascontiguousarray(words), np.ascontiguousarray(byte.astype(np.uint8).reshape(k // 512, 16, n))


def unpack_weight(words, scales, fmt):
    g, p, n, _ = words.shape
    if fmt == "e4m3":
        vals = np.ascontiguousarray(words).view(ml_dtypes.float8_e4m3fn).astype(np.float64)
    else:
        nib = np.empty((g, p, n, 4), np.uint8)
        nib[..., 0::2] = words & 0xF
        nib[..., 1::2] = words >> 4
        vals = E2M1[nib]
    vals = vals * np.repeat(np.exp2(scales.astype(np.float64) - 127.0), 8, axis=1)[..., None]
    return vals.transpose(0, 1, 3, 2).reshape(g * 512, n)
def pack4(w):
    words, scales = pack_weight(w, "e2m1")
    return words.reshape(words.shape[0], 128, -1), scales


def unpack4(words, scales):
    return unpack_weight(words.reshape(words.shape[0], 128, -1, 2), scales, "e2m1")


E, L, A, F = 2048, 1024, 1536, 512


def draw0():
    s = mx_kscale(L)
    u = mx_kscale(E)
    d = np.random.standard_normal((E, L)) * s * u[:, None]
    basis = np.random.standard_normal((L, A)) / np.sqrt(L) / s[:, None]
    r = 1.5 * np.random.standard_normal(E)
    frozen = np.random.standard_normal((E, F)) / np.sqrt(E) / u[:, None]
    ja_words, ja_scales = pack4(frozen)
    return {"d": bf(d),
            "basis": bf(basis),
            "r": bf(r),
            "ja_words": ja_words,
            "ja_scales": ja_scales}


def core(d, basis, r, ja_words, ja_scales):
    jb = mxq(f64(d), 1, "e4m3") @ mxq(f64(basis), 0, "e4m3")
    rr = f64(r)[:, None]
    wj = jb / (1.0 + rr * rr)
    ja = unpack4(ja_words, ja_scales)
    h = ja.T @ mxq(wj, 0, "e4m3")
    return h


def e4m3fn_bytes(y):
    return np.clip(np.asarray(y, np.float64), -448.0, 448.0).astype(np.float32).astype(ml_dtypes.float8_e4m3fn).view(np.uint8)


def e4m3fn_values(b):
    return np.asarray(b, np.uint8).view(ml_dtypes.float8_e4m3fn).astype(np.float64)


def setup_inputs():
    d = draw0()
    x0 = np.asarray(d['basis']).astype(np.float64)
    s = (np.max(np.abs(x0), axis=(1,), keepdims=True) / 448.0).astype(np.float32)
    out = {}
    for k, v in d.items():
        if k == 'basis':
            out['basis_bytes'] = e4m3fn_bytes(x0 / s.astype(np.float64))
            out['basis_scale'] = s
        else:
            out[k] = v
    return out


def reference(d, basis_bytes, basis_scale, r, ja_words, ja_scales):
    return core(d, e4m3fn_values(basis_bytes) * basis_scale.astype(np.float64), r, ja_words, ja_scales)

@@ -1,0 +1,365 @@
+from contextlib import ExitStack
+
+import concourse.mybir as mybir
+from concourse.masks import make_identity
+
+E, L, A, F = 2048, 1024, 1536, 512
+FLOPS = 2 * E * L * A + 2 * E * A * F
+
+F32 = mybir.dt.float32
+BF16 = mybir.dt.bfloat16
+I32 = mybir.dt.int32
+U32 = mybir.dt.uint32
+U8 = mybir.dt.uint8
+FP8 = mybir.dt.float8_e4m3fn
+FP8X4 = mybir.dt.float8_e4m3fn_x4
+FP4X4 = mybir.dt.float4_e2m1fn_x4
+MULT = mybir.AluOpType.mult
+ADD = mybir.AluOpType.add
+COPY = mybir.ActivationFunctionType.Copy
+
+P = 128
+T = 4
+S = L // (P * T)
+G = E // (P * T)
+W = 512
+J = A // W
+R = F // P
+STEPS = J * G * T
+
+PIECES = [(0, 0, 256), (0, 256, 256), (1, 0, 512), (2, 0, 512)]
+
+ROUNDS = [(0, g, "0000") for g in range(G)] + [(j, g, "01010101") for j in (1, 2) for g in (0, 2)]
+ROUNDS[-1] = (2, 2, "11101000")
+
+
+def tile_robust_information_block_s13_kernel(tc, d, basis_bytes, basis_scale, r, ja_words, ja_scales, out):
+    nc = tc.nc
+    with ExitStack() as ctx:
+        keep = ctx.enter_context(tc.tile_pool(name="keep", bufs=1))
+        convert = ctx.enter_context(tc.tile_pool(name="convert", bufs=3))
+        stage = ctx.enter_context(tc.tile_pool(name="stage", bufs=4))
+        psum = ctx.enter_context(tc.psum_pool(name="psum", bufs=1))
+        ctx.enter_context(tc.manual_schedule())
+
+        def bank(k):
+            return psum.tile([P, W], F32, name="bank_%d" % k)
+
+        ident = keep.tile([P, P], F32, name="ident")
+        make_identity(nc, ident[:])
+        zeros = keep.tile([P, W], BF16, name="zeros")
+        nc.vector.memset(zeros[:], 0.0)
+        ja_scale = keep.tile([P, G * F], U8, name="ja_scale", align_bytes=64)
+        nc.gpsimd.memset(ja_scale[:].bitcast(I32), 0)
+
+        row_scale = keep.tile([P, S, T], F32, name="row_scale")
+        nc.scalar.dma_start(out=row_scale[:], in_=basis_scale.rearrange("(s p t) o -> p s (t o)", p=P, t=T))
+        table = keep.tile([P, 1], F32, name="table")
+        nc.scalar.activation(out=table[:], in_=zeros[:, 0:1], func=COPY)
+
+        code_rows = basis_bytes.rearrange("(s p t) n -> s p t n", p=P, t=T)
+        codes_first = [keep.tile([P, T, W], U8, name="codes_first_%d" % s) for s in range(S)]
+        codes_rest = [keep.tile([P, T, A - W], U8, name="codes_rest_%d" % s) for s in range(S)]
+        d_rows = d.rearrange("(g p t) k -> g p t k", p=P, t=T)
+        d_raw = [keep.tile([P, T, L], BF16, name="d_raw_%d" % g) for g in range(G)]
+
+        def load_d(g, t, n):
+            nc.sync.dma_start(out=d_raw[g][:, t : t + n, :], in_=d_rows[g][:, t : t + n, :])
+
+        for s in range(S):
+            nc.sync.dma_start(out=codes_first[s][:], in_=code_rows[s][:, :, :W])
+            load_d(0, 2 * s, 1)
+            if s == 0:
+                load_d(0, 1, 1)
+        load_d(0, 3, 1)
+        load_d(1, 0, 2)
+        load_d(1, 2, 2)
+        residual = keep.tile([P, G, T], BF16, name="residual")
+        nc.sync.dma_start(out=residual[:], in_=r.rearrange("(g p t) -> p g t", p=P, t=T))
+        for s in range(S):
+            nc.sync.dma_start(out=codes_rest[s][:], in_=code_rows[s][:, :, W:])
+        for g in (2, 3):
+            load_d(g, 0, 2)
+            load_d(g, 2, 2)
+        ja = keep.tile([P, G, 2 * F], U8, name="ja", align_bytes=64)
+        nc.sync.dma_start(out=ja[:], in_=ja_words.rearrange("g p n -> p g n"))
+        for q in range(4):
+            nc.sync.dma_start(
+                out=ja_scale[32 * q : 32 * q + 4, :].rearrange("p (g n) -> p g n", g=G).bitcast(I32),
+                in_=ja_scales[:, 4 * q : 4 * q + 4, :].rearrange("g q n -> q g n").bitcast(I32),
+            )
+
+        basis_q = [keep.tile([P, S * W], U32, name="basis_q_%d" % j, align_bytes=64) for j in range(J)]
+        basis_s = [keep.tile([P, S * W], U8, name="basis_s_%d" % j, align_bytes=64) for j in range(J)]
+        d_q = [keep.tile([P, T * S * P], U32, name="d_q_%d" % g, align_bytes=64) for g in range(G)]
+        d_s = [keep.tile([P, T * S * P], U8, name="d_s_%d" % g, align_bytes=64) for g in range(G)]
+        wj_q = [[keep.tile([P, W], U32, name="wj_q_%d_%d" % (j, g), align_bytes=64) for g in range(G)] for j in range(J)]
+        wj_s = [[keep.tile([P, W], U8, name="wj_s_%d_%d" % (j, g), align_bytes=64) for g in range(G)] for j in range(J)]
+
+        def copy_on(engine, dst, src):
+            if engine == "vector":
+                nc.vector.tensor_copy(out=dst, in_=src)
+            else:
+                nc.scalar.copy(out=dst, in_=src)
+
+        def interleave_on(engine, dst, src):
+            copy_on(
+                engine,
+                dst.rearrange("p (c i) t -> p c t i", i=4),
+                src.rearrange("p t (c i) -> p c t i", i=4),
+            )
+
+        weight = keep.tile([P, G * T], F32, name="weight")
+
+        def make_weights():
+            values = residual[:].rearrange("p g t -> p (g t)")
+            square = keep.tile([P, G * T], F32, name="square")
+            nc.vector.tensor_tensor(out=square[:], in0=values, in1=values, op=MULT)
+            denominator = keep.tile([P, G * T], F32, name="denominator")
+            nc.vector.tensor_scalar(out=denominator[:], in0=square[:], scalar1=1.0, scalar2=None, op0=ADD)
+            nc.vector.reciprocal(out=weight[:], in_=denominator[:])
+
+        plane = {}
+        interleaved = {}
+
+        def widen(i, s, t, engine):
+            j, c, n = PIECES[i]
+            if (i, s) not in plane:
+                plane[i, s] = convert.tile([P, T, W], BF16, name="plane", align_bytes=64)
+            if j == 0:
+                codes = codes_first[s][:, t, c : c + n]
+            else:
+                codes = codes_rest[s][:, t, W * (j - 1) : W * j]
+            dst = plane[i, s][:, t, :n]
+            scale = row_scale[:, s, t : t + 1]
+            if engine == "vector":
+                nc.vector.tensor_scalar(out=dst, in0=codes.bitcast(FP8), scalar1=scale, scalar2=None, op0=MULT)
+            else:
+                nc.scalar.activation(out=dst, in_=codes.bitcast(FP8), func=COPY, scale=scale)
+
+        def interleave_basis(i, s, engine):
+            n = PIECES[i][2]
+            interleaved[i, s] = convert.tile([P, W, T], BF16, name="interleaved", align_bytes=64)
+            interleave_on(engine, interleaved[i, s][:, :n, :], plane[i, s][:, :, :n])
+
+        def quantize_basis(i, s):
+            j, c, n = PIECES[i]
+            c += s * W
+            nc.vector.quantize_mx(
+                out=basis_q[j][:, c : c + n].bitcast(FP8X4),
+                scales=basis_s[j][:, c : c + n],
+                in_=interleaved[i, s][:, :n, :].rearrange("p n t -> p (n t)"),
+            )
+
+        sorted_d = {}
+        d_bank = {}
+        d_grouped = {}
+
+        def sort_words(g, t):
+            sorted_d[g, t] = stage.tile([P, L], BF16, name="sorted_d")
+            nc.vector.tensor_copy(
+                out=sorted_d[g, t][:].bitcast(F32).rearrange("p (s u q) -> p s u q", s=S, u=2),
+                in_=d_raw[g][:, t, :].bitcast(F32).rearrange("p (s q u) -> p s u q", s=S, u=2),
+            )
+
+        def transpose_d(g, t):
+            d_bank[g, t] = bank(4 + t)
+            for s in range(S):
+                for u in range(2):
+                    o = (2 * s + u) * P
+                    if (g, t) in sorted_d:
+                        words = sorted_d[g, t][:].bitcast(F32)[:, o : o + P]
+                    else:
+                        words = d_raw[g][:, t, :].bitcast(F32)[:, 2 * P * s + u : 2 * P * (s + 1) : 2]
+                    nc.tensor.transpose(d_bank[g, t][:, o : o + P], words, ident[:])
+
+        def copy_d(g, t):
+            d_grouped[g, t] = stage.tile([P, S * P * T], BF16, name="d_grouped", align_bytes=64)
+            nc.scalar.copy(
+                out=d_grouped[g, t][:].bitcast(F32).rearrange("p (s e u) -> p s e u", s=S, u=2),
+                in_=d_bank[g, t][:].rearrange("p (s u e) -> p s e u", s=S, u=2),
+            )
+
+        def quantize_d(g, t):
+            columns = slice(t * S * P, (t + 1) * S * P)
+            nc.vector.quantize_mx(
+                out=d_q[g][:, columns].bitcast(FP8X4), scales=d_s[g][:, columns], in_=d_grouped[g, t][:]
+            )
+
+        by_vector = [(0, 0), (0, 1), (0, 2)]
+        steps = []
+        for j, g0, turns in ROUNDS:
+            for i, turn in enumerate(turns):
+                steps.append((j, g0 + int(turn), turns[:i].count(turn)))
+        jb_bank = {}
+        wj_plane = {}
+        wj = {}
+
+        def product(dst, j, g, t, c, n):
+            for s in range(S):
+                stationary = slice((t * S + s) * P, (t * S + s + 1) * P)
+                moving = slice(s * W + c, s * W + c + n)
+                nc.tensor.matmul_mx(
+                    out=dst,
+                    lhsT=d_q[g][:, stationary].bitcast(FP8X4),
+                    lhsT_scale=d_s[g][:, stationary],
+                    rhs=basis_q[j][:, moving].bitcast(FP8X4),
+                    rhs_scale=basis_s[j][:, moving],
+                    start=(s == 0),
+                    stop=(s == S - 1),
+                )
+
+        def stage_1(step):
+            j, g, b = steps[step]
+            jb_bank[step] = bank(step % 4)
+            if (j, g) in by_vector:
+                for t in range(T):
+                    product(jb_bank[step][:, t * P : (t + 1) * P], j, g, t, b * P, P)
+            else:
+                product(jb_bank[step][:], j, g, b, 0, W)
+
+        def empty(step):
+            j, g, b = steps[step]
+            if (j, g) in by_vector:
+                if b == 0:
+                    wj[j, g] = stage.tile([P, W, T], BF16, name="wj", align_bytes=64)
+                nc.vector.tensor_tensor(
+                    out=wj[j, g][:, b * P : (b + 1) * P, :],
+                    in0=jb_bank[step][:].rearrange("p (t n) -> p n t", t=T),
+                    in1=weight[:, g * T : (g + 1) * T].unsqueeze(1).to_broadcast([P, P, T]),
+                    op=MULT,
+                )
+            else:
+                if b == 0:
+                    wj_plane[j, g] = stage.tile([P, T, W], BF16, name="wj_plane", align_bytes=64)
+                nc.scalar.activation(
+                    out=wj_plane[j, g][:, b, :],
+                    in_=jb_bank[step][:],
+                    func=COPY,
+                    scale=weight[:, g * T + b : g * T + b + 1],
+                )
+
+        def interleave_wj(j, g):
+            wj[j, g] = stage.tile([P, W, T], BF16, name="wj", align_bytes=64)
+            interleave_on("vector", wj[j, g][:], wj_plane[j, g][:])
+
+        def quantize_wj(j, g):
+            nc.vector.quantize_mx(
+                out=wj_q[j][g][:].bitcast(FP8X4),
+                scales=wj_s[j][g][:],
+                in_=wj[j, g][:].rearrange("p n t -> p (n t)"),
+            )
+
+        h_bank = {}
+
+        def stage_2(j, f):
+            h_bank[j, f] = bank(f if j == J - 1 else 4 + f)
+            for g in range(G):
+                nc.tensor.matmul_mx(
+                    out=h_bank[j, f][:],
+                    lhsT=ja[:, g, 2 * P * f : 2 * P * (f + 1)].bitcast(FP4X4),
+                    lhsT_scale=ja_scale[:, g * F + f * P : g * F + (f + 1) * P],
+                    rhs=wj_q[j][g][:].bitcast(FP8X4),
+                    rhs_scale=wj_s[j][g][:],
+                    start=(g == 0),
+                    stop=(g == G - 1),
+                )
+
+        def store(j, f, parts):
+            h = stage.tile([P, W], F32, name="h")
+            for engine, c, n in parts:
+                copy_on(engine, h[:, c : c + n], h_bank[j, f][:, c : c + n])
+            for engine, c, n in parts:
+                nc.sync.dma_start(out=out[f * P : (f + 1) * P, j * W + c : j * W + c + n], in_=h[:, c : c + n])
+
+        def keep_clock(n):
+            for k in range(n):
+                nc.tensor.matmul(out=bank(k % 4)[:], lhsT=zeros[:, :P], rhs=zeros[:], start=True, stop=True)
+
+        keep_clock(6)
+        for t in range(3):
+            widen(0, 0, t, "vector")
+        widen(0, 0, 3, "scalar")
+        for t in range(T):
+            widen(0, 1, t, "vector" if t < 2 else "scalar")
+        for s in range(S):
+            interleave_basis(0, s, "vector")
+        for t in range(0, T, 2):
+            transpose_d(0, t)
+            transpose_d(0, t + 1)
+            keep_clock(2)
+        for s in range(S):
+            quantize_basis(0, s)
+        for t in range(T):
+            copy_d(0, t)
+        for t in range(T):
+            widen(1, t // 2, 2 * (t % 2), "vector")
+            widen(1, t // 2, 2 * (t % 2) + 1, "vector")
+            quantize_d(0, t)
+        make_weights()
+        for s in range(S):
+            interleave_basis(1, s, "vector")
+
+        work = {}
+
+        def before(step, job, *args):
+            work.setdefault(step, []).append((job, args))
+
+        for s in range(S):
+            before(1, quantize_basis, 1, s)
+        for g in range(1, G):
+            for t in range(T):
+                run = max(0, 4 * g - 5 + 2 * (t // 2))
+                if g == 3 and t >= 2:
+                    before(run - 3, sort_words, g, t)
+                before(run, transpose_d, g, t)
+                before(run, copy_d, g, t)
+                before(run + 1, quantize_d, g, t)
+        for t in range(T):
+            before(t, widen, 2, 0, t, "scalar")
+            before(3 + t, widen, 2, 1, t, "scalar")
+            before(7 + 2 * t, widen, 3, 0, t, "scalar" if t < 2 else "vector")
+            before(16 + 2 * t, widen, 3, 1, t, "vector")
+        before(5, interleave_basis, 2, 0, "vector")
+        before(8, quantize_basis, 2, 0)
+        before(10, interleave_basis, 2, 1, "scalar")
+        before(13, quantize_basis, 2, 1)
+        for s in range(S):
+            before(23, interleave_basis, 3, s, "vector")
+            before(32, quantize_basis, 3, s)
+        before(21, interleave_wj, 0, 3)
+        for g in range(G):
+            before(4 * g + 18, quantize_wj, 0, g)
+        for j in (1, 2):
+            for g in range(G):
+                end = 16 * j + 8 * (g // 2 + 1)
+                if end < STEPS:
+                    before(end + 5 + g % 2, interleave_wj, j, g)
+                    before(end + 6 + g % 2, quantize_wj, j, g)
+        before(46, interleave_wj, 2, 3)
+        before(47, quantize_wj, 2, 3)
+        for f in range(R):
+            before(31, stage_2, 0, f)
+            before(32, store, 0, f, [("vector", 0, W)])
+        before(45, stage_2, 1, 0)
+        before(46, store, 1, 0, [("vector", 0, W)])
+
+        for step in range(STEPS):
+            for job, args in work.get(step, []):
+                job(*args)
+            stage_1(step)
+            if step > 0:
+                empty(step - 1)
+        empty(STEPS - 1)
+
+        interleave_wj(2, 2)
+        quantize_wj(2, 2)
+        for f in range(1, R):
+            stage_2(1, f)
+            store(1, f, [("vector", 0, W)])
+        for f in range(R):
+            stage_2(2, f)
+            if f < R - 1:
+                store(2, f, [("vector" if f % 2 else "scalar", 0, W)])
+            else:
+                store(2, f, [("vector", W // 2, W // 2), ("scalar", 0, W // 2)])

@@ -25,25 +25,24 @@ G = E // (P * T)
 W = 512
 J = A // W
 R = F // P
-STEPS = J * G * T
 
-PIECES = [(0, 0, 256), (0, 256, 256), (1, 0, 512), (2, 0, 512)]
-
-ROUNDS = [(0, g, "0000") for g in range(G)] + [(j, g, "01010101") for j in (1, 2) for g in (0, 2)]
-ROUNDS[-1] = (2, 2, "11101000")
+PIECES = [(0, 256), (256, 256), (512, 512), (1024, 512)]
+DEPTH = {"bank": 8, "plane": 4, "interleaved": 3, "sorted_d": 4, "d_grouped": 6, "wj_plane": 8, "wj": 3, "h": 6}
 
 
 def tile_robust_information_block_s13_kernel(tc, d, basis_bytes, basis_scale, r, ja_words, ja_scales, out):
     nc = tc.nc
     with ExitStack() as ctx:
         keep = ctx.enter_context(tc.tile_pool(name="keep", bufs=1))
-        convert = ctx.enter_context(tc.tile_pool(name="convert", bufs=3))
-        stage = ctx.enter_context(tc.tile_pool(name="stage", bufs=4))
-        psum = ctx.enter_context(tc.psum_pool(name="psum", bufs=1))
+        stage = ctx.enter_context(tc.tile_pool(name="stage", bufs=1))
+        psum = ctx.enter_context(tc.psum_pool(name="psum", bufs=DEPTH["bank"]))
         ctx.enter_context(tc.manual_schedule())
 
-        def bank(k):
-            return psum.tile([P, W], F32, name="bank_%d" % k)
+        def staged(name, shape, dtype):
+            return stage.tile(shape, dtype, name=name, bufs=DEPTH[name], align_bytes=64)
+
+        def bank():
+            return psum.tile([P, W], F32, name="bank")
 
         ident = keep.tile([P, P], F32, name="ident")
         make_identity(nc, ident[:])
@@ -58,29 +57,47 @@ def tile_robust_information_block_s13_kernel(tc, d, basis_bytes, basis_scale, r,
         nc.scalar.activation(out=table[:], in_=zeros[:, 0:1], func=COPY)
 
         code_rows = basis_bytes.rearrange("(s p t) n -> s p t n", p=P, t=T)
-        codes_first = [keep.tile([P, T, W], U8, name="codes_first_%d" % s) for s in range(S)]
-        codes_rest = [keep.tile([P, T, A - W], U8, name="codes_rest_%d" % s) for s in range(S)]
         d_rows = d.rearrange("(g p t) k -> g p t k", p=P, t=T)
-        d_raw = [keep.tile([P, T, L], BF16, name="d_raw_%d" % g) for g in range(G)]
+        codes = {}
+        d_raw = {}
 
-        def load_d(g, t, n):
-            nc.sync.dma_start(out=d_raw[g][:, t : t + n, :], in_=d_rows[g][:, t : t + n, :])
+        def load_codes(first, last, s):
+            c0 = PIECES[first][0]
+            c1 = PIECES[last][0] + PIECES[last][1]
+            tile = keep.tile([P, T, c1 - c0], U8, name="codes_%d_%d" % (first, s))
+            nc.sync.dma_start(out=tile[:], in_=code_rows[s][:, :, c0:c1])
+            for i in range(first, last + 1):
+                c, n = PIECES[i]
+                for t in range(T):
+                    codes[i, s, t] = tile[:, t, c - c0 : c - c0 + n]
+
+        def load_d(g, t0, n):
+            tile = keep.tile([P, n, L], BF16, name="d_raw_%d_%d" % (g, t0))
+            nc.sync.dma_start(out=tile[:], in_=d_rows[g][:, t0 : t0 + n, :])
+            for t in range(n):
+                d_raw[g, t0 + t] = tile[:, t, :]
+
+        residual = keep.tile([P, G, T], BF16, name="residual")
+
+        def load_r():
+            nc.sync.dma_start(out=residual[:], in_=r.rearrange("(g p t) -> p g t", p=P, t=T))
 
         for s in range(S):
-            nc.sync.dma_start(out=codes_first[s][:], in_=code_rows[s][:, :, :W])
-            load_d(0, 2 * s, 1)
-            if s == 0:
-                load_d(0, 1, 1)
-        load_d(0, 3, 1)
+            load_codes(0, 0, s)
+        for t in range(T):
+            load_d(0, t, 1)
+            if t == 1:
+                load_r()
         load_d(1, 0, 2)
         load_d(1, 2, 2)
-        residual = keep.tile([P, G, T], BF16, name="residual")
-        nc.sync.dma_start(out=residual[:], in_=r.rearrange("(g p t) -> p g t", p=P, t=T))
         for s in range(S):
-            nc.sync.dma_start(out=codes_rest[s][:], in_=code_rows[s][:, :, W:])
+            load_codes(1, 1, s)
         for g in (2, 3):
             load_d(g, 0, 2)
             load_d(g, 2, 2)
+        for i in (2, 3):
+            for s in range(S):
+                load_codes(i, i, s)
         ja = keep.tile([P, G, 2 * F], U8, name="ja", align_bytes=64)
         nc.sync.dma_start(out=ja[:], in_=ja_words.rearrange("g p n -> p g n"))
         for q in range(4):
@@ -89,18 +106,26 @@ def tile_robust_information_block_s13_kernel(tc, d, basis_bytes, basis_scale, r,
                 in_=ja_scales[:, 4 * q : 4 * q + 4, :].rearrange("g q n -> q g n").bitcast(I32),
             )
 
-        basis_q = [keep.tile([P, S * W], U32, name="basis_q_%d" % j, align_bytes=64) for j in range(J)]
-        basis_s = [keep.tile([P, S * W], U8, name="basis_s_%d" % j, align_bytes=64) for j in range(J)]
+        basis_q = [keep.tile([P, A], U32, name="basis_q_%d" % s, align_bytes=64) for s in range(S)]
+        basis_s = [keep.tile([P, A], U8, name="basis_s_%d" % s, align_bytes=64) for s in range(S)]
         d_q = [keep.tile([P, T * S * P], U32, name="d_q_%d" % g, align_bytes=64) for g in range(G)]
         d_s = [keep.tile([P, T * S * P], U8, name="d_s_%d" % g, align_bytes=64) for g in range(G)]
         wj_q = [[keep.tile([P, W], U32, name="wj_q_%d_%d" % (j, g), align_bytes=64) for g in range(G)] for j in range(J)]
         wj_s = [[keep.tile([P, W], U8, name="wj_s_%d_%d" % (j, g), align_bytes=64) for g in range(G)] for j in range(J)]
+
+        made = {}
 
         def copy_on(engine, dst, src):
             if engine == "vector":
                 nc.vector.tensor_copy(out=dst, in_=src)
             else:
                 nc.scalar.copy(out=dst, in_=src)
+
+        def scale_on(engine, dst, src, scale):
+            if engine == "vector":
+                nc.vector.tensor_scalar(out=dst, in0=src, scalar1=scale, scalar2=None, op0=MULT)
+            else:
+                nc.scalar.activation(out=dst, in_=src, func=COPY, scale=scale)
 
         def interleave_on(engine, dst, src):
             copy_on(
@@ -109,257 +134,263 @@ def tile_robust_information_block_s13_kernel(tc, d, basis_bytes, basis_scale, r,
                 src.rearrange("p t (c i) -> p c t i", i=4),
             )
 
+        square = keep.tile([P, G * T], F32, name="square")
+        denominator = keep.tile([P, G * T], F32, name="denominator")
         weight = keep.tile([P, G * T], F32, name="weight")
 
-        def make_weights():
+        def weights(engine, step):
             values = residual[:].rearrange("p g t -> p (g t)")
-            square = keep.tile([P, G * T], F32, name="square")
-            nc.vector.tensor_tensor(out=square[:], in0=values, in1=values, op=MULT)
-            denominator = keep.tile([P, G * T], F32, name="denominator")
-            nc.vector.tensor_scalar(out=denominator[:], in0=square[:], scalar1=1.0, scalar2=None, op0=ADD)
-            nc.vector.reciprocal(out=weight[:], in_=denominator[:])
-
-        plane = {}
-        interleaved = {}
-
-        def widen(i, s, t, engine):
-            j, c, n = PIECES[i]
-            if (i, s) not in plane:
-                plane[i, s] = convert.tile([P, T, W], BF16, name="plane", align_bytes=64)
-            if j == 0:
-                codes = codes_first[s][:, t, c : c + n]
+            if step == 0:
+                nc.vector.tensor_tensor(out=square[:], in0=values, in1=values, op=MULT)
+            elif step == 1:
+                nc.vector.tensor_scalar(out=denominator[:], in0=square[:], scalar1=1.0, scalar2=None, op0=ADD)
             else:
-                codes = codes_rest[s][:, t, W * (j - 1) : W * j]
-            dst = plane[i, s][:, t, :n]
-            scale = row_scale[:, s, t : t + 1]
-            if engine == "vector":
-                nc.vector.tensor_scalar(out=dst, in0=codes.bitcast(FP8), scalar1=scale, scalar2=None, op0=MULT)
-            else:
-                nc.scalar.activation(out=dst, in_=codes.bitcast(FP8), func=COPY, scale=scale)
+                nc.vector.reciprocal(out=weight[:], in_=denominator[:])
 
-        def interleave_basis(i, s, engine):
-            n = PIECES[i][2]
-            interleaved[i, s] = convert.tile([P, W, T], BF16, name="interleaved", align_bytes=64)
-            interleave_on(engine, interleaved[i, s][:, :n, :], plane[i, s][:, :, :n])
+        def widen(engine, i, s, t):
+            if ("plane", i, s) not in made:
+                made["plane", i, s] = staged("plane", [P, T, PIECES[i][1]], BF16)
+            scale_on(engine, made["plane", i, s][:, t, :], codes[i, s, t].bitcast(FP8), row_scale[:, s, t : t + 1])
 
-        def quantize_basis(i, s):
-            j, c, n = PIECES[i]
-            c += s * W
+        def interleave_basis(engine, i, s):
+            made["interleaved", i, s] = staged("interleaved", [P, PIECES[i][1], T], BF16)
+            interleave_on(engine, made["interleaved", i, s][:], made["plane", i, s][:])
+
+        def quantize_basis(engine, i, s):
+            c, n = PIECES[i]
             nc.vector.quantize_mx(
-                out=basis_q[j][:, c : c + n].bitcast(FP8X4),
-                scales=basis_s[j][:, c : c + n],
-                in_=interleaved[i, s][:, :n, :].rearrange("p n t -> p (n t)"),
+                out=basis_q[s][:, c : c + n].bitcast(FP8X4),
+                scales=basis_s[s][:, c : c + n],
+                in_=made["interleaved", i, s][:].rearrange("p n t -> p (n t)"),
             )
 
-        sorted_d = {}
-        d_bank = {}
-        d_grouped = {}
-
-        def sort_words(g, t):
-            sorted_d[g, t] = stage.tile([P, L], BF16, name="sorted_d")
+        def sort_words(engine, g, t):
+            made["sorted_d", g, t] = staged("sorted_d", [P, L], BF16)
             nc.vector.tensor_copy(
-                out=sorted_d[g, t][:].bitcast(F32).rearrange("p (s u q) -> p s u q", s=S, u=2),
-                in_=d_raw[g][:, t, :].bitcast(F32).rearrange("p (s q u) -> p s u q", s=S, u=2),
+                out=made["sorted_d", g, t][:].bitcast(F32).rearrange("p (s u q) -> p s u q", s=S, u=2),
+                in_=d_raw[g, t].bitcast(F32).rearrange("p (s q u) -> p s u q", s=S, u=2),
             )
 
-        def transpose_d(g, t):
-            d_bank[g, t] = bank(4 + t)
+        def transpose_d(engine, g, t):
+            made["d_bank", g, t] = bank()
             for s in range(S):
                 for u in range(2):
                     o = (2 * s + u) * P
-                    if (g, t) in sorted_d:
-                        words = sorted_d[g, t][:].bitcast(F32)[:, o : o + P]
+                    if ("sorted_d", g, t) in made:
+                        words = made["sorted_d", g, t][:].bitcast(F32)[:, o : o + P]
                     else:
-                        words = d_raw[g][:, t, :].bitcast(F32)[:, 2 * P * s + u : 2 * P * (s + 1) : 2]
-                    nc.tensor.transpose(d_bank[g, t][:, o : o + P], words, ident[:])
+                        words = d_raw[g, t].bitcast(F32)[:, 2 * P * s + u : 2 * P * (s + 1) : 2]
+                    nc.tensor.transpose(made["d_bank", g, t][:, o : o + P], words, ident[:])
 
-        def copy_d(g, t):
-            d_grouped[g, t] = stage.tile([P, S * P * T], BF16, name="d_grouped", align_bytes=64)
-            nc.scalar.copy(
-                out=d_grouped[g, t][:].bitcast(F32).rearrange("p (s e u) -> p s e u", s=S, u=2),
-                in_=d_bank[g, t][:].rearrange("p (s u e) -> p s e u", s=S, u=2),
+        def copy_d(engine, g, t):
+            made["d_grouped", g, t] = staged("d_grouped", [P, S * P * T], BF16)
+            copy_on(
+                engine,
+                made["d_grouped", g, t][:].bitcast(F32).rearrange("p (s e u) -> p s e u", s=S, u=2),
+                made["d_bank", g, t][:].rearrange("p (s u e) -> p s e u", s=S, u=2),
             )
 
-        def quantize_d(g, t):
+        def quantize_d(engine, g, t):
             columns = slice(t * S * P, (t + 1) * S * P)
             nc.vector.quantize_mx(
-                out=d_q[g][:, columns].bitcast(FP8X4), scales=d_s[g][:, columns], in_=d_grouped[g, t][:]
+                out=d_q[g][:, columns].bitcast(FP8X4), scales=d_s[g][:, columns], in_=made["d_grouped", g, t][:]
             )
 
-        by_vector = [(0, 0), (0, 1), (0, 2)]
-        steps = []
-        for j, g0, turns in ROUNDS:
-            for i, turn in enumerate(turns):
-                steps.append((j, g0 + int(turn), turns[:i].count(turn)))
-        jb_bank = {}
-        wj_plane = {}
-        wj = {}
-
-        def product(dst, j, g, t, c, n):
+        def stage_1(engine, g, t, c, n):
+            made["jb_bank", g, t, c] = bank()
             for s in range(S):
                 stationary = slice((t * S + s) * P, (t * S + s + 1) * P)
-                moving = slice(s * W + c, s * W + c + n)
                 nc.tensor.matmul_mx(
-                    out=dst,
+                    out=made["jb_bank", g, t, c][:, :n],
                     lhsT=d_q[g][:, stationary].bitcast(FP8X4),
                     lhsT_scale=d_s[g][:, stationary],
-                    rhs=basis_q[j][:, moving].bitcast(FP8X4),
-                    rhs_scale=basis_s[j][:, moving],
+                    rhs=basis_q[s][:, c : c + n].bitcast(FP8X4),
+                    rhs_scale=basis_s[s][:, c : c + n],
                     start=(s == 0),
                     stop=(s == S - 1),
                 )
 
-        def stage_1(step):
-            j, g, b = steps[step]
-            jb_bank[step] = bank(step % 4)
-            if (j, g) in by_vector:
-                for t in range(T):
-                    product(jb_bank[step][:, t * P : (t + 1) * P], j, g, t, b * P, P)
-            else:
-                product(jb_bank[step][:], j, g, b, 0, W)
+        def weigh(engine, g, t, c, n):
+            j = c // W
+            if ("wj_plane", j, g) not in made:
+                made["wj_plane", j, g] = staged("wj_plane", [P, T, W], BF16)
+            scale_on(
+                engine,
+                made["wj_plane", j, g][:, t, c % W : c % W + n],
+                made["jb_bank", g, t, c][:, :n],
+                weight[:, g * T + t : g * T + t + 1],
+            )
 
-        def empty(step):
-            j, g, b = steps[step]
-            if (j, g) in by_vector:
-                if b == 0:
-                    wj[j, g] = stage.tile([P, W, T], BF16, name="wj", align_bytes=64)
-                nc.vector.tensor_tensor(
-                    out=wj[j, g][:, b * P : (b + 1) * P, :],
-                    in0=jb_bank[step][:].rearrange("p (t n) -> p n t", t=T),
-                    in1=weight[:, g * T : (g + 1) * T].unsqueeze(1).to_broadcast([P, P, T]),
-                    op=MULT,
-                )
-            else:
-                if b == 0:
-                    wj_plane[j, g] = stage.tile([P, T, W], BF16, name="wj_plane", align_bytes=64)
-                nc.scalar.activation(
-                    out=wj_plane[j, g][:, b, :],
-                    in_=jb_bank[step][:],
-                    func=COPY,
-                    scale=weight[:, g * T + b : g * T + b + 1],
-                )
+        def interleave_wj(engine, j, g):
+            made["wj", j, g] = staged("wj", [P, W, T], BF16)
+            interleave_on(engine, made["wj", j, g][:], made["wj_plane", j, g][:])
 
-        def interleave_wj(j, g):
-            wj[j, g] = stage.tile([P, W, T], BF16, name="wj", align_bytes=64)
-            interleave_on("vector", wj[j, g][:], wj_plane[j, g][:])
-
-        def quantize_wj(j, g):
+        def quantize_wj(engine, j, g):
             nc.vector.quantize_mx(
                 out=wj_q[j][g][:].bitcast(FP8X4),
                 scales=wj_s[j][g][:],
-                in_=wj[j, g][:].rearrange("p n t -> p (n t)"),
+                in_=made["wj", j, g][:].rearrange("p n t -> p (n t)"),
             )
 
-        h_bank = {}
-
-        def stage_2(j, f):
-            h_bank[j, f] = bank(f if j == J - 1 else 4 + f)
+        def stage_2(engine, f, c, n):
+            j = c // W
+            made["h_bank", f, c] = bank()
             for g in range(G):
                 nc.tensor.matmul_mx(
-                    out=h_bank[j, f][:],
+                    out=made["h_bank", f, c][:, :n],
                     lhsT=ja[:, g, 2 * P * f : 2 * P * (f + 1)].bitcast(FP4X4),
                     lhsT_scale=ja_scale[:, g * F + f * P : g * F + (f + 1) * P],
-                    rhs=wj_q[j][g][:].bitcast(FP8X4),
-                    rhs_scale=wj_s[j][g][:],
+                    rhs=wj_q[j][g][:, c % W : c % W + n].bitcast(FP8X4),
+                    rhs_scale=wj_s[j][g][:, c % W : c % W + n],
                     start=(g == 0),
                     stop=(g == G - 1),
                 )
 
-        def store(j, f, parts):
-            h = stage.tile([P, W], F32, name="h")
-            for engine, c, n in parts:
-                copy_on(engine, h[:, c : c + n], h_bank[j, f][:, c : c + n])
-            for engine, c, n in parts:
-                nc.sync.dma_start(out=out[f * P : (f + 1) * P, j * W + c : j * W + c + n], in_=h[:, c : c + n])
+        def store(engine, f, c, n):
+            h = staged("h", [P, n], F32)
+            copy_on(engine, h[:], made["h_bank", f, c][:, :n])
+            nc.sync.dma_start(out=out[f * P : (f + 1) * P, c : c + n], in_=h[:])
 
-        def keep_clock(n):
-            for k in range(n):
-                nc.tensor.matmul(out=bank(k % 4)[:], lhsT=zeros[:, :P], rhs=zeros[:], start=True, stop=True)
+        def warm(engine, k):
+            nc.tensor.matmul(out=bank()[:], lhsT=zeros[:, :P], rhs=zeros[:], start=True, stop=True)
 
-        keep_clock(6)
-        for t in range(3):
-            widen(0, 0, t, "vector")
-        widen(0, 0, 3, "scalar")
-        for t in range(T):
-            widen(0, 1, t, "vector" if t < 2 else "scalar")
-        for s in range(S):
-            interleave_basis(0, s, "vector")
-        for t in range(0, T, 2):
-            transpose_d(0, t)
-            transpose_d(0, t + 1)
-            keep_clock(2)
-        for s in range(S):
-            quantize_basis(0, s)
-        for t in range(T):
-            copy_d(0, t)
-        for t in range(T):
-            widen(1, t // 2, 2 * (t % 2), "vector")
-            widen(1, t // 2, 2 * (t % 2) + 1, "vector")
-            quantize_d(0, t)
-        make_weights()
-        for s in range(S):
-            interleave_basis(1, s, "vector")
+        def pieces_in(c, n):
+            return [i for i in range(len(PIECES)) if PIECES[i][0] < c + n and c < PIECES[i][0] + PIECES[i][1]]
 
-        work = {}
+        def writers_of_plane(j, g):
+            return [job for job in vector + scalar if job[0] == weigh and job[1] == g and job[3] // W == j]
 
-        def before(step, job, *args):
-            work.setdefault(step, []).append((job, args))
+        def needs(job):
+            kind, index = job[0], job[1:]
+            if kind == weights:
+                return [(weights, k) for k in range(index[0])]
+            if kind == interleave_basis:
+                return [(widen,) + index + (t,) for t in range(T)]
+            if kind == quantize_basis:
+                return [(interleave_basis,) + index]
+            if kind == transpose_d:
+                return [other for other in vector if other == (sort_words,) + index]
+            if kind == copy_d:
+                return [(transpose_d,) + index]
+            if kind == quantize_d:
+                return [(copy_d,) + index]
+            if kind == stage_1:
+                g, t, c, n = index
+                return [(quantize_d, g, t)] + [(quantize_basis, i, s) for i in pieces_in(c, n) for s in range(S)]
+            if kind == weigh:
+                return [(stage_1,) + index, (weights, 2)]
+            if kind == interleave_wj:
+                return writers_of_plane(*index)
+            if kind == quantize_wj:
+                return [(interleave_wj,) + index]
+            if kind == stage_2:
+                return [(quantize_wj, index[1] // W, g) for g in range(G)]
+            if kind == store:
+                return [(stage_2,) + index]
+            return []
 
-        for s in range(S):
-            before(1, quantize_basis, 1, s)
-        for g in range(1, G):
-            for t in range(T):
-                run = max(0, 4 * g - 5 + 2 * (t // 2))
-                if g == 3 and t >= 2:
-                    before(run - 3, sort_words, g, t)
-                before(run, transpose_d, g, t)
-                before(run, copy_d, g, t)
-                before(run + 1, quantize_d, g, t)
-        for t in range(T):
-            before(t, widen, 2, 0, t, "scalar")
-            before(3 + t, widen, 2, 1, t, "scalar")
-            before(7 + 2 * t, widen, 3, 0, t, "scalar" if t < 2 else "vector")
-            before(16 + 2 * t, widen, 3, 1, t, "vector")
-        before(5, interleave_basis, 2, 0, "vector")
-        before(8, quantize_basis, 2, 0)
-        before(10, interleave_basis, 2, 1, "scalar")
-        before(13, quantize_basis, 2, 1)
-        for s in range(S):
-            before(23, interleave_basis, 3, s, "vector")
-            before(32, quantize_basis, 3, s)
-        before(21, interleave_wj, 0, 3)
+        def takes(job):
+            kind, index = job[0], job[1:]
+            if kind == widen:
+                return ("plane", index[:2]), (interleave_basis,) + index[:2]
+            if kind == interleave_basis:
+                return ("interleaved", index), (quantize_basis,) + index
+            if kind == sort_words:
+                return ("sorted_d", index), (transpose_d,) + index
+            if kind == transpose_d:
+                return ("bank", job), (copy_d,) + index
+            if kind == copy_d:
+                return ("d_grouped", index), (quantize_d,) + index
+            if kind == stage_1:
+                return ("bank", job), (weigh,) + index
+            if kind == weigh:
+                return ("wj_plane", (index[2] // W, index[0])), (interleave_wj, index[2] // W, index[0])
+            if kind == interleave_wj:
+                return ("wj", index), (quantize_wj,) + index
+            if kind == stage_2:
+                return ("bank", job), (store,) + index
+            if kind == store:
+                return ("h", index), job
+            if kind == warm:
+                return ("bank", job), job
+            return None
+
+        def cell(kind, j, g):
+            return [(kind, g, t, j * W, W) for t in range(T)]
+
+        def half_cell(kind, g, h):
+            return [(kind, g, t, h * W // 2, W // 2) for t in range(T)]
+
+        def group(kind, g):
+            return [(kind, g, t) for t in range(T)]
+
+        def planes(i, s):
+            return [(widen, i, s, t) for t in range(T)]
+
+        def finish(i):
+            return [(interleave_basis, i, s) for s in range(S)] + [(quantize_basis, i, s) for s in range(S)]
+
+        def weave(first, second):
+            jobs = []
+            for k in range(max(len(first), len(second))):
+                jobs += first[k : k + 1] + second[k : k + 1]
+            return jobs
+
+        def convert_wj(j):
+            jobs = [(interleave_wj, j, 0)]
+            for g in range(1, G):
+                jobs += [(interleave_wj, j, g), (quantize_wj, j, g - 1)]
+            return jobs + [(quantize_wj, j, G - 1)]
+
+        def blocks(kind, j):
+            return [(kind, f, j * W, W) for f in range(R)]
+
+        def reader(job):
+            return ({transpose_d: copy_d, stage_1: weigh, stage_2: store}[job[0]],) + job[1:]
+
+        left = half_cell(stage_1, 0, 0) + half_cell(stage_1, 1, 0)[:2]
+        right = half_cell(stage_1, 0, 1) + half_cell(stage_1, 1, 1)[:2]
+        tensor = [(warm, k) for k in range(5)] + group(transpose_d, 0)[:2] + [(warm, 5)] + group(transpose_d, 0)[2:] + [(warm, 6)] + left[:2]
+        tensor += group(transpose_d, 1) + left[2:] + group(transpose_d, 2)
+        tensor += right + cell(stage_1, 0, 1)[2:]
+        tensor += group(transpose_d, 3) + cell(stage_1, 0, 2) + cell(stage_1, 0, 3)
         for g in range(G):
-            before(4 * g + 18, quantize_wj, 0, g)
-        for j in (1, 2):
-            for g in range(G):
-                end = 16 * j + 8 * (g // 2 + 1)
-                if end < STEPS:
-                    before(end + 5 + g % 2, interleave_wj, j, g)
-                    before(end + 6 + g % 2, quantize_wj, j, g)
-        before(46, interleave_wj, 2, 3)
-        before(47, quantize_wj, 2, 3)
+            tensor += cell(stage_1, 1, g)
+        tensor += cell(stage_1, 2, 0) + cell(stage_1, 2, 1)
         for f in range(R):
-            before(31, stage_2, 0, f)
-            before(32, store, 0, f, [("vector", 0, W)])
-        before(45, stage_2, 1, 0)
-        before(46, store, 1, 0, [("vector", 0, W)])
+            tensor += cell(stage_1, 2, 2 + f // 2)[2 * (f % 2) : 2 * (f % 2) + 2] + blocks(stage_2, 0)[f : f + 1]
+        tensor += blocks(stage_2, 1) + blocks(stage_2, 2)[:-1]
+        tensor += [(stage_2, R - 1, A - W + h * W // 2, W // 2) for h in range(2)]
 
-        for step in range(STEPS):
-            for job, args in work.get(step, []):
-                job(*args)
-            stage_1(step)
-            if step > 0:
-                empty(step - 1)
-        empty(STEPS - 1)
+        scalar = planes(0, 0)[3:] + planes(0, 1)[2:] + [reader(job) for job in tensor[:-1] if job[0] != warm]
+        vector = planes(0, 0)[:3] + planes(0, 1)[:2] + finish(0)
+        vector += weave([(weights, k) for k in range(3)], group(quantize_d, 0))
+        vector += planes(1, 0)[:2] + group(quantize_d, 1)[:1] + planes(1, 0)[2:] + group(quantize_d, 1)[1:2] + planes(1, 1) + weave(finish(1), group(quantize_d, 1)[2:])
+        vector += weave(group(sort_words, 3), group(quantize_d, 2)) + planes(2, 0) + planes(2, 1)
+        vector += finish(2)[:1] + group(quantize_d, 3) + finish(2)[1:]
+        vector += planes(3, 0) + planes(3, 1) + finish(3) + convert_wj(0) + convert_wj(1) + convert_wj(2)
+        vector += [reader(tensor[-1])]
 
-        interleave_wj(2, 2)
-        quantize_wj(2, 2)
-        for f in range(1, R):
-            stage_2(1, f)
-            store(1, f, [("vector", 0, W)])
-        for f in range(R):
-            stage_2(2, f)
-            if f < R - 1:
-                store(2, f, [("vector" if f % 2 else "scalar", 0, W)])
-            else:
-                store(2, f, [("vector", W // 2, W // 2), ("scalar", 0, W // 2)])
+        lists = {"tensor": tensor, "scalar": scalar, "vector": vector}
+        position = {engine: 0 for engine in lists}
+        written = set()
+        taken = {name: [] for name in DEPTH}
+        while any(position[engine] < len(lists[engine]) for engine in lists):
+            before = len(written)
+            for engine in lists:
+                if position[engine] == len(lists[engine]):
+                    continue
+                job = lists[engine][position[engine]]
+                if not all(other in written for other in needs(job)):
+                    continue
+                take = takes(job)
+                if take is not None:
+                    (name, index), last_reader = take
+                    if index not in [entry[0] for entry in taken[name]]:
+                        if len(taken[name]) >= DEPTH[name] and taken[name][-DEPTH[name]][1] not in written:
+                            continue
+                        taken[name].append((index, last_reader))
+                job[0](engine, *job[1:])
+                written.add(job)
+                position[engine] += 1
+            assert len(written) > before

@@ -27,7 +27,7 @@ J = A // W
 R = F // P
 
 PIECES = [(0, 256), (256, 256), (512, 512), (1024, 512)]
-DEPTH = {"bank": 8, "plane": 4, "interleaved": 3, "sorted_d": 4, "d_grouped": 6, "wj_plane": 8, "wj": 3, "h": 6}
+DEPTH = {"bank": 8, "plane": 3, "interleaved": 3, "sorted_d": 4, "d_grouped": 6, "wj_plane": 10, "wj": 3, "wj_late": 1, "h": 6}
 
 
 def tile_robust_information_block_s13_kernel(tc, d, basis_bytes, basis_scale, r, ja_words, ja_scales, out):
@@ -89,15 +89,17 @@ def tile_robust_information_block_s13_kernel(tc, d, basis_bytes, basis_scale, r,
             if t == 1:
                 load_r()
         load_d(1, 0, 2)
-        load_d(1, 2, 2)
         for s in range(S):
             load_codes(1, 1, s)
-        for g in (2, 3):
-            load_d(g, 0, 2)
-            load_d(g, 2, 2)
-        for i in (2, 3):
-            for s in range(S):
-                load_codes(i, i, s)
+        load_d(1, 2, 2)
+        load_d(2, 0, 2)
+        load_d(2, 2, 2)
+        for s in range(S):
+            load_codes(2, 2, s)
+        load_d(3, 0, 2)
+        load_d(3, 2, 2)
+        for s in range(S):
+            load_codes(3, 3, s)
         ja = keep.tile([P, G, 2 * F], U8, name="ja", align_bytes=64)
         nc.sync.dma_start(out=ja[:], in_=ja_words.rearrange("g p n -> p g n"))
         for q in range(4):
@@ -222,7 +224,7 @@ def tile_robust_information_block_s13_kernel(tc, d, basis_bytes, basis_scale, r,
             )
 
         def interleave_wj(engine, j, g):
-            made["wj", j, g] = staged("wj", [P, W, T], BF16)
+            made["wj", j, g] = staged("wj" if engine == "vector" else "wj_late", [P, W, T], BF16)
             interleave_on(engine, made["wj", j, g][:], made["wj_plane", j, g][:])
 
         def quantize_wj(engine, j, g):
@@ -232,10 +234,11 @@ def tile_robust_information_block_s13_kernel(tc, d, basis_bytes, basis_scale, r,
                 in_=made["wj", j, g][:].rearrange("p n t -> p (n t)"),
             )
 
-        def stage_2(engine, f, c, n):
+        def stage_2(engine, f, c, n, first, last):
             j = c // W
-            made["h_bank", f, c] = bank()
-            for g in range(G):
+            if first == 0:
+                made["h_bank", f, c] = bank()
+            for g in range(first, last):
                 nc.tensor.matmul_mx(
                     out=made["h_bank", f, c][:, :n],
                     lhsT=ja[:, g, 2 * P * f : 2 * P * (f + 1)].bitcast(FP4X4),
@@ -284,9 +287,9 @@ def tile_robust_information_block_s13_kernel(tc, d, basis_bytes, basis_scale, r,
             if kind == quantize_wj:
                 return [(interleave_wj,) + index]
             if kind == stage_2:
-                return [(quantize_wj, index[1] // W, g) for g in range(G)]
+                return [(quantize_wj, index[1] // W, g) for g in range(index[3], index[4])]
             if kind == store:
-                return [(stage_2,) + index]
+                return [other for other in tensor if other[:4] == (stage_2,) + index]
             return []
 
         def takes(job):
@@ -306,9 +309,9 @@ def tile_robust_information_block_s13_kernel(tc, d, basis_bytes, basis_scale, r,
             if kind == weigh:
                 return ("wj_plane", (index[2] // W, index[0])), (interleave_wj, index[2] // W, index[0])
             if kind == interleave_wj:
-                return ("wj", index), (quantize_wj,) + index
+                return ("wj" if job in vector else "wj_late", index), (quantize_wj,) + index
             if kind == stage_2:
-                return ("bank", job), (store,) + index
+                return ("bank", job[:4]), (store,) + index[:3]
             if kind == store:
                 return ("h", index), job
             if kind == warm:
@@ -343,33 +346,40 @@ def tile_robust_information_block_s13_kernel(tc, d, basis_bytes, basis_scale, r,
             return jobs + [(quantize_wj, j, G - 1)]
 
         def blocks(kind, j):
-            return [(kind, f, j * W, W) for f in range(R)]
+            return [(kind, f, j * W, W) + ((0, G) if kind == stage_2 else ()) for f in range(R)]
 
         def reader(job):
-            return ({transpose_d: copy_d, stage_1: weigh, stage_2: store}[job[0]],) + job[1:]
+            return ({transpose_d: copy_d, stage_1: weigh, stage_2: store}[job[0]],) + job[1 : 4 if job[0] == stage_2 else None]
 
         left = half_cell(stage_1, 0, 0) + half_cell(stage_1, 1, 0)[:2]
         right = half_cell(stage_1, 0, 1) + half_cell(stage_1, 1, 1)[:2]
-        tensor = [(warm, k) for k in range(5)] + group(transpose_d, 0)[:2] + [(warm, 5)] + group(transpose_d, 0)[2:] + [(warm, 6)] + left[:2]
-        tensor += group(transpose_d, 1) + left[2:] + group(transpose_d, 2)
-        tensor += right + cell(stage_1, 0, 1)[2:]
-        tensor += group(transpose_d, 3) + cell(stage_1, 0, 2) + cell(stage_1, 0, 3)
-        for g in range(G):
-            tensor += cell(stage_1, 1, g)
-        tensor += cell(stage_1, 2, 0) + cell(stage_1, 2, 1)
-        for f in range(R):
-            tensor += cell(stage_1, 2, 2 + f // 2)[2 * (f % 2) : 2 * (f % 2) + 2] + blocks(stage_2, 0)[f : f + 1]
-        tensor += blocks(stage_2, 1) + blocks(stage_2, 2)[:-1]
-        tensor += [(stage_2, R - 1, A - W + h * W // 2, W // 2) for h in range(2)]
+        turns = group(transpose_d, 1) + group(transpose_d, 2)
+        tensor = [(warm, k) for k in range(5)] + group(transpose_d, 0)[:2] + [(warm, 10 + k) for k in range(1)]
+        tensor += group(transpose_d, 0)[2:] + [(warm, 20 + k) for k in range(1)]
+        for k in range(0, 6, 2):
+            tensor += left[k : k + 2] + turns[k : k + 2]
+        tensor += right[:2] + turns[6:] + right[2:] + cell(stage_1, 0, 1)[2:] + group(transpose_d, 3)
+        tensor += cell(stage_1, 0, 2) + cell(stage_1, 0, 3)
+        for j in (1, 2):
+            for g in range(G):
+                tensor += cell(stage_1, j, g)
+        tensor += blocks(stage_2, 0) + blocks(stage_2, 1)
+        tensor += [(stage_2, f, A - W, W, g, g + 1) for g in range(G) for f in range(2)] + blocks(stage_2, 2)[2:3]
+        tensor += [(stage_2, R - 1, A - W + h * W // 2, W // 2, 0, G) for h in range(2)]
 
-        scalar = planes(0, 0)[3:] + planes(0, 1)[2:] + [reader(job) for job in tensor[:-1] if job[0] != warm]
+        scalar = planes(0, 0)[3:] + planes(0, 1)[2:] + [reader(job) for job in tensor[:-1] if job[0] != warm and (job[0] != stage_2 or job[5] == G)]
         vector = planes(0, 0)[:3] + planes(0, 1)[:2] + finish(0)
         vector += weave([(weights, k) for k in range(3)], group(quantize_d, 0))
-        vector += planes(1, 0)[:2] + group(quantize_d, 1)[:1] + planes(1, 0)[2:] + group(quantize_d, 1)[1:2] + planes(1, 1) + weave(finish(1), group(quantize_d, 1)[2:])
-        vector += weave(group(sort_words, 3), group(quantize_d, 2)) + planes(2, 0) + planes(2, 1)
-        vector += finish(2)[:1] + group(quantize_d, 3) + finish(2)[1:]
+        vector += planes(1, 0) + planes(1, 1) + finish(1)[:1] + group(quantize_d, 1)[:2] + finish(1)[1:3] + weave(group(quantize_d, 1)[2:], finish(1)[3:])
+        vector += planes(2, 0) + group(quantize_d, 2)[:2] + planes(2, 1) + group(sort_words, 3)
+        vector += group(quantize_d, 2)[2:] + finish(2)[:2] + group(quantize_d, 3)[:2] + weave(finish(2)[2:], group(quantize_d, 3)[2:])
         vector += planes(3, 0) + planes(3, 1) + finish(3) + convert_wj(0) + convert_wj(1) + convert_wj(2)
         vector += [reader(tensor[-1])]
+        last = (interleave_wj, J - 1, G - 1)
+        vector.remove(last)
+        k = scalar.index(cell(weigh, J - 1, G - 1)[-1]) + 1
+        scalar = scalar[:k] + [last] + scalar[k:]
+
 
         lists = {"tensor": tensor, "scalar": scalar, "vector": vector}
         position = {engine: 0 for engine in lists}

@@ -26,7 +26,7 @@ W = 512
 J = A // W
 R = F // P
 
-PIECES = [(0, 256), (256, 256), (512, 512), (1024, 512)]
+PIECES = [(0, 256), (256, 256), (512, 256), (768, 256), (1024, 512)]
 DEPTH = {"bank": 8, "plane": 3, "interleaved": 3, "sorted_d": 4, "d_grouped": 6, "wj_plane": 10, "wj": 3, "wj_late": 1, "h": 6}
 
 
@@ -46,10 +46,13 @@ def tile_robust_information_block_s13_kernel(tc, d, basis_bytes, basis_scale, r,
 
         ident = keep.tile([P, P], F32, name="ident")
         make_identity(nc, ident[:])
+        residual = keep.tile([P, G, T], BF16, name="residual")
+        nc.gpsimd.dma_start(out=residual[:], in_=r.rearrange("(g p t) -> p g t", p=P, t=T))
+
         zeros = keep.tile([P, W], BF16, name="zeros")
         nc.vector.memset(zeros[:], 0.0)
         ja_scale = keep.tile([P, G * F], U8, name="ja_scale", align_bytes=64)
-        nc.gpsimd.memset(ja_scale[:].bitcast(I32), 0)
+        nc.vector.memset(ja_scale[:].bitcast(I32), 0)
 
         row_scale = keep.tile([P, S, T], F32, name="row_scale")
         nc.scalar.dma_start(out=row_scale[:], in_=basis_scale.rearrange("(s p t) o -> p s (t o)", p=P, t=T))
@@ -77,17 +80,11 @@ def tile_robust_information_block_s13_kernel(tc, d, basis_bytes, basis_scale, r,
             for t in range(n):
                 d_raw[g, t0 + t] = tile[:, t, :]
 
-        residual = keep.tile([P, G, T], BF16, name="residual")
-
-        def load_r():
-            nc.sync.dma_start(out=residual[:], in_=r.rearrange("(g p t) -> p g t", p=P, t=T))
 
         for s in range(S):
             load_codes(0, 0, s)
         for t in range(T):
             load_d(0, t, 1)
-            if t == 1:
-                load_r()
         load_d(1, 0, 2)
         for s in range(S):
             load_codes(1, 1, s)
@@ -95,11 +92,11 @@ def tile_robust_information_block_s13_kernel(tc, d, basis_bytes, basis_scale, r,
         load_d(2, 0, 2)
         load_d(2, 2, 2)
         for s in range(S):
-            load_codes(2, 2, s)
+            load_codes(2, 3, s)
         load_d(3, 0, 2)
         load_d(3, 2, 2)
         for s in range(S):
-            load_codes(3, 3, s)
+            load_codes(4, 4, s)
         ja = keep.tile([P, G, 2 * F], U8, name="ja", align_bytes=64)
         nc.sync.dma_start(out=ja[:], in_=ja_words.rearrange("g p n -> p g n"))
         for q in range(4):
@@ -199,11 +196,15 @@ def tile_robust_information_block_s13_kernel(tc, d, basis_bytes, basis_scale, r,
             )
 
         def stage_1(engine, g, t, c, n):
-            made["jb_bank", g, t, c] = bank()
+            if n == W or t % 2 == 0:
+                whole = bank()
+                made["jb_bank", g, t, c] = whole[:, :n]
+                if n < W:
+                    made["jb_bank", g, t + 1, c] = whole[:, n:]
             for s in range(S):
                 stationary = slice((t * S + s) * P, (t * S + s + 1) * P)
                 nc.tensor.matmul_mx(
-                    out=made["jb_bank", g, t, c][:, :n],
+                    out=made["jb_bank", g, t, c],
                     lhsT=d_q[g][:, stationary].bitcast(FP8X4),
                     lhsT_scale=d_s[g][:, stationary],
                     rhs=basis_q[s][:, c : c + n].bitcast(FP8X4),
@@ -219,7 +220,7 @@ def tile_robust_information_block_s13_kernel(tc, d, basis_bytes, basis_scale, r,
             scale_on(
                 engine,
                 made["wj_plane", j, g][:, t, c % W : c % W + n],
-                made["jb_bank", g, t, c][:, :n],
+                made["jb_bank", g, t, c],
                 weight[:, g * T + t : g * T + t + 1],
             )
 
@@ -281,7 +282,8 @@ def tile_robust_information_block_s13_kernel(tc, d, basis_bytes, basis_scale, r,
                 g, t, c, n = index
                 return [(quantize_d, g, t)] + [(quantize_basis, i, s) for i in pieces_in(c, n) for s in range(S)]
             if kind == weigh:
-                return [(stage_1,) + index, (weights, 2)]
+                g, t, c, n = index
+                return [(stage_1, g, t if n == W else t | 1, c, n), (weights, 2)]
             if kind == interleave_wj:
                 return writers_of_plane(*index)
             if kind == quantize_wj:
@@ -305,7 +307,9 @@ def tile_robust_information_block_s13_kernel(tc, d, basis_bytes, basis_scale, r,
             if kind == copy_d:
                 return ("d_grouped", index), (quantize_d,) + index
             if kind == stage_1:
-                return ("bank", job), (weigh,) + index
+                g, t, c, n = index
+                last = t if n == W else t | 1
+                return ("bank", (stage_1, g, last, c)), (weigh, g, last, c, n)
             if kind == weigh:
                 return ("wj_plane", (index[2] // W, index[0])), (interleave_wj, index[2] // W, index[0])
             if kind == interleave_wj:
@@ -351,17 +355,16 @@ def tile_robust_information_block_s13_kernel(tc, d, basis_bytes, basis_scale, r,
         def reader(job):
             return ({transpose_d: copy_d, stage_1: weigh, stage_2: store}[job[0]],) + job[1 : 4 if job[0] == stage_2 else None]
 
-        left = half_cell(stage_1, 0, 0) + half_cell(stage_1, 1, 0)[:2]
-        right = half_cell(stage_1, 0, 1) + half_cell(stage_1, 1, 1)[:2]
-        turns = group(transpose_d, 1) + group(transpose_d, 2)
+        left = half_cell(stage_1, 0, 0) + half_cell(stage_1, 1, 0)
         tensor = [(warm, k) for k in range(5)] + group(transpose_d, 0)[:2] + [(warm, 10 + k) for k in range(1)]
         tensor += group(transpose_d, 0)[2:] + [(warm, 20 + k) for k in range(1)]
-        for k in range(0, 6, 2):
-            tensor += left[k : k + 2] + turns[k : k + 2]
-        tensor += right[:2] + turns[6:] + right[2:] + cell(stage_1, 0, 1)[2:] + group(transpose_d, 3)
-        tensor += cell(stage_1, 0, 2) + cell(stage_1, 0, 3)
+        tensor += left[:2] + group(transpose_d, 1)[:2] + left[2:4] + group(transpose_d, 1)[2:] + left[4:6]
+        tensor += group(transpose_d, 2) + left[6:] + half_cell(stage_1, 0, 1) + half_cell(stage_1, 1, 1)
+        tensor += group(transpose_d, 3) + cell(stage_1, 0, 2) + cell(stage_1, 0, 3)
+        for h in range(2):
+            tensor += [(stage_1, g, t, W + h * W // 2, W // 2) for g in range(1) for t in range(T)]
         for j in (1, 2):
-            for g in range(G):
+            for g in range(1 if j == 1 else 0, G):
                 tensor += cell(stage_1, j, g)
         tensor += blocks(stage_2, 0) + blocks(stage_2, 1)
         tensor += [(stage_2, f, A - W, W, g, g + 1) for g in range(G) for f in range(2)] + blocks(stage_2, 2)[2:3]
@@ -370,10 +373,11 @@ def tile_robust_information_block_s13_kernel(tc, d, basis_bytes, basis_scale, r,
         scalar = planes(0, 0)[3:] + planes(0, 1)[2:] + [reader(job) for job in tensor[:-1] if job[0] != warm and (job[0] != stage_2 or job[5] == G)]
         vector = planes(0, 0)[:3] + planes(0, 1)[:2] + finish(0)
         vector += weave([(weights, k) for k in range(3)], group(quantize_d, 0))
-        vector += planes(1, 0) + planes(1, 1) + finish(1)[:1] + group(quantize_d, 1)[:2] + finish(1)[1:3] + weave(group(quantize_d, 1)[2:], finish(1)[3:])
-        vector += planes(2, 0) + group(quantize_d, 2)[:2] + planes(2, 1) + group(sort_words, 3)
-        vector += group(quantize_d, 2)[2:] + finish(2)[:2] + group(quantize_d, 3)[:2] + weave(finish(2)[2:], group(quantize_d, 3)[2:])
-        vector += planes(3, 0) + planes(3, 1) + finish(3) + convert_wj(0) + convert_wj(1) + convert_wj(2)
+        vector += planes(1, 0) + planes(1, 1) + finish(1)[:2] + group(quantize_d, 1)[:2] + group(sort_words, 2)
+        vector += weave(group(quantize_d, 1)[2:], finish(1)[2:])
+        vector += planes(2, 0) + planes(2, 1) + group(quantize_d, 2)[:2] + group(sort_words, 3) + group(quantize_d, 2)[2:]
+        vector += finish(2) + weave(group(quantize_d, 3), planes(3, 0)) + planes(3, 1) + finish(3)
+        vector += planes(4, 0) + planes(4, 1) + finish(4) + convert_wj(0) + convert_wj(1) + convert_wj(2)
         vector += [reader(tensor[-1])]
         last = (interleave_wj, J - 1, G - 1)
         vector.remove(last)

@@ -44,11 +44,10 @@ def tile_robust_information_block_s13_kernel(tc, d, basis_bytes, basis_scale, r,
         def bank():
             return psum.tile([P, W], F32, name="bank")
 
+        r_rows = keep.tile([P, P * T], BF16, name="r_rows")
+        nc.gpsimd.memset(r_rows[:].bitcast(I32), 0)
         ident = keep.tile([P, P], F32, name="ident")
         make_identity(nc, ident[:])
-        residual = keep.tile([P, G, T], BF16, name="residual")
-        nc.gpsimd.dma_start(out=residual[:], in_=r.rearrange("(g p t) -> p g t", p=P, t=T))
-
         zeros = keep.tile([P, W], BF16, name="zeros")
         nc.vector.memset(zeros[:], 0.0)
         ja_scale = keep.tile([P, G * F], U8, name="ja_scale", align_bytes=64)
@@ -56,6 +55,7 @@ def tile_robust_information_block_s13_kernel(tc, d, basis_bytes, basis_scale, r,
 
         row_scale = keep.tile([P, S, T], F32, name="row_scale")
         nc.scalar.dma_start(out=row_scale[:], in_=basis_scale.rearrange("(s p t) o -> p s (t o)", p=P, t=T))
+        nc.scalar.dma_start(out=r_rows[:G, :], in_=r.rearrange("(g e) -> g e", g=G))
         table = keep.tile([P, 1], F32, name="table")
         nc.scalar.activation(out=table[:], in_=zeros[:, 0:1], func=COPY)
 
@@ -137,11 +137,22 @@ def tile_robust_information_block_s13_kernel(tc, d, basis_bytes, basis_scale, r,
         denominator = keep.tile([P, G * T], F32, name="denominator")
         weight = keep.tile([P, G * T], F32, name="weight")
 
+        residual = keep.tile([P, G * T], BF16, name="residual")
+
+        def turn_r(engine):
+            made["r_bank"] = bank()
+            for u in range(2):
+                nc.tensor.transpose(made["r_bank"][:, u * P : (u + 1) * P], r_rows[:].bitcast(F32)[:, u::2], ident[:])
+
         def weights(engine, step):
-            values = residual[:].rearrange("p g t -> p (g t)")
             if step == 0:
-                nc.vector.tensor_tensor(out=square[:], in0=values, in1=values, op=MULT)
+                nc.vector.tensor_copy(
+                    out=residual[:].bitcast(F32).rearrange("p (g u) -> p g u", u=2),
+                    in_=made["r_bank"][:, : 2 * P].rearrange("p (u k) -> p k u", u=2)[:, :G, :],
+                )
             elif step == 1:
+                nc.vector.tensor_tensor(out=square[:], in0=residual[:], in1=residual[:], op=MULT)
+            elif step == 2:
                 nc.vector.tensor_scalar(out=denominator[:], in0=square[:], scalar1=1.0, scalar2=None, op0=ADD)
             else:
                 nc.vector.reciprocal(out=weight[:], in_=denominator[:])
@@ -267,7 +278,7 @@ def tile_robust_information_block_s13_kernel(tc, d, basis_bytes, basis_scale, r,
         def needs(job):
             kind, index = job[0], job[1:]
             if kind == weights:
-                return [(weights, k) for k in range(index[0])]
+                return [(turn_r,)] + [(weights, k) for k in range(index[0])]
             if kind == interleave_basis:
                 return [(widen,) + index + (t,) for t in range(T)]
             if kind == quantize_basis:
@@ -283,7 +294,7 @@ def tile_robust_information_block_s13_kernel(tc, d, basis_bytes, basis_scale, r,
                 return [(quantize_d, g, t)] + [(quantize_basis, i, s) for i in pieces_in(c, n) for s in range(S)]
             if kind == weigh:
                 g, t, c, n = index
-                return [(stage_1, g, t if n == W else t | 1, c, n), (weights, 2)]
+                return [(stage_1, g, t if n == W else t | 1, c, n), (weights, 3)]
             if kind == interleave_wj:
                 return writers_of_plane(*index)
             if kind == quantize_wj:
@@ -318,6 +329,8 @@ def tile_robust_information_block_s13_kernel(tc, d, basis_bytes, basis_scale, r,
                 return ("bank", job[:4]), (store,) + index[:3]
             if kind == store:
                 return ("h", index), job
+            if kind == turn_r:
+                return ("bank", job), (weights, 0)
             if kind == warm:
                 return ("bank", job), job
             return None
@@ -356,7 +369,7 @@ def tile_robust_information_block_s13_kernel(tc, d, basis_bytes, basis_scale, r,
             return ({transpose_d: copy_d, stage_1: weigh, stage_2: store}[job[0]],) + job[1 : 4 if job[0] == stage_2 else None]
 
         left = half_cell(stage_1, 0, 0) + half_cell(stage_1, 1, 0)
-        tensor = [(warm, k) for k in range(5)] + group(transpose_d, 0)[:2] + [(warm, 10 + k) for k in range(1)]
+        tensor = [(warm, k) for k in range(4)] + [(turn_r,)] + group(transpose_d, 0)[:2] + [(warm, 10 + k) for k in range(1)]
         tensor += group(transpose_d, 0)[2:] + [(warm, 20 + k) for k in range(1)]
         tensor += left[:2] + group(transpose_d, 1)[:2] + left[2:4] + group(transpose_d, 1)[2:] + left[4:6]
         tensor += group(transpose_d, 2) + left[6:] + half_cell(stage_1, 0, 1) + half_cell(stage_1, 1, 1)
@@ -370,9 +383,9 @@ def tile_robust_information_block_s13_kernel(tc, d, basis_bytes, basis_scale, r,
         tensor += [(stage_2, f, A - W, W, g, g + 1) for g in range(G) for f in range(2)] + blocks(stage_2, 2)[2:3]
         tensor += [(stage_2, R - 1, A - W + h * W // 2, W // 2, 0, G) for h in range(2)]
 
-        scalar = planes(0, 0)[3:] + planes(0, 1)[2:] + [reader(job) for job in tensor[:-1] if job[0] != warm and (job[0] != stage_2 or job[5] == G)]
-        vector = planes(0, 0)[:3] + planes(0, 1)[:2] + finish(0)
-        vector += weave([(weights, k) for k in range(3)], group(quantize_d, 0))
+        scalar = planes(0, 0)[3:] + planes(0, 1)[2:] + [reader(job) for job in tensor[:-1] if job[0] not in (warm, turn_r) and (job[0] != stage_2 or job[5] == G)]
+        vector = planes(0, 0)[:3] + planes(0, 1)[:2] + weave(finish(0), [(weights, k) for k in range(4)])
+        vector += group(quantize_d, 0)
         vector += planes(1, 0) + planes(1, 1) + finish(1)[:2] + group(quantize_d, 1)[:2] + group(sort_words, 2)
         vector += weave(group(quantize_d, 1)[2:], finish(1)[2:])
         vector += planes(2, 0) + planes(2, 1) + group(quantize_d, 2)[:2] + group(sort_words, 3) + group(quantize_d, 2)[2:]

@@ -27,7 +27,7 @@ J = A // W
 R = F // P
 
 PIECES = [(0, 256), (256, 256), (512, 256), (768, 256), (1024, 512)]
-DEPTH = {"bank": 8, "plane": 3, "interleaved": 3, "sorted_d": 4, "d_grouped": 6, "wj_plane": 10, "wj": 3, "wj_late": 1, "h": 6}
+DEPTH = {"bank": 8, "plane": 4, "interleaved": 3, "sorted_d": 3, "d_grouped": 4, "wj_plane": 9, "wj": 3, "wj_late": 1, "h": 5}
 
 
 def tile_robust_information_block_s13_kernel(tc, d, basis_bytes, basis_scale, r, ja_words, ja_scales, out):
@@ -74,29 +74,20 @@ def tile_robust_information_block_s13_kernel(tc, d, basis_bytes, basis_scale, r,
                 for t in range(T):
                     codes[i, s, t] = tile[:, t, c - c0 : c - c0 + n]
 
-        def load_d(g, t0, n):
-            tile = keep.tile([P, n, L], BF16, name="d_raw_%d_%d" % (g, t0))
-            nc.sync.dma_start(out=tile[:], in_=d_rows[g][:, t0 : t0 + n, :])
-            for t in range(n):
-                d_raw[g, t0 + t] = tile[:, t, :]
-
+        def load_d(g, t, n):
+            d_raw[g, t] = keep.tile([P, n, L], BF16, name="d_raw_%d_%d" % (g, t))
+            nc.sync.dma_start(out=d_raw[g, t][:], in_=d_rows[g][:, t : t + n, :])
 
         for s in range(S):
-            load_codes(0, 0, s)
+            load_codes(0, 1, s)
         for t in range(T):
             load_d(0, t, 1)
-        load_d(1, 0, 2)
-        for s in range(S):
-            load_codes(1, 1, s)
-        load_d(1, 2, 2)
-        load_d(2, 0, 2)
-        load_d(2, 2, 2)
-        for s in range(S):
-            load_codes(2, 3, s)
-        load_d(3, 0, 2)
-        load_d(3, 2, 2)
-        for s in range(S):
-            load_codes(4, 4, s)
+        for g in range(1, G):
+            load_d(g, 0, 2)
+            load_d(g, 2, 2)
+        for first, last in ((2, 3), (4, 4)):
+            for s in range(S):
+                load_codes(first, last, s)
         ja = keep.tile([P, G, 2 * F], U8, name="ja", align_bytes=64)
         nc.sync.dma_start(out=ja[:], in_=ja_words.rearrange("g p n -> p g n"))
         for q in range(4):
@@ -109,8 +100,8 @@ def tile_robust_information_block_s13_kernel(tc, d, basis_bytes, basis_scale, r,
         basis_s = [keep.tile([P, A], U8, name="basis_s_%d" % s, align_bytes=64) for s in range(S)]
         d_q = [keep.tile([P, T * S * P], U32, name="d_q_%d" % g, align_bytes=64) for g in range(G)]
         d_s = [keep.tile([P, T * S * P], U8, name="d_s_%d" % g, align_bytes=64) for g in range(G)]
-        wj_q = [[keep.tile([P, W], U32, name="wj_q_%d_%d" % (j, g), align_bytes=64) for g in range(G)] for j in range(J)]
-        wj_s = [[keep.tile([P, W], U8, name="wj_s_%d_%d" % (j, g), align_bytes=64) for g in range(G)] for j in range(J)]
+        wj_q = [keep.tile([P, G * W], U32, name="wj_q_%d" % j, align_bytes=64) for j in range(J)]
+        wj_s = [keep.tile([P, G * W], U8, name="wj_s_%d" % j, align_bytes=64) for j in range(J)]
 
         made = {}
 
@@ -129,15 +120,14 @@ def tile_robust_information_block_s13_kernel(tc, d, basis_bytes, basis_scale, r,
         def interleave_on(engine, dst, src):
             copy_on(
                 engine,
-                dst.rearrange("p (c i) t -> p c t i", i=4),
-                src.rearrange("p t (c i) -> p c t i", i=4),
+                dst.rearrange("p m (c i) t -> p m c t i", i=4),
+                src.rearrange("p m t (c i) -> p m c t i", i=4),
             )
 
+        residual = keep.tile([P, G * T], BF16, name="residual")
         square = keep.tile([P, G * T], F32, name="square")
         denominator = keep.tile([P, G * T], F32, name="denominator")
         weight = keep.tile([P, G * T], F32, name="weight")
-
-        residual = keep.tile([P, G * T], BF16, name="residual")
 
         def turn_r(engine):
             made["r_bank"] = bank()
@@ -159,11 +149,11 @@ def tile_robust_information_block_s13_kernel(tc, d, basis_bytes, basis_scale, r,
 
         def widen(engine, i, s, t):
             if ("plane", i, s) not in made:
-                made["plane", i, s] = staged("plane", [P, T, PIECES[i][1]], BF16)
-            scale_on(engine, made["plane", i, s][:, t, :], codes[i, s, t].bitcast(FP8), row_scale[:, s, t : t + 1])
+                made["plane", i, s] = staged("plane", [P, 1, T, PIECES[i][1]], BF16)
+            scale_on(engine, made["plane", i, s][:, 0, t, :], codes[i, s, t].bitcast(FP8), row_scale[:, s, t : t + 1])
 
         def interleave_basis(engine, i, s):
-            made["interleaved", i, s] = staged("interleaved", [P, PIECES[i][1], T], BF16)
+            made["interleaved", i, s] = staged("interleaved", [P, 1, PIECES[i][1], T], BF16)
             interleave_on(engine, made["interleaved", i, s][:], made["plane", i, s][:])
 
         def quantize_basis(engine, i, s):
@@ -171,39 +161,47 @@ def tile_robust_information_block_s13_kernel(tc, d, basis_bytes, basis_scale, r,
             nc.vector.quantize_mx(
                 out=basis_q[s][:, c : c + n].bitcast(FP8X4),
                 scales=basis_s[s][:, c : c + n],
-                in_=made["interleaved", i, s][:].rearrange("p n t -> p (n t)"),
+                in_=made["interleaved", i, s][:].rearrange("p m n t -> p (m n t)"),
             )
 
         def sort_words(engine, g, t):
-            made["sorted_d", g, t] = staged("sorted_d", [P, L], BF16)
+            made["sorted_d", g, t] = staged("sorted_d", [P, 2, L], BF16)
             nc.vector.tensor_copy(
-                out=made["sorted_d", g, t][:].bitcast(F32).rearrange("p (s u q) -> p s u q", s=S, u=2),
-                in_=d_raw[g, t].bitcast(F32).rearrange("p (s q u) -> p s u q", s=S, u=2),
+                out=made["sorted_d", g, t][:].bitcast(F32).rearrange("p m (s u q) -> p (m s) u q", s=S, u=2),
+                in_=d_raw[g, t][:].bitcast(F32).rearrange("p m (s q u) -> p (m s) u q", s=S, u=2),
             )
 
         def transpose_d(engine, g, t):
             made["d_bank", g, t] = bank()
+            first = t if (g, t) in d_raw else t - 1
             for s in range(S):
                 for u in range(2):
                     o = (2 * s + u) * P
-                    if ("sorted_d", g, t) in made:
-                        words = made["sorted_d", g, t][:].bitcast(F32)[:, o : o + P]
+                    if ("sorted_d", g, first) in made:
+                        words = made["sorted_d", g, first][:, t - first, :].bitcast(F32)[:, o : o + P]
                     else:
-                        words = d_raw[g, t].bitcast(F32)[:, 2 * P * s + u : 2 * P * (s + 1) : 2]
+                        words = d_raw[g, first][:, t - first, :].bitcast(F32)[:, 2 * P * s + u : 2 * P * (s + 1) : 2]
                     nc.tensor.transpose(made["d_bank", g, t][:, o : o + P], words, ident[:])
 
+        def quantiser_of(g, t):
+            return [job for job in vector if job[:2] == (quantize_d, g) and job[2] <= t < job[2] + job[3]][0]
+
         def copy_d(engine, g, t):
-            made["d_grouped", g, t] = staged("d_grouped", [P, S * P * T], BF16)
+            first, n = quantiser_of(g, t)[2:]
+            if t == first:
+                made["d_grouped", g, first] = staged("d_grouped", [P, n, S * P * T], BF16)
             copy_on(
                 engine,
-                made["d_grouped", g, t][:].bitcast(F32).rearrange("p (s e u) -> p s e u", s=S, u=2),
+                made["d_grouped", g, first][:, t - first, :].bitcast(F32).rearrange("p (s e u) -> p s e u", s=S, u=2),
                 made["d_bank", g, t][:].rearrange("p (s u e) -> p s e u", s=S, u=2),
             )
 
-        def quantize_d(engine, g, t):
-            columns = slice(t * S * P, (t + 1) * S * P)
+        def quantize_d(engine, g, t, n):
+            columns = slice(t * S * P, (t + n) * S * P)
             nc.vector.quantize_mx(
-                out=d_q[g][:, columns].bitcast(FP8X4), scales=d_s[g][:, columns], in_=made["d_grouped", g, t][:]
+                out=d_q[g][:, columns].bitcast(FP8X4),
+                scales=d_s[g][:, columns],
+                in_=made["d_grouped", g, t][:].rearrange("p m c -> p (m c)"),
             )
 
         def stage_1(engine, g, t, c, n):
@@ -224,26 +222,33 @@ def tile_robust_information_block_s13_kernel(tc, d, basis_bytes, basis_scale, r,
                     stop=(s == S - 1),
                 )
 
+        def interleaver_of(j, g):
+            return [
+                job for job in vector + scalar if job[:2] == (interleave_wj, j) and job[2] <= g < job[2] + job[3]
+            ][0]
+
         def weigh(engine, g, t, c, n):
             j = c // W
-            if ("wj_plane", j, g) not in made:
-                made["wj_plane", j, g] = staged("wj_plane", [P, T, W], BF16)
+            first, cells = interleaver_of(j, g)[2:]
+            if ("wj_plane", j, first) not in made:
+                made["wj_plane", j, first] = staged("wj_plane", [P, cells, T, W], BF16)
             scale_on(
                 engine,
-                made["wj_plane", j, g][:, t, c % W : c % W + n],
+                made["wj_plane", j, first][:, g - first, t, c % W : c % W + n],
                 made["jb_bank", g, t, c],
                 weight[:, g * T + t : g * T + t + 1],
             )
 
-        def interleave_wj(engine, j, g):
-            made["wj", j, g] = staged("wj" if engine == "vector" else "wj_late", [P, W, T], BF16)
+        def interleave_wj(engine, j, g, cells):
+            made["wj", j, g] = staged("wj" if engine == "vector" else "wj_late", [P, cells, W, T], BF16)
             interleave_on(engine, made["wj", j, g][:], made["wj_plane", j, g][:])
 
-        def quantize_wj(engine, j, g):
+        def quantize_wj(engine, j, g, cells):
+            columns = slice(g * W, (g + cells) * W)
             nc.vector.quantize_mx(
-                out=wj_q[j][g][:].bitcast(FP8X4),
-                scales=wj_s[j][g][:],
-                in_=made["wj", j, g][:].rearrange("p n t -> p (n t)"),
+                out=wj_q[j][:, columns].bitcast(FP8X4),
+                scales=wj_s[j][:, columns],
+                in_=made["wj", j, g][:].rearrange("p m n t -> p (m n t)"),
             )
 
         def stage_2(engine, f, c, n, first, last):
@@ -251,12 +256,13 @@ def tile_robust_information_block_s13_kernel(tc, d, basis_bytes, basis_scale, r,
             if first == 0:
                 made["h_bank", f, c] = bank()
             for g in range(first, last):
+                moving = slice(g * W + c % W, g * W + c % W + n)
                 nc.tensor.matmul_mx(
                     out=made["h_bank", f, c][:, :n],
                     lhsT=ja[:, g, 2 * P * f : 2 * P * (f + 1)].bitcast(FP4X4),
                     lhsT_scale=ja_scale[:, g * F + f * P : g * F + (f + 1) * P],
-                    rhs=wj_q[j][g][:, c % W : c % W + n].bitcast(FP8X4),
-                    rhs_scale=wj_s[j][g][:, c % W : c % W + n],
+                    rhs=wj_q[j][:, moving].bitcast(FP8X4),
+                    rhs_scale=wj_s[j][:, moving],
                     start=(g == 0),
                     stop=(g == G - 1),
                 )
@@ -269,12 +275,6 @@ def tile_robust_information_block_s13_kernel(tc, d, basis_bytes, basis_scale, r,
         def warm(engine, k):
             nc.tensor.matmul(out=bank()[:], lhsT=zeros[:, :P], rhs=zeros[:], start=True, stop=True)
 
-        def pieces_in(c, n):
-            return [i for i in range(len(PIECES)) if PIECES[i][0] < c + n and c < PIECES[i][0] + PIECES[i][1]]
-
-        def writers_of_plane(j, g):
-            return [job for job in vector + scalar if job[0] == weigh and job[1] == g and job[3] // W == j]
-
         def needs(job):
             kind, index = job[0], job[1:]
             if kind == weights:
@@ -284,23 +284,31 @@ def tile_robust_information_block_s13_kernel(tc, d, basis_bytes, basis_scale, r,
             if kind == quantize_basis:
                 return [(interleave_basis,) + index]
             if kind == transpose_d:
-                return [other for other in vector if other == (sort_words,) + index]
+                return [other for other in vector if other == (sort_words, index[0], index[1] // 2 * 2)]
             if kind == copy_d:
                 return [(transpose_d,) + index]
             if kind == quantize_d:
-                return [(copy_d,) + index]
+                g, t, n = index
+                return [(copy_d, g, t + k) for k in range(n)]
             if kind == stage_1:
                 g, t, c, n = index
-                return [(quantize_d, g, t)] + [(quantize_basis, i, s) for i in pieces_in(c, n) for s in range(S)]
+                pieces = [i for i in range(len(PIECES)) if PIECES[i][0] < c + n and c < PIECES[i][0] + PIECES[i][1]]
+                return [quantiser_of(g, t)] + [(quantize_basis, i, s) for i in pieces for s in range(S)]
             if kind == weigh:
                 g, t, c, n = index
                 return [(stage_1, g, t if n == W else t | 1, c, n), (weights, 3)]
             if kind == interleave_wj:
-                return writers_of_plane(*index)
+                j, g, cells = index
+                return [
+                    other
+                    for other in vector + scalar
+                    if other[0] == weigh and g <= other[1] < g + cells and other[3] // W == j
+                ]
             if kind == quantize_wj:
                 return [(interleave_wj,) + index]
             if kind == stage_2:
-                return [(quantize_wj, index[1] // W, g) for g in range(index[3], index[4])]
+                f, c, n, first, last = index
+                return [(quantize_wj,) + interleaver_of(c // W, g)[1:] for g in range(first, last)]
             if kind == store:
                 return [other for other in tensor if other[:4] == (stage_2,) + index]
             return []
@@ -312,17 +320,18 @@ def tile_robust_information_block_s13_kernel(tc, d, basis_bytes, basis_scale, r,
             if kind == interleave_basis:
                 return ("interleaved", index), (quantize_basis,) + index
             if kind == sort_words:
-                return ("sorted_d", index), (transpose_d,) + index
+                return ("sorted_d", index), (transpose_d, index[0], index[1] + 1)
             if kind == transpose_d:
                 return ("bank", job), (copy_d,) + index
             if kind == copy_d:
-                return ("d_grouped", index), (quantize_d,) + index
+                return ("d_grouped", quantiser_of(*index)), quantiser_of(*index)
             if kind == stage_1:
                 g, t, c, n = index
                 last = t if n == W else t | 1
                 return ("bank", (stage_1, g, last, c)), (weigh, g, last, c, n)
             if kind == weigh:
-                return ("wj_plane", (index[2] // W, index[0])), (interleave_wj, index[2] // W, index[0])
+                reader_job = interleaver_of(index[2] // W, index[0])
+                return ("wj_plane", reader_job), reader_job
             if kind == interleave_wj:
                 return ("wj" if job in vector else "wj_late", index), (quantize_wj,) + index
             if kind == stage_2:
@@ -338,11 +347,20 @@ def tile_robust_information_block_s13_kernel(tc, d, basis_bytes, basis_scale, r,
         def cell(kind, j, g):
             return [(kind, g, t, j * W, W) for t in range(T)]
 
-        def half_cell(kind, g, h):
-            return [(kind, g, t, h * W // 2, W // 2) for t in range(T)]
+        def half_cell(j, g, h):
+            return [(stage_1, g, t, j * W + h * W // 2, W // 2) for t in range(T)]
 
         def group(kind, g):
             return [(kind, g, t) for t in range(T)]
+
+        def singles(g):
+            return [(quantize_d, g, t, 1) for t in range(T)]
+
+        def pairs(g):
+            return [(quantize_d, g, t, 2) for t in (0, 2)]
+
+        def sorts(g):
+            return [(sort_words, g, t) for t in (0, 2)]
 
         def planes(i, s):
             return [(widen, i, s, t) for t in range(T)]
@@ -356,47 +374,41 @@ def tile_robust_information_block_s13_kernel(tc, d, basis_bytes, basis_scale, r,
                 jobs += first[k : k + 1] + second[k : k + 1]
             return jobs
 
-        def convert_wj(j):
-            jobs = [(interleave_wj, j, 0)]
-            for g in range(1, G):
-                jobs += [(interleave_wj, j, g), (quantize_wj, j, g - 1)]
-            return jobs + [(quantize_wj, j, G - 1)]
-
-        def blocks(kind, j):
-            return [(kind, f, j * W, W) + ((0, G) if kind == stage_2 else ()) for f in range(R)]
+        def blocks(j):
+            return [(stage_2, f, j * W, W, 0, G) for f in range(R)]
 
         def reader(job):
             return ({transpose_d: copy_d, stage_1: weigh, stage_2: store}[job[0]],) + job[1 : 4 if job[0] == stage_2 else None]
 
-        left = half_cell(stage_1, 0, 0) + half_cell(stage_1, 1, 0)
-        tensor = [(warm, k) for k in range(4)] + [(turn_r,)] + group(transpose_d, 0)[:2] + [(warm, 10 + k) for k in range(1)]
-        tensor += group(transpose_d, 0)[2:] + [(warm, 20 + k) for k in range(1)]
-        tensor += left[:2] + group(transpose_d, 1)[:2] + left[2:4] + group(transpose_d, 1)[2:] + left[4:6]
-        tensor += group(transpose_d, 2) + left[6:] + half_cell(stage_1, 0, 1) + half_cell(stage_1, 1, 1)
+        tensor = [(warm, k) for k in range(6)] + group(transpose_d, 0)[:2] + [(turn_r,)] + [(warm, 10 + k) for k in range(1)]
+        tensor += group(transpose_d, 0)[2:] + [(warm, 20 + k) for k in range(0)]
+        tensor += half_cell(0, 0, 0)[:2] + group(transpose_d, 1)[:2] + half_cell(0, 0, 0)[2:] + group(transpose_d, 1)[2:]
+        tensor += half_cell(0, 0, 1) + group(transpose_d, 2) + cell(stage_1, 0, 1)
         tensor += group(transpose_d, 3) + cell(stage_1, 0, 2) + cell(stage_1, 0, 3)
-        for h in range(2):
-            tensor += [(stage_1, g, t, W + h * W // 2, W // 2) for g in range(1) for t in range(T)]
+        tensor += half_cell(1, 0, 0) + half_cell(1, 0, 1)
         for j in (1, 2):
             for g in range(1 if j == 1 else 0, G):
                 tensor += cell(stage_1, j, g)
-        tensor += blocks(stage_2, 0) + blocks(stage_2, 1)
-        tensor += [(stage_2, f, A - W, W, g, g + 1) for g in range(G) for f in range(2)] + blocks(stage_2, 2)[2:3]
-        tensor += [(stage_2, R - 1, A - W + h * W // 2, W // 2, 0, G) for h in range(2)]
+        for j in range(J):
+            tensor += [(stage_2, f, j * W, W, g, g + 1) for g in range(G) for f in range(2)] + blocks(j)[2:]
+        tensor = tensor[:-1] + [(stage_2, R - 1, A - W + h * W // 2, W // 2, 0, G) for h in range(2)]
 
-        scalar = planes(0, 0)[3:] + planes(0, 1)[2:] + [reader(job) for job in tensor[:-1] if job[0] not in (warm, turn_r) and (job[0] != stage_2 or job[5] == G)]
-        vector = planes(0, 0)[:3] + planes(0, 1)[:2] + weave(finish(0), [(weights, k) for k in range(4)])
-        vector += group(quantize_d, 0)
-        vector += planes(1, 0) + planes(1, 1) + finish(1)[:2] + group(quantize_d, 1)[:2] + group(sort_words, 2)
-        vector += weave(group(quantize_d, 1)[2:], finish(1)[2:])
-        vector += planes(2, 0) + planes(2, 1) + group(quantize_d, 2)[:2] + group(sort_words, 3) + group(quantize_d, 2)[2:]
-        vector += finish(2) + weave(group(quantize_d, 3), planes(3, 0)) + planes(3, 1) + finish(3)
-        vector += planes(4, 0) + planes(4, 1) + finish(4) + convert_wj(0) + convert_wj(1) + convert_wj(2)
-        vector += [reader(tensor[-1])]
-        last = (interleave_wj, J - 1, G - 1)
-        vector.remove(last)
+        scalar = [reader(job) for job in tensor[:-1] if job[0] not in (warm, turn_r) and (job[0] != stage_2 or job[5] == G)]
+        scalar = planes(0, 0)[3:] + planes(1, 0)[:2] + planes(0, 1)[2:] + planes(1, 0)[2:] + scalar[:2] + planes(1, 1)[:2] + scalar[2:4] + planes(1, 1)[2:] + scalar[4:]
         k = scalar.index(cell(weigh, J - 1, G - 1)[-1]) + 1
-        scalar = scalar[:k] + [last] + scalar[k:]
+        scalar = scalar[:k] + [(interleave_wj, J - 1, G - 1, 1)] + scalar[k:]
 
+        vector = planes(0, 0)[:3] + planes(0, 1)[:2] + finish(0)
+        vector += weave(singles(0)[:2] + finish(1)[:1] + singles(0)[2:], [(weights, k) for k in range(4)]) + finish(1)[1:]
+        vector += pairs(1)[:1] + sorts(2) + pairs(1)[1:] + sorts(3)
+        vector += planes(2, 0) + pairs(2)[:1] + planes(2, 1) + pairs(2)[1:] + finish(2)[:2] + planes(3, 0) + finish(2)[2:]
+        vector += pairs(3)[:1] + planes(3, 1) + pairs(3)[1:] + finish(3)
+        vector += planes(4, 0) + planes(4, 1) + finish(4)
+        for j in range(J):
+            interleave = [(interleave_wj, j, g, 1) for g in range(G)]
+            quantize = [(quantize_wj, j, g, 1) for g in range(G)]
+            vector += [job for job in interleave[:1] + weave(interleave[1:], quantize) if job not in scalar]
+        vector += [reader(tensor[-1])]
 
         lists = {"tensor": tensor, "scalar": scalar, "vector": vector}
         position = {engine: 0 for engine in lists}

@@ -27,7 +27,7 @@ J = A // W
 R = F // P
 
 PIECES = [(0, 256), (256, 256), (512, 256), (768, 256), (1024, 512)]
-DEPTH = {"bank": 8, "plane": 4, "interleaved": 3, "sorted_d": 3, "d_grouped": 4, "wj_plane": 9, "wj": 3, "wj_late": 1, "h": 5}
+DEPTH = {"bank": 8, "plane": 4, "interleaved": 3, "sorted_d": 3, "d_grouped": 3, "wj_plane": 8, "wj": 3, "wj_late": 1, "h": 5}
 
 
 def tile_robust_information_block_s13_kernel(tc, d, basis_bytes, basis_scale, r, ja_words, ja_scales, out):
@@ -41,6 +41,10 @@ def tile_robust_information_block_s13_kernel(tc, d, basis_bytes, basis_scale, r,
         def staged(name, shape, dtype):
             return stage.tile(shape, dtype, name=name, bufs=DEPTH[name], align_bytes=64)
 
+        def placed(name, columns, dtype, size, start):
+            skip = start // size
+            return keep.tile([P, skip + columns], dtype, name=name, align_bytes=256)[:, skip:]
+
         def bank():
             return psum.tile([P, W], F32, name="bank")
 
@@ -50,7 +54,7 @@ def tile_robust_information_block_s13_kernel(tc, d, basis_bytes, basis_scale, r,
         make_identity(nc, ident[:])
         zeros = keep.tile([P, W], BF16, name="zeros")
         nc.vector.memset(zeros[:], 0.0)
-        ja_scale = keep.tile([P, G * F], U8, name="ja_scale", align_bytes=64)
+        ja_scale = placed("ja_scale", G * F, U8, 1, 192)
         nc.vector.memset(ja_scale[:].bitcast(I32), 0)
 
         row_scale = keep.tile([P, S, T], F32, name="row_scale")
@@ -82,13 +86,15 @@ def tile_robust_information_block_s13_kernel(tc, d, basis_bytes, basis_scale, r,
             load_codes(0, 1, s)
         for t in range(T):
             load_d(0, t, 1)
-        for g in range(1, G):
+        for g in (1, 2):
             load_d(g, 0, 2)
             load_d(g, 2, 2)
-        for first, last in ((2, 3), (4, 4)):
-            for s in range(S):
-                load_codes(first, last, s)
-        ja = keep.tile([P, G, 2 * F], U8, name="ja", align_bytes=64)
+        for s in range(S):
+            load_d(3, 2 * s, 2)
+            load_codes(2, 3, s)
+        for s in range(S):
+            load_codes(4, 4, s)
+        ja = placed("ja", G * 2 * F, U8, 1, 128).rearrange("p (g n) -> p g n", g=G)
         nc.sync.dma_start(out=ja[:], in_=ja_words.rearrange("g p n -> p g n"))
         for q in range(4):
             nc.sync.dma_start(
@@ -96,12 +102,12 @@ def tile_robust_information_block_s13_kernel(tc, d, basis_bytes, basis_scale, r,
                 in_=ja_scales[:, 4 * q : 4 * q + 4, :].rearrange("g q n -> q g n").bitcast(I32),
             )
 
-        basis_q = [keep.tile([P, A], U32, name="basis_q_%d" % s, align_bytes=64) for s in range(S)]
-        basis_s = [keep.tile([P, A], U8, name="basis_s_%d" % s, align_bytes=64) for s in range(S)]
-        d_q = [keep.tile([P, T * S * P], U32, name="d_q_%d" % g, align_bytes=64) for g in range(G)]
-        d_s = [keep.tile([P, T * S * P], U8, name="d_s_%d" % g, align_bytes=64) for g in range(G)]
-        wj_q = [keep.tile([P, G * W], U32, name="wj_q_%d" % j, align_bytes=64) for j in range(J)]
-        wj_s = [keep.tile([P, G * W], U8, name="wj_s_%d" % j, align_bytes=64) for j in range(J)]
+        basis_q = [placed("basis_q_%d" % s, A, U32, 4, 0) for s in range(S)]
+        basis_s = [placed("basis_s_%d" % s, A, U8, 1, 64) for s in range(S)]
+        d_q = [placed("d_q_%d" % g, T * S * P, U32, 4, 128) for g in range(G)]
+        d_s = [placed("d_s_%d" % g, T * S * P, U8, 1, 192) for g in range(G)]
+        wj_q = [placed("wj_q_%d" % j, G * W, U32, 4, 0) for j in range(J)]
+        wj_s = [placed("wj_s_%d" % j, G * W, U8, 1, 64) for j in range(J)]
 
         made = {}
 
@@ -120,8 +126,8 @@ def tile_robust_information_block_s13_kernel(tc, d, basis_bytes, basis_scale, r,
         def interleave_on(engine, dst, src):
             copy_on(
                 engine,
-                dst.rearrange("p m (c i) t -> p m c t i", i=4),
-                src.rearrange("p m t (c i) -> p m c t i", i=4),
+                dst.rearrange("p (c i) t -> p c t i", i=4),
+                src.rearrange("p t (c i) -> p c t i", i=4),
             )
 
         residual = keep.tile([P, G * T], BF16, name="residual")
@@ -149,11 +155,11 @@ def tile_robust_information_block_s13_kernel(tc, d, basis_bytes, basis_scale, r,
 
         def widen(engine, i, s, t):
             if ("plane", i, s) not in made:
-                made["plane", i, s] = staged("plane", [P, 1, T, PIECES[i][1]], BF16)
-            scale_on(engine, made["plane", i, s][:, 0, t, :], codes[i, s, t].bitcast(FP8), row_scale[:, s, t : t + 1])
+                made["plane", i, s] = staged("plane", [P, T, PIECES[i][1]], BF16)
+            scale_on(engine, made["plane", i, s][:, t, :], codes[i, s, t].bitcast(FP8), row_scale[:, s, t : t + 1])
 
         def interleave_basis(engine, i, s):
-            made["interleaved", i, s] = staged("interleaved", [P, 1, PIECES[i][1], T], BF16)
+            made["interleaved", i, s] = staged("interleaved", [P, PIECES[i][1], T], BF16)
             interleave_on(engine, made["interleaved", i, s][:], made["plane", i, s][:])
 
         def quantize_basis(engine, i, s):
@@ -161,7 +167,7 @@ def tile_robust_information_block_s13_kernel(tc, d, basis_bytes, basis_scale, r,
             nc.vector.quantize_mx(
                 out=basis_q[s][:, c : c + n].bitcast(FP8X4),
                 scales=basis_s[s][:, c : c + n],
-                in_=made["interleaved", i, s][:].rearrange("p m n t -> p (m n t)"),
+                in_=made["interleaved", i, s][:].rearrange("p n t -> p (n t)"),
             )
 
         def sort_words(engine, g, t):
@@ -222,33 +228,33 @@ def tile_robust_information_block_s13_kernel(tc, d, basis_bytes, basis_scale, r,
                     stop=(s == S - 1),
                 )
 
-        def interleaver_of(j, g):
-            return [
-                job for job in vector + scalar if job[:2] == (interleave_wj, j) and job[2] <= g < job[2] + job[3]
-            ][0]
-
         def weigh(engine, g, t, c, n):
             j = c // W
-            first, cells = interleaver_of(j, g)[2:]
-            if ("wj_plane", j, first) not in made:
-                made["wj_plane", j, first] = staged("wj_plane", [P, cells, T, W], BF16)
+            if ("wj_plane", j, g) not in made:
+                made["wj_plane", j, g] = staged("wj_plane", [P, T, W], BF16)
             scale_on(
                 engine,
-                made["wj_plane", j, first][:, g - first, t, c % W : c % W + n],
+                made["wj_plane", j, g][:, t, c % W : c % W + n],
                 made["jb_bank", g, t, c],
                 weight[:, g * T + t : g * T + t + 1],
             )
 
-        def interleave_wj(engine, j, g, cells):
-            made["wj", j, g] = staged("wj" if engine == "vector" else "wj_late", [P, cells, W, T], BF16)
-            interleave_on(engine, made["wj", j, g][:], made["wj_plane", j, g][:])
+        def interleavers(j, g):
+            return [job for job in vector + scalar if job[:3] == (interleave_wj, j, g)]
 
-        def quantize_wj(engine, j, g, cells):
-            columns = slice(g * W, (g + cells) * W)
+        def wj_name(j, g):
+            return "wj" if all(job in vector for job in interleavers(j, g)) else "wj_late"
+
+        def interleave_wj(engine, j, g, c, n):
+            if ("wj", j, g) not in made:
+                made["wj", j, g] = staged(wj_name(j, g), [P, W, T], BF16)
+            interleave_on(engine, made["wj", j, g][:, c : c + n, :], made["wj_plane", j, g][:, :, c : c + n])
+
+        def quantize_wj(engine, j, g):
             nc.vector.quantize_mx(
-                out=wj_q[j][:, columns].bitcast(FP8X4),
-                scales=wj_s[j][:, columns],
-                in_=made["wj", j, g][:].rearrange("p m n t -> p (m n t)"),
+                out=wj_q[j][:, g * W : (g + 1) * W].bitcast(FP8X4),
+                scales=wj_s[j][:, g * W : (g + 1) * W],
+                in_=made["wj", j, g][:].rearrange("p n t -> p (n t)"),
             )
 
         def stage_2(engine, f, c, n, first, last):
@@ -298,17 +304,13 @@ def tile_robust_information_block_s13_kernel(tc, d, basis_bytes, basis_scale, r,
                 g, t, c, n = index
                 return [(stage_1, g, t if n == W else t | 1, c, n), (weights, 3)]
             if kind == interleave_wj:
-                j, g, cells = index
-                return [
-                    other
-                    for other in vector + scalar
-                    if other[0] == weigh and g <= other[1] < g + cells and other[3] // W == j
-                ]
+                j, g = index[:2]
+                return [other for other in vector + scalar if other[:2] == (weigh, g) and other[3] // W == j]
             if kind == quantize_wj:
-                return [(interleave_wj,) + index]
+                return interleavers(*index)
             if kind == stage_2:
                 f, c, n, first, last = index
-                return [(quantize_wj,) + interleaver_of(c // W, g)[1:] for g in range(first, last)]
+                return [(quantize_wj, c // W, g) for g in range(first, last)]
             if kind == store:
                 return [other for other in tensor if other[:4] == (stage_2,) + index]
             return []
@@ -330,10 +332,10 @@ def tile_robust_information_block_s13_kernel(tc, d, basis_bytes, basis_scale, r,
                 last = t if n == W else t | 1
                 return ("bank", (stage_1, g, last, c)), (weigh, g, last, c, n)
             if kind == weigh:
-                reader_job = interleaver_of(index[2] // W, index[0])
-                return ("wj_plane", reader_job), reader_job
+                j, g = index[2] // W, index[0]
+                return ("wj_plane", (j, g)), interleavers(j, g)[-1]
             if kind == interleave_wj:
-                return ("wj" if job in vector else "wj_late", index), (quantize_wj,) + index
+                return (wj_name(*index[:2]), index[:2]), (quantize_wj,) + index[:2]
             if kind == stage_2:
                 return ("bank", job[:4]), (store,) + index[:3]
             if kind == store:
@@ -385,7 +387,9 @@ def tile_robust_information_block_s13_kernel(tc, d, basis_bytes, basis_scale, r,
         tensor += half_cell(0, 0, 0)[:2] + group(transpose_d, 1)[:2] + half_cell(0, 0, 0)[2:] + group(transpose_d, 1)[2:]
         tensor += half_cell(0, 0, 1) + group(transpose_d, 2) + cell(stage_1, 0, 1)
         tensor += group(transpose_d, 3) + cell(stage_1, 0, 2) + cell(stage_1, 0, 3)
-        tensor += half_cell(1, 0, 0) + half_cell(1, 0, 1)
+        for h in range(2):
+            for g in range(1):
+                tensor += half_cell(1, g, h)
         for j in (1, 2):
             for g in range(1 if j == 1 else 0, G):
                 tensor += cell(stage_1, j, g)
@@ -395,18 +399,18 @@ def tile_robust_information_block_s13_kernel(tc, d, basis_bytes, basis_scale, r,
 
         scalar = [reader(job) for job in tensor[:-1] if job[0] not in (warm, turn_r) and (job[0] != stage_2 or job[5] == G)]
         scalar = planes(0, 0)[3:] + planes(1, 0)[:2] + planes(0, 1)[2:] + planes(1, 0)[2:] + scalar[:2] + planes(1, 1)[:2] + scalar[2:4] + planes(1, 1)[2:] + scalar[4:]
-        k = scalar.index(cell(weigh, J - 1, G - 1)[-1]) + 1
-        scalar = scalar[:k] + [(interleave_wj, J - 1, G - 1, 1)] + scalar[k:]
+        k = scalar.index(cell(weigh, J - 1, G - 1)[-1]) + 3
+        scalar = scalar[:k] + [(interleave_wj, J - 1, G - 1, 0, W)] + scalar[k:]
 
         vector = planes(0, 0)[:3] + planes(0, 1)[:2] + finish(0)
         vector += weave(singles(0)[:2] + finish(1)[:1] + singles(0)[2:], [(weights, k) for k in range(4)]) + finish(1)[1:]
-        vector += pairs(1)[:1] + sorts(2) + pairs(1)[1:] + sorts(3)
-        vector += planes(2, 0) + pairs(2)[:1] + planes(2, 1) + pairs(2)[1:] + finish(2)[:2] + planes(3, 0) + finish(2)[2:]
-        vector += pairs(3)[:1] + planes(3, 1) + pairs(3)[1:] + finish(3)
+        vector += pairs(1)[:1] + sorts(2) + pairs(1)[1:]
+        vector += sorts(3)[:1] + planes(2, 0) + planes(3, 0) + sorts(3)[1:] + pairs(2)[:1] + planes(2, 1) + pairs(2)[1:]
+        vector += finish(2) + pairs(3)[:1] + planes(3, 1) + pairs(3)[1:] + finish(3)
         vector += planes(4, 0) + planes(4, 1) + finish(4)
         for j in range(J):
-            interleave = [(interleave_wj, j, g, 1) for g in range(G)]
-            quantize = [(quantize_wj, j, g, 1) for g in range(G)]
+            interleave = [(interleave_wj, j, g, 0, W) for g in range(G)]
+            quantize = [(quantize_wj, j, g) for g in range(G)]
             vector += [job for job in interleave[:1] + weave(interleave[1:], quantize) if job not in scalar]
         vector += [reader(tensor[-1])]
 

@@ -86,14 +86,12 @@ def tile_robust_information_block_s13_kernel(tc, d, basis_bytes, basis_scale, r,
             load_codes(0, 1, s)
         for t in range(T):
             load_d(0, t, 1)
-        for g in (1, 2):
+        for g in range(1, G):
             load_d(g, 0, 2)
             load_d(g, 2, 2)
-        for s in range(S):
-            load_d(3, 2 * s, 2)
-            load_codes(2, 3, s)
-        for s in range(S):
-            load_codes(4, 4, s)
+        for first, last in ((2, 3), (4, 4)):
+            for s in range(S):
+                load_codes(first, last, s)
         ja = placed("ja", G * 2 * F, U8, 1, 128).rearrange("p (g n) -> p g n", g=G)
         nc.sync.dma_start(out=ja[:], in_=ja_words.rearrange("g p n -> p g n"))
         for q in range(4):
@@ -382,16 +380,16 @@ def tile_robust_information_block_s13_kernel(tc, d, basis_bytes, basis_scale, r,
         def reader(job):
             return ({transpose_d: copy_d, stage_1: weigh, stage_2: store}[job[0]],) + job[1 : 4 if job[0] == stage_2 else None]
 
-        tensor = [(warm, k) for k in range(6)] + group(transpose_d, 0)[:2] + [(turn_r,)] + [(warm, 10 + k) for k in range(1)]
+        tensor = [(warm, k) for k in range(7)] + group(transpose_d, 0)[:2] + [(turn_r,)] + [(warm, 10 + k) for k in range(1)]
         tensor += group(transpose_d, 0)[2:] + [(warm, 20 + k) for k in range(0)]
         tensor += half_cell(0, 0, 0)[:2] + group(transpose_d, 1)[:2] + half_cell(0, 0, 0)[2:] + group(transpose_d, 1)[2:]
         tensor += half_cell(0, 0, 1) + group(transpose_d, 2) + cell(stage_1, 0, 1)
         tensor += group(transpose_d, 3) + cell(stage_1, 0, 2) + cell(stage_1, 0, 3)
         for h in range(2):
-            for g in range(1):
+            for g in range(2):
                 tensor += half_cell(1, g, h)
         for j in (1, 2):
-            for g in range(1 if j == 1 else 0, G):
+            for g in range(2 if j == 1 else 0, G):
                 tensor += cell(stage_1, j, g)
         for j in range(J):
             tensor += [(stage_2, f, j * W, W, g, g + 1) for g in range(G) for f in range(2)] + blocks(j)[2:]
@@ -404,9 +402,9 @@ def tile_robust_information_block_s13_kernel(tc, d, basis_bytes, basis_scale, r,
 
         vector = planes(0, 0)[:3] + planes(0, 1)[:2] + finish(0)
         vector += weave(singles(0)[:2] + finish(1)[:1] + singles(0)[2:], [(weights, k) for k in range(4)]) + finish(1)[1:]
-        vector += pairs(1)[:1] + sorts(2) + pairs(1)[1:]
-        vector += sorts(3)[:1] + planes(2, 0) + planes(3, 0) + sorts(3)[1:] + pairs(2)[:1] + planes(2, 1) + pairs(2)[1:]
-        vector += finish(2) + pairs(3)[:1] + planes(3, 1) + pairs(3)[1:] + finish(3)
+        vector += pairs(1)[:1] + sorts(2) + pairs(1)[1:] + sorts(3)
+        vector += pairs(2)[:1] + planes(2, 0) + pairs(2)[1:] + planes(2, 1) + finish(2)[:2] + pairs(3)[:1] + finish(2)[2:] + pairs(3)[1:]
+        vector += planes(3, 0) + planes(3, 1) + finish(3)
         vector += planes(4, 0) + planes(4, 1) + finish(4)
         for j in range(J):
             interleave = [(interleave_wj, j, g, 0, W) for g in range(G)]

@@ -241,7 +241,7 @@ def tile_robust_information_block_s13_kernel(tc, d, basis_bytes, basis_scale, r,
             return [job for job in vector + scalar if job[:3] == (interleave_wj, j, g)]
 
         def wj_name(j, g):
-            return "wj" if all(job in vector for job in interleavers(j, g)) else "wj_late"
+            return "wj" if all(job in vector for job in interleavers(j, g)) and (j, g) != (0, 0) else "wj_late"
 
         def interleave_wj(engine, j, g, c, n):
             if ("wj", j, g) not in made:
@@ -277,10 +277,13 @@ def tile_robust_information_block_s13_kernel(tc, d, basis_bytes, basis_scale, r,
             nc.sync.dma_start(out=out[f * P : (f + 1) * P, c : c + n], in_=h[:])
 
         def warm(engine, k):
-            nc.tensor.matmul(out=bank()[:], lhsT=zeros[:, :P], rhs=zeros[:], start=True, stop=True)
+            source = zeros[:] if k < 2 else made["plane", 0, 0][:].rearrange("p t n -> p (t n)")[:, :W]
+            nc.tensor.matmul(out=bank()[:], lhsT=source[:, :P], rhs=source, start=True, stop=True)
 
         def needs(job):
             kind, index = job[0], job[1:]
+            if kind == warm:
+                return [(widen, 0, 0, t) for t in range(2)] if index[0] >= 2 else []
             if kind == weights:
                 return [(turn_r,)] + [(weights, k) for k in range(index[0])]
             if kind == interleave_basis:
@@ -316,7 +319,7 @@ def tile_robust_information_block_s13_kernel(tc, d, basis_bytes, basis_scale, r,
         def takes(job):
             kind, index = job[0], job[1:]
             if kind == widen:
-                return ("plane", index[:2]), (interleave_basis,) + index[:2]
+                return ("plane", index[:2]), (warm, 10) if index[:2] == (0, 0) else (interleave_basis,) + index[:2]
             if kind == interleave_basis:
                 return ("interleaved", index), (quantize_basis,) + index
             if kind == sort_words:
@@ -380,7 +383,7 @@ def tile_robust_information_block_s13_kernel(tc, d, basis_bytes, basis_scale, r,
         def reader(job):
             return ({transpose_d: copy_d, stage_1: weigh, stage_2: store}[job[0]],) + job[1 : 4 if job[0] == stage_2 else None]
 
-        tensor = [(warm, k) for k in range(7)] + group(transpose_d, 0)[:2] + [(turn_r,)] + [(warm, 10 + k) for k in range(1)]
+        tensor = [(warm, k) for k in range(4)] + group(transpose_d, 0)[:2] + [(turn_r,)] + [(warm, 10 + k) for k in range(1)]
         tensor += group(transpose_d, 0)[2:] + [(warm, 20 + k) for k in range(0)]
         tensor += half_cell(0, 0, 0)[:2] + group(transpose_d, 1)[:2] + half_cell(0, 0, 0)[2:] + group(transpose_d, 1)[2:]
         tensor += half_cell(0, 0, 1) + group(transpose_d, 2) + cell(stage_1, 0, 1)
@@ -397,17 +400,22 @@ def tile_robust_information_block_s13_kernel(tc, d, basis_bytes, basis_scale, r,
 
         scalar = [reader(job) for job in tensor[:-1] if job[0] not in (warm, turn_r) and (job[0] != stage_2 or job[5] == G)]
         scalar = planes(0, 0)[3:] + planes(1, 0)[:2] + planes(0, 1)[2:] + planes(1, 0)[2:] + scalar[:2] + planes(1, 1)[:2] + scalar[2:4] + planes(1, 1)[2:] + scalar[4:]
-        k = scalar.index(cell(weigh, J - 1, G - 1)[-1]) + 3
+        for k in range(len(scalar) - 1):
+            if scalar[k][0] == weigh and scalar[k][2] % 2 == 0 and scalar[k + 1][:3] == (weigh, scalar[k][1], scalar[k][2] + 1):
+                scalar[k : k + 2] = [scalar[k + 1], scalar[k]]
+        k = scalar.index(cell(weigh, J - 1, G - 1)[-2]) + 3
         scalar = scalar[:k] + [(interleave_wj, J - 1, G - 1, 0, W)] + scalar[k:]
 
         vector = planes(0, 0)[:3] + planes(0, 1)[:2] + finish(0)
         vector += weave(singles(0)[:2] + finish(1)[:1] + singles(0)[2:], [(weights, k) for k in range(4)]) + finish(1)[1:]
-        vector += pairs(1)[:1] + sorts(2) + pairs(1)[1:] + sorts(3)
+        vector += pairs(1)[:1] + sorts(2) + pairs(1)[1:] + sorts(3)[:1] + [(interleave_wj, 0, 0, 0, W // 2)] + sorts(3)[1:]
         vector += pairs(2)[:1] + planes(2, 0) + pairs(2)[1:] + planes(2, 1) + finish(2)[:2] + pairs(3)[:1] + finish(2)[2:] + pairs(3)[1:]
         vector += planes(3, 0) + planes(3, 1) + finish(3)
         vector += planes(4, 0) + planes(4, 1) + finish(4)
         for j in range(J):
             interleave = [(interleave_wj, j, g, 0, W) for g in range(G)]
+            if j == 0:
+                interleave[0] = (interleave_wj, 0, 0, W // 2, W // 2)
             quantize = [(quantize_wj, j, g) for g in range(G)]
             vector += [job for job in interleave[:1] + weave(interleave[1:], quantize) if job not in scalar]
         vector += [reader(tensor[-1])]

@@ -27,7 +27,7 @@ J = A // W
 R = F // P
 
 PIECES = [(0, 256), (256, 256), (512, 256), (768, 256), (1024, 512)]
-DEPTH = {"bank": 8, "plane": 4, "interleaved": 3, "sorted_d": 3, "d_grouped": 3, "wj_plane": 8, "wj": 3, "wj_late": 1, "h": 5}
+DEPTH = {"bank": 8, "plane": 4, "interleaved": 2, "sorted_d": 4, "d_grouped": 3, "wj_plane": 8, "wj": 3, "wj_late": 1, "h": 5}
 
 
 def tile_robust_information_block_s13_kernel(tc, d, basis_bytes, basis_scale, r, ja_words, ja_scales, out):
@@ -383,10 +383,10 @@ def tile_robust_information_block_s13_kernel(tc, d, basis_bytes, basis_scale, r,
         def reader(job):
             return ({transpose_d: copy_d, stage_1: weigh, stage_2: store}[job[0]],) + job[1 : 4 if job[0] == stage_2 else None]
 
-        tensor = [(warm, k) for k in range(4)] + group(transpose_d, 0)[:2] + [(turn_r,)] + [(warm, 10 + k) for k in range(1)]
+        tensor = [(warm, k) for k in range(5)] + group(transpose_d, 0)[:2] + [(turn_r,)] + [(warm, 10 + k) for k in range(1)]
         tensor += group(transpose_d, 0)[2:] + [(warm, 20 + k) for k in range(0)]
-        tensor += half_cell(0, 0, 0)[:2] + group(transpose_d, 1)[:2] + half_cell(0, 0, 0)[2:] + group(transpose_d, 1)[2:]
-        tensor += half_cell(0, 0, 1) + group(transpose_d, 2) + cell(stage_1, 0, 1)
+        tensor += half_cell(0, 0, 0)[:2] + group(transpose_d, 1)[:2] + half_cell(0, 0, 0)[2:] + half_cell(0, 0, 1)
+        tensor += group(transpose_d, 1)[2:] + group(transpose_d, 2) + cell(stage_1, 0, 1)
         tensor += group(transpose_d, 3) + cell(stage_1, 0, 2) + cell(stage_1, 0, 3)
         for h in range(2):
             for g in range(2):
@@ -399,7 +399,7 @@ def tile_robust_information_block_s13_kernel(tc, d, basis_bytes, basis_scale, r,
         tensor = tensor[:-1] + [(stage_2, R - 1, A - W + h * W // 2, W // 2, 0, G) for h in range(2)]
 
         scalar = [reader(job) for job in tensor[:-1] if job[0] not in (warm, turn_r) and (job[0] != stage_2 or job[5] == G)]
-        scalar = planes(0, 0)[3:] + planes(1, 0)[:2] + planes(0, 1)[2:] + planes(1, 0)[2:] + scalar[:2] + planes(1, 1)[:2] + scalar[2:4] + planes(1, 1)[2:] + scalar[4:]
+        scalar = planes(0, 0)[3:] + planes(1, 0)[:2] + planes(0, 1)[2:] + planes(1, 0)[2:] + planes(1, 1)[:1] + scalar[:2] + planes(1, 1)[1:3] + scalar[2:4] + scalar[4:]
         for k in range(len(scalar) - 1):
             if scalar[k][0] == weigh and scalar[k][2] % 2 == 0 and scalar[k + 1][:3] == (weigh, scalar[k][1], scalar[k][2] + 1):
                 scalar[k : k + 2] = [scalar[k + 1], scalar[k]]
@@ -407,8 +407,8 @@ def tile_robust_information_block_s13_kernel(tc, d, basis_bytes, basis_scale, r,
         scalar = scalar[:k] + [(interleave_wj, J - 1, G - 1, 0, W)] + scalar[k:]
 
         vector = planes(0, 0)[:3] + planes(0, 1)[:2] + finish(0)
-        vector += weave(singles(0)[:2] + finish(1)[:1] + singles(0)[2:], [(weights, k) for k in range(4)]) + finish(1)[1:]
-        vector += pairs(1)[:1] + sorts(2) + pairs(1)[1:] + sorts(3)[:1] + [(interleave_wj, 0, 0, 0, W // 2)] + sorts(3)[1:]
+        vector += weave(singles(0)[:2] + planes(1, 1)[3:] + finish(1)[:1], [(weights, k) for k in range(4)]) + weave(singles(0)[2:], finish(1)[1:])
+        vector += sorts(1)[1:] + pairs(1)[:1] + sorts(2) + [(interleave_wj, 0, 0, 0, W // 2)] + weave(sorts(3), pairs(1)[1:])
         vector += pairs(2)[:1] + planes(2, 0) + pairs(2)[1:] + planes(2, 1) + finish(2)[:2] + pairs(3)[:1] + finish(2)[2:] + pairs(3)[1:]
         vector += planes(3, 0) + planes(3, 1) + finish(3)
         vector += planes(4, 0) + planes(4, 1) + finish(4)

@@ -26,11 +26,27 @@ W = 512
 J = A // W
 R = F // P
 
-PIECES = [(0, 256), (256, 256), (512, 256), (768, 256), (1024, 512)]
-DEPTH = {"bank": 8, "plane": 4, "interleaved": 2, "sorted_d": 4, "d_grouped": 3, "wj_plane": 8, "wj": 3, "wj_late": 1, "h": 5}
+HALF = W // 2
+
+PIECES = [(0, HALF), (HALF, HALF), (W, HALF), (W + HALF, HALF), (2 * W, W)]
+DEPTH = {
+    "bank": 8,
+    "plane": 4,
+    "interleaved": 2,
+    "sorted_d": 4,
+    "d_grouped": 3,
+    "wj_plane": 8,
+    "wj": 3,
+    "wj_aside": 1,
+    "h": 6,
+}
+MOVING_WORDS, MOVING_SCALES, STATIONARY_WORDS, STATIONARY_SCALES = 0, 64, 128, 192
+WARM_ON_ZEROS, WARM_BEFORE_D = 2, 5
 
 
-def tile_robust_information_block_s13_kernel(tc, d, basis_bytes, basis_scale, r, ja_words, ja_scales, out):
+def tile_robust_information_block_s13_kernel(
+    tc, d, basis_bytes, basis_scale, r, ja_words, ja_scales, out
+):
     nc = tc.nc
     with ExitStack() as ctx:
         keep = ctx.enter_context(tc.tile_pool(name="keep", bufs=1))
@@ -54,7 +70,7 @@ def tile_robust_information_block_s13_kernel(tc, d, basis_bytes, basis_scale, r,
         make_identity(nc, ident[:])
         zeros = keep.tile([P, W], BF16, name="zeros")
         nc.vector.memset(zeros[:], 0.0)
-        ja_scale = placed("ja_scale", G * F, U8, 1, 192)
+        ja_scale = placed("ja_scale", G * F, U8, 1, STATIONARY_SCALES)
         nc.vector.memset(ja_scale[:].bitcast(I32), 0)
 
         row_scale = keep.tile([P, S, T], F32, name="row_scale")
@@ -92,7 +108,7 @@ def tile_robust_information_block_s13_kernel(tc, d, basis_bytes, basis_scale, r,
         for first, last in ((2, 3), (4, 4)):
             for s in range(S):
                 load_codes(first, last, s)
-        ja = placed("ja", G * 2 * F, U8, 1, 128).rearrange("p (g n) -> p g n", g=G)
+        ja = placed("ja", G * 2 * F, U8, 1, STATIONARY_WORDS).rearrange("p (g n) -> p g n", g=G)
         nc.sync.dma_start(out=ja[:], in_=ja_words.rearrange("g p n -> p g n"))
         for q in range(4):
             nc.sync.dma_start(
@@ -100,12 +116,12 @@ def tile_robust_information_block_s13_kernel(tc, d, basis_bytes, basis_scale, r,
                 in_=ja_scales[:, 4 * q : 4 * q + 4, :].rearrange("g q n -> q g n").bitcast(I32),
             )
 
-        basis_q = [placed("basis_q_%d" % s, A, U32, 4, 0) for s in range(S)]
-        basis_s = [placed("basis_s_%d" % s, A, U8, 1, 64) for s in range(S)]
-        d_q = [placed("d_q_%d" % g, T * S * P, U32, 4, 128) for g in range(G)]
-        d_s = [placed("d_s_%d" % g, T * S * P, U8, 1, 192) for g in range(G)]
-        wj_q = [placed("wj_q_%d" % j, G * W, U32, 4, 0) for j in range(J)]
-        wj_s = [placed("wj_s_%d" % j, G * W, U8, 1, 64) for j in range(J)]
+        basis_q = [placed("basis_q_%d" % s, A, U32, 4, MOVING_WORDS) for s in range(S)]
+        basis_s = [placed("basis_s_%d" % s, A, U8, 1, MOVING_SCALES) for s in range(S)]
+        d_q = [placed("d_q_%d" % g, T * S * P, U32, 4, STATIONARY_WORDS) for g in range(G)]
+        d_s = [placed("d_s_%d" % g, T * S * P, U8, 1, STATIONARY_SCALES) for g in range(G)]
+        wj_q = [placed("wj_q_%d" % j, G * W, U32, 4, MOVING_WORDS) for j in range(J)]
+        wj_s = [placed("wj_s_%d" % j, G * W, U8, 1, MOVING_SCALES) for j in range(J)]
 
         made = {}
 
@@ -241,7 +257,7 @@ def tile_robust_information_block_s13_kernel(tc, d, basis_bytes, basis_scale, r,
             return [job for job in vector + scalar if job[:3] == (interleave_wj, j, g)]
 
         def wj_name(j, g):
-            return "wj" if all(job in vector for job in interleavers(j, g)) and (j, g) != (0, 0) else "wj_late"
+            return "wj_aside" if (j, g) in ((0, 0), (J - 1, G - 1)) else "wj"
 
         def interleave_wj(engine, j, g, c, n):
             if ("wj", j, g) not in made:
@@ -277,13 +293,13 @@ def tile_robust_information_block_s13_kernel(tc, d, basis_bytes, basis_scale, r,
             nc.sync.dma_start(out=out[f * P : (f + 1) * P, c : c + n], in_=h[:])
 
         def warm(engine, k):
-            source = zeros[:] if k < 2 else made["plane", 0, 0][:].rearrange("p t n -> p (t n)")[:, :W]
+            source = zeros[:] if k < WARM_ON_ZEROS else made["plane", 0, 0][:].rearrange("p t n -> p (t n)")[:, :W]
             nc.tensor.matmul(out=bank()[:], lhsT=source[:, :P], rhs=source, start=True, stop=True)
 
         def needs(job):
             kind, index = job[0], job[1:]
             if kind == warm:
-                return [(widen, 0, 0, t) for t in range(2)] if index[0] >= 2 else []
+                return [(widen, 0, 0, t) for t in range(W // HALF)] if index[0] >= WARM_ON_ZEROS else []
             if kind == weights:
                 return [(turn_r,)] + [(weights, k) for k in range(index[0])]
             if kind == interleave_basis:
@@ -319,7 +335,8 @@ def tile_robust_information_block_s13_kernel(tc, d, basis_bytes, basis_scale, r,
         def takes(job):
             kind, index = job[0], job[1:]
             if kind == widen:
-                return ("plane", index[:2]), (warm, 10) if index[:2] == (0, 0) else (interleave_basis,) + index[:2]
+                last_reader = (warm, WARM_BEFORE_D) if index[:2] == (0, 0) else (interleave_basis,) + index[:2]
+                return ("plane", index[:2]), last_reader
             if kind == interleave_basis:
                 return ("interleaved", index), (quantize_basis,) + index
             if kind == sort_words:
@@ -351,7 +368,7 @@ def tile_robust_information_block_s13_kernel(tc, d, basis_bytes, basis_scale, r,
             return [(kind, g, t, j * W, W) for t in range(T)]
 
         def half_cell(j, g, h):
-            return [(stage_1, g, t, j * W + h * W // 2, W // 2) for t in range(T)]
+            return [(stage_1, g, t, j * W + h * HALF, HALF) for t in range(T)]
 
         def group(kind, g):
             return [(kind, g, t) for t in range(T)]
@@ -381,41 +398,47 @@ def tile_robust_information_block_s13_kernel(tc, d, basis_bytes, basis_scale, r,
             return [(stage_2, f, j * W, W, 0, G) for f in range(R)]
 
         def reader(job):
-            return ({transpose_d: copy_d, stage_1: weigh, stage_2: store}[job[0]],) + job[1 : 4 if job[0] == stage_2 else None]
+            if job[0] == stage_2:
+                return (store,) + job[1:4]
+            return (copy_d if job[0] == transpose_d else weigh,) + job[1:]
 
-        tensor = [(warm, k) for k in range(5)] + group(transpose_d, 0)[:2] + [(turn_r,)] + [(warm, 10 + k) for k in range(1)]
-        tensor += group(transpose_d, 0)[2:] + [(warm, 20 + k) for k in range(0)]
+        def fills_bank(job):
+            return job[0] in (transpose_d, stage_1) or (job[0] == stage_2 and job[5] == G)
+
+        tensor = [(warm, k) for k in range(WARM_BEFORE_D)] + group(transpose_d, 0)[:2]
+        tensor += [(turn_r,), (warm, WARM_BEFORE_D)] + group(transpose_d, 0)[2:]
         tensor += half_cell(0, 0, 0)[:2] + group(transpose_d, 1)[:2] + half_cell(0, 0, 0)[2:] + half_cell(0, 0, 1)
         tensor += group(transpose_d, 1)[2:] + group(transpose_d, 2) + cell(stage_1, 0, 1)
         tensor += group(transpose_d, 3) + cell(stage_1, 0, 2) + cell(stage_1, 0, 3)
         for h in range(2):
-            for g in range(2):
-                tensor += half_cell(1, g, h)
+            tensor += half_cell(1, 0, h) + half_cell(1, 1, h)
+        tensor += cell(stage_1, 1, 2) + cell(stage_1, 1, 3) + cell(stage_1, 2, 0) + cell(stage_1, 2, 1)
+        last_members = cell(stage_1, 2, 2) + cell(stage_1, 2, 3)
+        for f in range(R):
+            tensor += last_members[2 * f : 2 * f + 2] + blocks(0)[f : f + 1]
         for j in (1, 2):
-            for g in range(2 if j == 1 else 0, G):
-                tensor += cell(stage_1, j, g)
-        for j in range(J):
             tensor += [(stage_2, f, j * W, W, g, g + 1) for g in range(G) for f in range(2)] + blocks(j)[2:]
-        tensor = tensor[:-1] + [(stage_2, R - 1, A - W + h * W // 2, W // 2, 0, G) for h in range(2)]
+        tensor = tensor[:-1] + [(stage_2, R - 1, A - W + h * HALF, HALF, 0, G) for h in range(2)]
 
-        scalar = [reader(job) for job in tensor[:-1] if job[0] not in (warm, turn_r) and (job[0] != stage_2 or job[5] == G)]
-        scalar = planes(0, 0)[3:] + planes(1, 0)[:2] + planes(0, 1)[2:] + planes(1, 0)[2:] + planes(1, 1)[:1] + scalar[:2] + planes(1, 1)[1:3] + scalar[2:4] + scalar[4:]
-        for k in range(len(scalar) - 1):
-            if scalar[k][0] == weigh and scalar[k][2] % 2 == 0 and scalar[k + 1][:3] == (weigh, scalar[k][1], scalar[k][2] + 1):
-                scalar[k : k + 2] = [scalar[k + 1], scalar[k]]
-        k = scalar.index(cell(weigh, J - 1, G - 1)[-2]) + 3
+        empty = [reader(job) for job in tensor[:-1] if fills_bank(job)]
+        scalar = planes(0, 0)[3:] + planes(1, 0)[:2] + planes(0, 1)[2:] + planes(1, 0)[2:] + planes(1, 1)[:1]
+        scalar += empty[:2] + planes(1, 1)[1:3] + empty[2:]
+        k = scalar.index(reader(blocks(0)[-1])) + 1
         scalar = scalar[:k] + [(interleave_wj, J - 1, G - 1, 0, W)] + scalar[k:]
 
         vector = planes(0, 0)[:3] + planes(0, 1)[:2] + finish(0)
-        vector += weave(singles(0)[:2] + planes(1, 1)[3:] + finish(1)[:1], [(weights, k) for k in range(4)]) + weave(singles(0)[2:], finish(1)[1:])
-        vector += sorts(1)[1:] + pairs(1)[:1] + sorts(2) + [(interleave_wj, 0, 0, 0, W // 2)] + weave(sorts(3), pairs(1)[1:])
-        vector += pairs(2)[:1] + planes(2, 0) + pairs(2)[1:] + planes(2, 1) + finish(2)[:2] + pairs(3)[:1] + finish(2)[2:] + pairs(3)[1:]
-        vector += planes(3, 0) + planes(3, 1) + finish(3)
-        vector += planes(4, 0) + planes(4, 1) + finish(4)
+        vector += weave(singles(0)[:2] + planes(1, 1)[3:] + finish(1)[:1], [(weights, k) for k in range(4)])
+        vector += weave(singles(0)[2:], finish(1)[1:])
+        vector += sorts(1)[1:] + pairs(1)[:1] + sorts(2) + [(interleave_wj, 0, 0, 0, HALF)]
+        vector += weave(sorts(3), pairs(1)[1:])
+        vector += pairs(2)[:1] + planes(2, 0) + pairs(2)[1:] + planes(2, 1)
+        vector += finish(2)[:2] + pairs(3)[:1] + finish(2)[2:] + pairs(3)[1:]
+        for i in (3, 4):
+            vector += planes(i, 0) + planes(i, 1) + finish(i)
         for j in range(J):
             interleave = [(interleave_wj, j, g, 0, W) for g in range(G)]
             if j == 0:
-                interleave[0] = (interleave_wj, 0, 0, W // 2, W // 2)
+                interleave[0] = (interleave_wj, 0, 0, HALF, HALF)
             quantize = [(quantize_wj, j, g) for g in range(G)]
             vector += [job for job in interleave[:1] + weave(interleave[1:], quantize) if job not in scalar]
         vector += [reader(tensor[-1])]

@@ -167,14 +167,27 @@ def tile_robust_information_block_s13_kernel(
             else:
                 nc.vector.reciprocal(out=weight[:], in_=denominator[:])
 
+        def in_pairs(i):
+            return PIECES[i][0] >= W
+
         def widen(engine, i, s, t):
+            n = PIECES[i][1]
             if ("plane", i, s) not in made:
-                made["plane", i, s] = staged("plane", [P, T, PIECES[i][1]], BF16)
-            scale_on(engine, made["plane", i, s][:, t, :], codes[i, s, t].bitcast(FP8), row_scale[:, s, t : t + 1])
+                made["plane", i, s] = staged("plane", [P, 2, n, 2] if in_pairs(i) else [P, T, n], BF16)
+            tile = made["plane", i, s]
+            dst = tile[:, t // 2, :, t % 2] if in_pairs(i) else tile[:, t, :]
+            scale_on(engine, dst, codes[i, s, t].bitcast(FP8), row_scale[:, s, t : t + 1])
 
         def interleave_basis(engine, i, s):
             made["interleaved", i, s] = staged("interleaved", [P, PIECES[i][1], T], BF16)
-            interleave_on(engine, made["interleaved", i, s][:], made["plane", i, s][:])
+            if in_pairs(i):
+                words = made["plane", i, s][:].rearrange("p u n e -> p u (n e)").bitcast(F32)
+                nc.vector.tensor_copy(
+                    out=made["interleaved", i, s][:].bitcast(F32).rearrange("p (c i) u -> p c u i", i=2),
+                    in_=words.rearrange("p u (c i) -> p c u i", i=2),
+                )
+            else:
+                interleave_on(engine, made["interleaved", i, s][:], made["plane", i, s][:])
 
         def quantize_basis(engine, i, s):
             c, n = PIECES[i]
@@ -423,6 +436,8 @@ def tile_robust_information_block_s13_kernel(
         empty = [reader(job) for job in tensor[:-1] if fills_bank(job)]
         scalar = planes(0, 0)[3:] + planes(1, 0)[:2] + planes(0, 1)[2:] + planes(1, 0)[2:] + planes(1, 1)[:1]
         scalar += empty[:2] + planes(1, 1)[1:3] + empty[2:]
+        k = scalar.index(cell(weigh, 0, 1)[2])
+        scalar[k : k + 4] = scalar[k + 2 : k + 4] + scalar[k : k + 2]
         k = scalar.index(reader(blocks(0)[-1])) + 1
         scalar = scalar[:k] + [(interleave_wj, J - 1, G - 1, 0, W)] + scalar[k:]
 

@@ -38,7 +38,7 @@ DEPTH = {
     "wj_plane": 8,
     "wj": 3,
     "wj_aside": 1,
-    "h": 6,
+    "rows": 10,
 }
 MOVING_WORDS, MOVING_SCALES, STATIONARY_WORDS, STATIONARY_SCALES = 0, 64, 128, 192
 WARM_ON_ZEROS, WARM_BEFORE_D = 2, 5
@@ -95,7 +95,7 @@ def tile_robust_information_block_s13_kernel(
                     codes[i, s, t] = tile[:, t, c - c0 : c - c0 + n]
 
         def load_d(g, t, n):
-            d_raw[g, t] = keep.tile([P, n, L], BF16, name="d_raw_%d_%d" % (g, t))
+            d_raw[g, t] = staged("rows", [P, n, L], BF16)
             nc.sync.dma_start(out=d_raw[g, t][:], in_=d_rows[g][:, t : t + n, :])
 
         for s in range(S):
@@ -140,8 +140,8 @@ def tile_robust_information_block_s13_kernel(
         def interleave_on(engine, dst, src):
             copy_on(
                 engine,
-                dst.rearrange("p (c i) t -> p c t i", i=4),
-                src.rearrange("p t (c i) -> p c t i", i=4),
+                dst.rearrange("p (c i) t -> p c t i", i=2),
+                src.rearrange("p t (c i) -> p c t i", i=2),
             )
 
         residual = keep.tile([P, G * T], BF16, name="residual")
@@ -277,12 +277,18 @@ def tile_robust_information_block_s13_kernel(
                 made["wj", j, g] = staged(wj_name(j, g), [P, W, T], BF16)
             interleave_on(engine, made["wj", j, g][:, c : c + n, :], made["wj_plane", j, g][:, :, c : c + n])
 
-        def quantize_wj(engine, j, g):
+        def quantize_wj(engine, j, g, c, n):
             nc.vector.quantize_mx(
-                out=wj_q[j][:, g * W : (g + 1) * W].bitcast(FP8X4),
-                scales=wj_s[j][:, g * W : (g + 1) * W],
-                in_=made["wj", j, g][:].rearrange("p n t -> p (n t)"),
+                out=wj_q[j][:, g * W + c : g * W + c + n].bitcast(FP8X4),
+                scales=wj_s[j][:, g * W + c : g * W + c + n],
+                in_=made["wj", j, g][:, c : c + n, :].rearrange("p n t -> p (n t)"),
             )
+
+        def quantisers(j, g):
+            return [job for job in vector if job[:3] == (quantize_wj, j, g)]
+
+        def overlap(job, c, n):
+            return job[3] < c + n and c < job[3] + job[4]
 
         def stage_2(engine, f, c, n, first, last):
             j = c // W
@@ -301,7 +307,7 @@ def tile_robust_information_block_s13_kernel(
                 )
 
         def store(engine, f, c, n):
-            h = staged("h", [P, n], F32)
+            h = staged("rows", [P, n], F32)
             copy_on(engine, h[:], made["h_bank", f, c][:, :n])
             nc.sync.dma_start(out=out[f * P : (f + 1) * P, c : c + n], in_=h[:])
 
@@ -337,10 +343,10 @@ def tile_robust_information_block_s13_kernel(
                 j, g = index[:2]
                 return [other for other in vector + scalar if other[:2] == (weigh, g) and other[3] // W == j]
             if kind == quantize_wj:
-                return interleavers(*index)
+                return [other for other in interleavers(*index[:2]) if overlap(other, *index[2:])]
             if kind == stage_2:
                 f, c, n, first, last = index
-                return [(quantize_wj, c // W, g) for g in range(first, last)]
+                return [q for g in range(first, last) for q in quantisers(c // W, g) if overlap(q, c % W, n)]
             if kind == store:
                 return [other for other in tensor if other[:4] == (stage_2,) + index]
             return []
@@ -366,11 +372,11 @@ def tile_robust_information_block_s13_kernel(
                 j, g = index[2] // W, index[0]
                 return ("wj_plane", (j, g)), interleavers(j, g)[-1]
             if kind == interleave_wj:
-                return (wj_name(*index[:2]), index[:2]), (quantize_wj,) + index[:2]
+                return (wj_name(*index[:2]), index[:2]), quantisers(*index[:2])[-1]
             if kind == stage_2:
                 return ("bank", job[:4]), (store,) + index[:3]
             if kind == store:
-                return ("h", index), job
+                return ("rows", index), job
             if kind == turn_r:
                 return ("bank", job), (weights, 0)
             if kind == warm:
@@ -429,9 +435,9 @@ def tile_robust_information_block_s13_kernel(
         last_members = cell(stage_1, 2, 2) + cell(stage_1, 2, 3)
         for f in range(R):
             tensor += last_members[2 * f : 2 * f + 2] + blocks(0)[f : f + 1]
-        for j in (1, 2):
-            tensor += [(stage_2, f, j * W, W, g, g + 1) for g in range(G) for f in range(2)] + blocks(j)[2:]
-        tensor = tensor[:-1] + [(stage_2, R - 1, A - W + h * HALF, HALF, 0, G) for h in range(2)]
+        for c, n in ((W, W), (2 * W, HALF), (2 * W + HALF, HALF)):
+            tensor += [(stage_2, f, c, n, g, g + 1) for g in range(G) for f in range(2)]
+            tensor += [(stage_2, f, c, n, 0, G) for f in range(2, R)]
 
         empty = [reader(job) for job in tensor[:-1] if fills_bank(job)]
         scalar = planes(0, 0)[3:] + planes(1, 0)[:2] + planes(0, 1)[2:] + planes(1, 0)[2:] + planes(1, 1)[:1]
@@ -439,7 +445,8 @@ def tile_robust_information_block_s13_kernel(
         k = scalar.index(cell(weigh, 0, 1)[2])
         scalar[k : k + 4] = scalar[k + 2 : k + 4] + scalar[k : k + 2]
         k = scalar.index(reader(blocks(0)[-1])) + 1
-        scalar = scalar[:k] + [(interleave_wj, J - 1, G - 1, 0, W)] + scalar[k:]
+        halves = [(interleave_wj, J - 1, G - 1, h * HALF, HALF) for h in range(2)]
+        scalar = scalar[:k] + halves[:1] + scalar[k : k + 2] + halves[1:] + scalar[k + 2 :]
 
         vector = planes(0, 0)[:3] + planes(0, 1)[:2] + finish(0)
         vector += weave(singles(0)[:2] + planes(1, 1)[3:] + finish(1)[:1], [(weights, k) for k in range(4)])
@@ -450,11 +457,11 @@ def tile_robust_information_block_s13_kernel(
         vector += finish(2)[:2] + pairs(3)[:1] + finish(2)[2:] + pairs(3)[1:]
         for i in (3, 4):
             vector += planes(i, 0) + planes(i, 1) + finish(i)
-        for j in range(J):
-            interleave = [(interleave_wj, j, g, 0, W) for g in range(G)]
+        for j, c, n in ((0, 0, W), (1, 0, W), (2, 0, HALF), (2, HALF, HALF)):
+            interleave = [(interleave_wj, j, g, c, n) for g in range(G)]
             if j == 0:
                 interleave[0] = (interleave_wj, 0, 0, HALF, HALF)
-            quantize = [(quantize_wj, j, g) for g in range(G)]
+            quantize = [(quantize_wj, j, g, c, n) for g in range(G)]
             vector += [job for job in interleave[:1] + weave(interleave[1:], quantize) if job not in scalar]
         vector += [reader(tensor[-1])]
 
@@ -462,6 +469,7 @@ def tile_robust_information_block_s13_kernel(
         position = {engine: 0 for engine in lists}
         written = set()
         taken = {name: [] for name in DEPTH}
+        taken["rows"] = [(key, (transpose_d, key[0], key[1] + d_raw[key].shape[1] - 1)) for key in d_raw]
         while any(position[engine] < len(lists[engine]) for engine in lists):
             before = len(written)
             for engine in lists:

@@ -27,10 +27,10 @@ J = A // W
 R = F // P
 
 HALF = W // 2
+BANKS = 8
 
 PIECES = [(0, HALF), (HALF, HALF), (W, HALF), (W + HALF, HALF), (2 * W, W)]
 DEPTH = {
-    "bank": 8,
     "plane": 4,
     "interleaved": 2,
     "sorted_d": 4,
@@ -51,7 +51,7 @@ def tile_robust_information_block_s13_kernel(
     with ExitStack() as ctx:
         keep = ctx.enter_context(tc.tile_pool(name="keep", bufs=1))
         stage = ctx.enter_context(tc.tile_pool(name="stage", bufs=1))
-        psum = ctx.enter_context(tc.psum_pool(name="psum", bufs=DEPTH["bank"]))
+        psum = ctx.enter_context(tc.psum_pool(name="psum", bufs=1))
         ctx.enter_context(tc.manual_schedule())
 
         def staged(name, shape, dtype):
@@ -61,8 +61,10 @@ def tile_robust_information_block_s13_kernel(
             skip = start // size
             return keep.tile([P, skip + columns], dtype, name=name, align_bytes=256)[:, skip:]
 
+        held = {}
+
         def bank():
-            return psum.tile([P, W], F32, name="bank")
+            return psum.tile([P, W], F32, name=made["next_bank"])
 
         r_rows = keep.tile([P, P * T], BF16, name="r_rows")
         nc.gpsimd.memset(r_rows[:].bitcast(I32), 0)
@@ -354,7 +356,7 @@ def tile_robust_information_block_s13_kernel(
         def takes(job):
             kind, index = job[0], job[1:]
             if kind == widen:
-                last_reader = (warm, WARM_BEFORE_D) if index[:2] == (0, 0) else (interleave_basis,) + index[:2]
+                last_reader = [job for job in tensor if job[0] == warm][-1] if index[:2] == (0, 0) else (interleave_basis,) + index[:2]
                 return ("plane", index[:2]), last_reader
             if kind == interleave_basis:
                 return ("interleaved", index), (quantize_basis,) + index
@@ -419,15 +421,17 @@ def tile_robust_information_block_s13_kernel(
         def reader(job):
             if job[0] == stage_2:
                 return (store,) + job[1:4]
+            if job[0] in (warm, turn_r):
+                return takes(job)[1]
             return (copy_d if job[0] == transpose_d else weigh,) + job[1:]
 
         def fills_bank(job):
-            return job[0] in (transpose_d, stage_1) or (job[0] == stage_2 and job[5] == G)
+            return job[0] != stage_2 or job[5] == G
 
-        tensor = [(warm, k) for k in range(WARM_BEFORE_D)] + group(transpose_d, 0)[:2]
-        tensor += [(turn_r,), (warm, WARM_BEFORE_D)] + group(transpose_d, 0)[2:]
-        tensor += half_cell(0, 0, 0)[:2] + group(transpose_d, 1)[:2] + half_cell(0, 0, 0)[2:] + half_cell(0, 0, 1)
-        tensor += group(transpose_d, 1)[2:] + group(transpose_d, 2) + cell(stage_1, 0, 1)
+        tensor = [(warm, k) for k in range(WARM_BEFORE_D)] + group(transpose_d, 0)[:2] + [(turn_r,), (warm, WARM_BEFORE_D)] + group(transpose_d, 0)[2:]
+        tensor += half_cell(0, 0, 0)[:2] + group(transpose_d, 1)[:2] + half_cell(0, 0, 0)[2:]
+        tensor += group(transpose_d, 1)[2:] + half_cell(0, 0, 1)
+        tensor += group(transpose_d, 2) + cell(stage_1, 0, 1)
         tensor += group(transpose_d, 3) + cell(stage_1, 0, 2) + cell(stage_1, 0, 3)
         for h in range(2):
             tensor += half_cell(1, 0, h) + half_cell(1, 1, h)
@@ -439,31 +443,33 @@ def tile_robust_information_block_s13_kernel(
             tensor += [(stage_2, f, c, n, g, g + 1) for g in range(G) for f in range(2)]
             tensor += [(stage_2, f, c, n, 0, G) for f in range(2, R)]
 
-        empty = [reader(job) for job in tensor[:-1] if fills_bank(job)]
-        scalar = planes(0, 0)[3:] + planes(1, 0)[:2] + planes(0, 1)[2:] + planes(1, 0)[2:] + planes(1, 1)[:1]
-        scalar += empty[:2] + planes(1, 1)[1:3] + empty[2:]
-        k = scalar.index(cell(weigh, 0, 1)[2])
-        scalar[k : k + 4] = scalar[k + 2 : k + 4] + scalar[k : k + 2]
+        empty = [reader(job) for job in tensor if fills_bank(job)]
+        k = empty.index(cell(weigh, 0, 1)[2])
+        empty[k : k + 6] = empty[k + 2 : k + 6] + empty[k : k + 2]
+        freed = [job for job in empty if job in [takes(other)[1] for other in tensor]]
+        last_copies = empty[-3::2]
+        helped = {3: cell(weigh, 0, 3)[3:], 4: []}
+        scalar = planes(1, 0) + planes(1, 1)
+        scalar += [job for job in empty if job[0] in (copy_d, weigh, store) and job not in helped[3] + helped[4] + last_copies]
         k = scalar.index(reader(blocks(0)[-1])) + 1
         halves = [(interleave_wj, J - 1, G - 1, h * HALF, HALF) for h in range(2)]
-        scalar = scalar[:k] + halves[:1] + scalar[k : k + 2] + halves[1:] + scalar[k + 2 :]
+        scalar = scalar[: k + 2] + halves[1:] + scalar[k + 2 :]
 
-        vector = planes(0, 0)[:3] + planes(0, 1)[:2] + finish(0)
-        vector += weave(singles(0)[:2] + planes(1, 1)[3:] + finish(1)[:1], [(weights, k) for k in range(4)])
-        vector += weave(singles(0)[2:], finish(1)[1:])
-        vector += sorts(1)[1:] + pairs(1)[:1] + sorts(2) + [(interleave_wj, 0, 0, 0, HALF)]
-        vector += weave(sorts(3), pairs(1)[1:])
+        vector = planes(0, 0) + finish(0)[:1] + planes(0, 1) + finish(0)[2:3] + finish(0)[1:2]
+        vector += weave(singles(0)[:1] + finish(0)[3:] + singles(0)[1:2] + finish(1)[:1], [(weights, k) for k in range(4)])
+        vector += singles(0)[2:] + finish(1)[1:]
+        vector += weave(sorts(2), pairs(1)) + weave(sorts(3), [(interleave_wj, 0, 0, 0, HALF)])
         vector += pairs(2)[:1] + planes(2, 0) + pairs(2)[1:] + planes(2, 1)
         vector += finish(2)[:2] + pairs(3)[:1] + finish(2)[2:] + pairs(3)[1:]
         for i in (3, 4):
-            vector += planes(i, 0) + planes(i, 1) + finish(i)
+            vector += planes(i, 0) + planes(i, 1) + finish(i) + helped[i]
         for j, c, n in ((0, 0, W), (1, 0, W), (2, 0, HALF), (2, HALF, HALF)):
             interleave = [(interleave_wj, j, g, c, n) for g in range(G)]
             if j == 0:
                 interleave[0] = (interleave_wj, 0, 0, HALF, HALF)
             quantize = [(quantize_wj, j, g, c, n) for g in range(G)]
             vector += [job for job in interleave[:1] + weave(interleave[1:], quantize) if job not in scalar]
-        vector += [reader(tensor[-1])]
+        vector += last_copies
 
         lists = {"tensor": tensor, "scalar": scalar, "vector": vector}
         position = {engine: 0 for engine in lists}
@@ -481,7 +487,14 @@ def tile_robust_information_block_s13_kernel(
                 take = takes(job)
                 if take is not None:
                     (name, index), last_reader = take
-                    if index not in [entry[0] for entry in taken[name]]:
+                    if name == "bank":
+                        if last_reader not in held:
+                            n = len(held) - BANKS
+                            if n >= 0 and freed[n] not in written:
+                                continue
+                            made["next_bank"] = held[freed[n]] if n >= 0 else "bank_%d" % len(held)
+                            held[last_reader] = made["next_bank"]
+                    elif index not in [entry[0] for entry in taken[name]]:
                         if len(taken[name]) >= DEPTH[name] and taken[name][-DEPTH[name]][1] not in written:
                             continue
                         taken[name].append((index, last_reader))

@@ -41,7 +41,8 @@ DEPTH = {
     "rows": 10,
 }
 MOVING_WORDS, MOVING_SCALES, STATIONARY_WORDS, STATIONARY_SCALES = 0, 64, 128, 192
-WARM_ON_ZEROS, WARM_BEFORE_D = 2, 5
+ZW = (0, 0, 0)
+WARM_ON_ZEROS = len(ZW)
 
 
 def tile_robust_information_block_s13_kernel(
@@ -102,7 +103,8 @@ def tile_robust_information_block_s13_kernel(
 
         for s in range(S):
             load_codes(0, 1, s)
-        for t in range(T):
+            load_d(0, s, 1)
+        for t in range(S, T):
             load_d(0, t, 1)
         for g in range(1, G):
             load_d(g, 0, 2)
@@ -314,8 +316,11 @@ def tile_robust_information_block_s13_kernel(
             nc.sync.dma_start(out=out[f * P : (f + 1) * P, c : c + n], in_=h[:])
 
         def warm(engine, k):
-            source = zeros[:] if k < WARM_ON_ZEROS else made["plane", 0, 0][:].rearrange("p t n -> p (t n)")[:, :W]
-            nc.tensor.matmul(out=bank()[:], lhsT=source[:, :P], rhs=source, start=True, stop=True)
+            if k < WARM_ON_ZEROS:
+                source = zeros[:].bitcast(F32)
+            else:
+                source = made["plane", 0, 0][:].rearrange("p t n -> p (t n)")[:, :W]
+            nc.tensor.matmul(out=bank()[:, : source.shape[1]], lhsT=source[:, :P], rhs=source, start=True, stop=True)
 
         def needs(job):
             kind, index = job[0], job[1:]
@@ -428,7 +433,9 @@ def tile_robust_information_block_s13_kernel(
         def fills_bank(job):
             return job[0] != stage_2 or job[5] == G
 
-        tensor = [(warm, k) for k in range(WARM_BEFORE_D)] + group(transpose_d, 0)[:2] + [(turn_r,), (warm, WARM_BEFORE_D)] + group(transpose_d, 0)[2:]
+        d0 = group(transpose_d, 0)
+        w = [(warm, k) for k in range(WARM_ON_ZEROS, WARM_ON_ZEROS + 4)]
+        tensor = [(warm, k) for k in range(WARM_ON_ZEROS)] + d0[:1] + w[:2] + d0[1:2] + [(turn_r,)] + w[2:3] + d0[2:]
         tensor += half_cell(0, 0, 0)[:2] + group(transpose_d, 1)[:2] + half_cell(0, 0, 0)[2:]
         tensor += group(transpose_d, 1)[2:] + half_cell(0, 0, 1)
         tensor += group(transpose_d, 2) + cell(stage_1, 0, 1)
@@ -447,17 +454,16 @@ def tile_robust_information_block_s13_kernel(
         k = empty.index(cell(weigh, 0, 1)[2])
         empty[k : k + 6] = empty[k + 2 : k + 6] + empty[k : k + 2]
         freed = [job for job in empty if job in [takes(other)[1] for other in tensor]]
-        last_copies = empty[-3::2]
+        last_copies = empty[-5::2]
         helped = {3: cell(weigh, 0, 3)[3:], 4: []}
-        scalar = planes(1, 0) + planes(1, 1)
-        scalar += [job for job in empty if job[0] in (copy_d, weigh, store) and job not in helped[3] + helped[4] + last_copies]
+        scalar = [job for job in empty if job[0] in (copy_d, weigh, store) and job not in helped[3] + helped[4] + last_copies]
+        scalar = planes(1, 0) + scalar[:1] + planes(1, 1) + scalar[1:]
         k = scalar.index(reader(blocks(0)[-1])) + 1
         halves = [(interleave_wj, J - 1, G - 1, h * HALF, HALF) for h in range(2)]
-        scalar = scalar[: k + 2] + halves[1:] + scalar[k + 2 :]
+        scalar = scalar[: k + 0] + [(interleave_wj, J - 1, G - 2, HALF, HALF)] + scalar[k + 0 : k + 4] + halves[1:] + scalar[k + 4 :]
 
-        vector = planes(0, 0) + finish(0)[:1] + planes(0, 1) + finish(0)[2:3] + finish(0)[1:2]
-        vector += weave(singles(0)[:1] + finish(0)[3:] + singles(0)[1:2] + finish(1)[:1], [(weights, k) for k in range(4)])
-        vector += singles(0)[2:] + finish(1)[1:]
+        ws = [(weights, k) for k in range(4)]
+        vector = planes(0, 0) + finish(0)[:1] + planes(0, 1) + finish(0)[2:3] + finish(0)[1:2] + weave(singles(0)[:1] + finish(0)[3:] + singles(0)[1:2] + finish(1)[:1], ws) + singles(0)[2:] + finish(1)[1:]
         vector += weave(sorts(2), pairs(1)) + weave(sorts(3), [(interleave_wj, 0, 0, 0, HALF)])
         vector += pairs(2)[:1] + planes(2, 0) + pairs(2)[1:] + planes(2, 1)
         vector += finish(2)[:2] + pairs(3)[:1] + finish(2)[2:] + pairs(3)[1:]

@@ -87,15 +87,15 @@ def tile_robust_information_block_s13_kernel(
         codes = {}
         d_raw = {}
 
-        def load_codes(first, last, s):
+        def load_codes(first, last, s, t0=0, t1=T):
             c0 = PIECES[first][0]
             c1 = PIECES[last][0] + PIECES[last][1]
-            tile = keep.tile([P, T, c1 - c0], U8, name="codes_%d_%d" % (first, s))
-            nc.sync.dma_start(out=tile[:], in_=code_rows[s][:, :, c0:c1])
+            tile = keep.tile([P, t1 - t0, c1 - c0], U8, name="codes_%d_%d_%d" % (first, s, t0))
+            nc.sync.dma_start(out=tile[:], in_=code_rows[s][:, t0:t1, c0:c1])
             for i in range(first, last + 1):
                 c, n = PIECES[i]
-                for t in range(T):
-                    codes[i, s, t] = tile[:, t, c - c0 : c - c0 + n]
+                for t in range(t0, t1):
+                    codes[i, s, t] = tile[:, t - t0, c - c0 : c - c0 + n]
 
         def load_d(g, t, n):
             d_raw[g, t] = staged("rows", [P, n, L], BF16)
@@ -438,8 +438,7 @@ def tile_robust_information_block_s13_kernel(
         tensor = [(warm, k) for k in range(WARM_ON_ZEROS)] + d0[:1] + w[:2] + d0[1:2] + [(turn_r,)] + w[2:3] + d0[2:]
         tensor += half_cell(0, 0, 0)[:2] + group(transpose_d, 1)[:2] + half_cell(0, 0, 0)[2:]
         tensor += group(transpose_d, 1)[2:] + half_cell(0, 0, 1)
-        tensor += group(transpose_d, 2) + cell(stage_1, 0, 1)
-        tensor += group(transpose_d, 3) + cell(stage_1, 0, 2) + cell(stage_1, 0, 3)
+        tensor += group(transpose_d, 2) + cell(stage_1, 0, 1) + group(transpose_d, 3) + cell(stage_1, 0, 2) + cell(stage_1, 0, 3)
         for h in range(2):
             tensor += half_cell(1, 0, h) + half_cell(1, 1, h)
         tensor += cell(stage_1, 1, 2) + cell(stage_1, 1, 3) + cell(stage_1, 2, 0) + cell(stage_1, 2, 1)
@@ -454,19 +453,18 @@ def tile_robust_information_block_s13_kernel(
         k = empty.index(cell(weigh, 0, 1)[2])
         empty[k : k + 6] = empty[k + 2 : k + 6] + empty[k : k + 2]
         freed = [job for job in empty if job in [takes(other)[1] for other in tensor]]
-        last_copies = empty[-5::2]
+        last_copies = empty[-3::2]
         helped = {3: cell(weigh, 0, 3)[3:], 4: []}
         scalar = [job for job in empty if job[0] in (copy_d, weigh, store) and job not in helped[3] + helped[4] + last_copies]
         scalar = planes(1, 0) + scalar[:1] + planes(1, 1) + scalar[1:]
         k = scalar.index(reader(blocks(0)[-1])) + 1
         halves = [(interleave_wj, J - 1, G - 1, h * HALF, HALF) for h in range(2)]
-        scalar = scalar[: k + 0] + [(interleave_wj, J - 1, G - 2, HALF, HALF)] + scalar[k + 0 : k + 4] + halves[1:] + scalar[k + 4 :]
+        scalar = scalar[: k + 2] + halves[1:] + scalar[k + 2 :]
 
         ws = [(weights, k) for k in range(4)]
-        vector = planes(0, 0) + finish(0)[:1] + planes(0, 1) + finish(0)[2:3] + finish(0)[1:2] + weave(singles(0)[:1] + finish(0)[3:] + singles(0)[1:2] + finish(1)[:1], ws) + singles(0)[2:] + finish(1)[1:]
+        vector = planes(0, 0) + finish(0)[:1] + planes(0, 1) + finish(0)[2:3] + finish(0)[1:2] + weave(singles(0)[:1] + finish(0)[3:] + singles(0)[1:2] + finish(1)[:1], ws) + singles(0)[2:] + finish(1)[1:2] + sorts(1)[1:] + finish(1)[2:]
         vector += weave(sorts(2), pairs(1)) + weave(sorts(3), [(interleave_wj, 0, 0, 0, HALF)])
-        vector += pairs(2)[:1] + planes(2, 0) + pairs(2)[1:] + planes(2, 1)
-        vector += finish(2)[:2] + pairs(3)[:1] + finish(2)[2:] + pairs(3)[1:]
+        vector += pairs(2)[:1] + planes(2, 0) + pairs(2)[1:] + planes(2, 1) + pairs(3)[:1] + finish(2)[:2] + pairs(3)[1:] + finish(2)[2:]
         for i in (3, 4):
             vector += planes(i, 0) + planes(i, 1) + finish(i) + helped[i]
         for j, c, n in ((0, 0, W), (1, 0, W), (2, 0, HALF), (2, HALF, HALF)):

@@ -27,6 +27,11 @@ J = A // W
 R = F // P
 
 HALF = W // 2
+GATED = {(0, 1): "interleaved"}
+ASIDE = ((0, 0), (2, 3))
+PAIRED = ()
+DI = 2
+PASSES = [(0, 1, 2, 3), (3, 0, 1, 2), (0, 1, 2, 3)]
 BANKS = 8
 
 PIECES = [(0, HALF), (HALF, HALF), (W, HALF), (W + HALF, HALF), (2 * W, W)]
@@ -37,11 +42,12 @@ DEPTH = {
     "d_grouped": 3,
     "wj_plane": 8,
     "wj": 3,
+    "wj_chain": 1,
     "wj_aside": 1,
     "rows": 10,
 }
 MOVING_WORDS, MOVING_SCALES, STATIONARY_WORDS, STATIONARY_SCALES = 0, 64, 128, 192
-ZW = (0, 0, 0)
+ZW = (0, 0)
 WARM_ON_ZEROS = len(ZW)
 
 
@@ -103,8 +109,7 @@ def tile_robust_information_block_s13_kernel(
 
         for s in range(S):
             load_codes(0, 1, s)
-            load_d(0, s, 1)
-        for t in range(S, T):
+        for t in range(T):
             load_d(0, t, 1)
         for g in range(1, G):
             load_d(g, 0, 2)
@@ -132,6 +137,8 @@ def tile_robust_information_block_s13_kernel(
         def copy_on(engine, dst, src):
             if engine == "vector":
                 nc.vector.tensor_copy(out=dst, in_=src)
+            elif engine == "gpsimd":
+                nc.gpsimd.tensor_scalar(out=dst, in0=src, scalar1=1.0, scalar2=0.0, op0=MULT, op1=ADD)
             else:
                 nc.scalar.copy(out=dst, in_=src)
 
@@ -142,6 +149,9 @@ def tile_robust_information_block_s13_kernel(
                 nc.scalar.activation(out=dst, in_=src, func=COPY, scale=scale)
 
         def interleave_on(engine, dst, src):
+            if engine == "gpsimd":
+                copy_on(engine, dst, src.rearrange("p t n -> p n t"))
+                return
             copy_on(
                 engine,
                 dst.rearrange("p (c i) t -> p c t i", i=2),
@@ -242,11 +252,10 @@ def tile_robust_information_block_s13_kernel(
             )
 
         def stage_1(engine, g, t, c, n):
-            if n == W or t % 2 == 0:
-                whole = bank()
-                made["jb_bank", g, t, c] = whole[:, :n]
-                if n < W:
-                    made["jb_bank", g, t + 1, c] = whole[:, n:]
+            if t % (W // n) == 0:
+                made["whole_bank", g, t, c] = bank()
+                for k in range(W // n):
+                    made["jb_bank", g, t + k, c] = made["whole_bank", g, t, c][:, k * n : (k + 1) * n]
             for s in range(S):
                 stationary = slice((t * S + s) * P, (t * S + s + 1) * P)
                 nc.tensor.matmul_mx(
@@ -270,16 +279,46 @@ def tile_robust_information_block_s13_kernel(
                 weight[:, g * T + t : g * T + t + 1],
             )
 
+        def direct(engine, j, g, c, n):
+            if ("wj", j, g) not in made:
+                made["wj", j, g] = staged(wj_name(j, g), [P, W, T], BF16)
+            nc.vector.tensor_tensor(
+                out=made["wj", j, g][:, c : c + n, :].rearrange("p (c i) t -> p c t i", i=DI),
+                in0=made["whole_bank", g, 0, j * W + c][:].rearrange("p (t c i) -> p c t i", t=T, i=DI),
+                in1=weight[:, g * T : (g + 1) * T].unsqueeze(1).unsqueeze(3).to_broadcast([P, n // DI, T, DI]),
+                op=MULT,
+            )
+
+        def pairwise(engine, g, t, c, n):
+            j = c // W
+            if ("wj_plane", j, g) not in made:
+                made["wj_plane", j, g] = staged("wj_plane", [P, 2, W, 2], BF16)
+            nc.vector.tensor_tensor(
+                out=made["wj_plane", j, g][:, t // 2, c % W : c % W + n, :].rearrange("p (c i) e -> p c e i", i=DI),
+                in0=made["whole_bank", g, t - 1, c][:].rearrange("p (e c i) -> p c e i", e=2, i=DI),
+                in1=weight[:, g * T + t - 1 : g * T + t + 1].unsqueeze(1).unsqueeze(3).to_broadcast([P, n // DI, 2, DI]),
+                op=MULT,
+            )
+
         def interleavers(j, g):
-            return [job for job in vector + scalar if job[:3] == (interleave_wj, j, g)]
+            return [job for job in vector + scalar + gpsimd if job[0] in (interleave_wj, direct) and job[1:3] == (j, g)]
 
         def wj_name(j, g):
-            return "wj_aside" if (j, g) in ((0, 0), (J - 1, G - 1)) else "wj"
+            if (j, g) in GATED:
+                return GATED[j, g]
+            return "wj_aside" if (j, g) in ASIDE else "wj"
 
         def interleave_wj(engine, j, g, c, n):
             if ("wj", j, g) not in made:
                 made["wj", j, g] = staged(wj_name(j, g), [P, W, T], BF16)
-            interleave_on(engine, made["wj", j, g][:, c : c + n, :], made["wj_plane", j, g][:, :, c : c + n])
+            if (j, g) in PAIRED:
+                words = made["wj_plane", j, g][:].rearrange("p u n e -> p u (n e)").bitcast(F32)
+                nc.vector.tensor_copy(
+                    out=made["wj", j, g][:, c : c + n, :].bitcast(F32).rearrange("p (c i) u -> p c u i", i=2),
+                    in_=words[:, :, c : c + n].rearrange("p u (c i) -> p c u i", i=2),
+                )
+            else:
+                interleave_on(engine, made["wj", j, g][:, c : c + n, :], made["wj_plane", j, g][:, :, c : c + n])
 
         def quantize_wj(engine, j, g, c, n):
             nc.vector.quantize_mx(
@@ -298,7 +337,8 @@ def tile_robust_information_block_s13_kernel(
             j = c // W
             if first == 0:
                 made["h_bank", f, c] = bank()
-            for g in range(first, last):
+            for k in range(first, last):
+                g = PASSES[j][k]
                 moving = slice(g * W + c % W, g * W + c % W + n)
                 nc.tensor.matmul_mx(
                     out=made["h_bank", f, c][:, :n],
@@ -306,8 +346,8 @@ def tile_robust_information_block_s13_kernel(
                     lhsT_scale=ja_scale[:, g * F + f * P : g * F + (f + 1) * P],
                     rhs=wj_q[j][:, moving].bitcast(FP8X4),
                     rhs_scale=wj_s[j][:, moving],
-                    start=(g == 0),
-                    stop=(g == G - 1),
+                    start=(k == 0),
+                    stop=(k == G - 1),
                 )
 
         def store(engine, f, c, n):
@@ -317,7 +357,7 @@ def tile_robust_information_block_s13_kernel(
 
         def warm(engine, k):
             if k < WARM_ON_ZEROS:
-                source = zeros[:].bitcast(F32)
+                source = zeros[:]
             else:
                 source = made["plane", 0, 0][:].rearrange("p t n -> p (t n)")[:, :W]
             nc.tensor.matmul(out=bank()[:, : source.shape[1]], lhsT=source[:, :P], rhs=source, start=True, stop=True)
@@ -343,17 +383,21 @@ def tile_robust_information_block_s13_kernel(
                 g, t, c, n = index
                 pieces = [i for i in range(len(PIECES)) if PIECES[i][0] < c + n and c < PIECES[i][0] + PIECES[i][1]]
                 return [quantiser_of(g, t)] + [(quantize_basis, i, s) for i in pieces for s in range(S)]
-            if kind == weigh:
+            if kind in (weigh, pairwise):
                 g, t, c, n = index
                 return [(stage_1, g, t if n == W else t | 1, c, n), (weights, 3)]
             if kind == interleave_wj:
                 j, g = index[:2]
-                return [other for other in vector + scalar if other[:2] == (weigh, g) and other[3] // W == j]
+                before = [gate[j, g]] if (j, g) in gate else []
+                return before + [other for other in vector + scalar if other[:2] in ((weigh, g), (pairwise, g)) and other[3] // W == j]
+            if kind == direct:
+                j, g, c, n = index
+                return [(stage_1, g, T - 1, j * W + c, n)]
             if kind == quantize_wj:
                 return [other for other in interleavers(*index[:2]) if overlap(other, *index[2:])]
             if kind == stage_2:
                 f, c, n, first, last = index
-                return [q for g in range(first, last) for q in quantisers(c // W, g) if overlap(q, c % W, n)]
+                return [q for g in PASSES[c // W][first:last] for q in quantisers(c // W, g) if overlap(q, c % W, n)]
             if kind == store:
                 return [other for other in tensor if other[:4] == (stage_2,) + index]
             return []
@@ -373,12 +417,12 @@ def tile_robust_information_block_s13_kernel(
                 return ("d_grouped", quantiser_of(*index)), quantiser_of(*index)
             if kind == stage_1:
                 g, t, c, n = index
-                last = t if n == W else t | 1
-                return ("bank", (stage_1, g, last, c)), (weigh, g, last, c, n)
-            if kind == weigh:
+                last = t | (W // n - 1)
+                return ("bank", (stage_1, g, last, c)), reader((stage_1, g, last, c, n))
+            if kind in (weigh, pairwise):
                 j, g = index[2] // W, index[0]
                 return ("wj_plane", (j, g)), interleavers(j, g)[-1]
-            if kind == interleave_wj:
+            if kind in (interleave_wj, direct):
                 return (wj_name(*index[:2]), index[:2]), quantisers(*index[:2])[-1]
             if kind == stage_2:
                 return ("bank", job[:4]), (store,) + index[:3]
@@ -395,6 +439,15 @@ def tile_robust_information_block_s13_kernel(
 
         def half_cell(j, g, h):
             return [(stage_1, g, t, j * W + h * HALF, HALF) for t in range(T)]
+
+        def quarters(j, g):
+            return [(stage_1, g, t, j * W + c, W // T) for c in range(0, W, W // T) for t in range(T)]
+
+        def directs(j, g):
+            return [(direct, j, g, c, W // T) for c in range(0, W, W // T)]
+
+        def pairwises(j, g):
+            return [(pairwise, g, t, j * W + h * HALF, HALF) for h in range(2) for t in (1, 3)]
 
         def group(kind, g):
             return [(kind, g, t) for t in range(T)]
@@ -428,54 +481,64 @@ def tile_robust_information_block_s13_kernel(
                 return (store,) + job[1:4]
             if job[0] in (warm, turn_r):
                 return takes(job)[1]
+            if job[0] == stage_1 and job[4] == W // T:
+                return (direct, job[3] // W, job[1], job[3] % W, job[4])
+            if job[0] == stage_1 and (job[3] // W, job[1]) in PAIRED:
+                return (pairwise,) + job[1:]
             return (copy_d if job[0] == transpose_d else weigh,) + job[1:]
 
         def fills_bank(job):
+            if job[0] == stage_1 and job[4] == W // T:
+                return job[2] == T - 1
+            if job[0] == stage_1 and (job[3] // W, job[1]) in PAIRED:
+                return job[2] % 2 == 1
             return job[0] != stage_2 or job[5] == G
 
         d0 = group(transpose_d, 0)
         w = [(warm, k) for k in range(WARM_ON_ZEROS, WARM_ON_ZEROS + 4)]
-        tensor = [(warm, k) for k in range(WARM_ON_ZEROS)] + d0[:1] + w[:2] + d0[1:2] + [(turn_r,)] + w[2:3] + d0[2:]
+        tensor = [(warm, k) for k in range(WARM_ON_ZEROS)] + w[:3] + d0[:2] + [(turn_r,)] + w[3:] + d0[2:]
         tensor += half_cell(0, 0, 0)[:2] + group(transpose_d, 1)[:2] + half_cell(0, 0, 0)[2:]
         tensor += group(transpose_d, 1)[2:] + half_cell(0, 0, 1)
         tensor += group(transpose_d, 2) + cell(stage_1, 0, 1) + group(transpose_d, 3) + cell(stage_1, 0, 2) + cell(stage_1, 0, 3)
         for h in range(2):
             tensor += half_cell(1, 0, h) + half_cell(1, 1, h)
-        tensor += cell(stage_1, 1, 2) + cell(stage_1, 1, 3) + cell(stage_1, 2, 0) + cell(stage_1, 2, 1)
-        last_members = cell(stage_1, 2, 2) + cell(stage_1, 2, 3)
-        for f in range(R):
-            tensor += last_members[2 * f : 2 * f + 2] + blocks(0)[f : f + 1]
-        for c, n in ((W, W), (2 * W, HALF), (2 * W + HALF, HALF)):
+        tensor += cell(stage_1, 1, 2) + quarters(1, 3) + cell(stage_1, 2, 0) + cell(stage_1, 2, 1) + cell(stage_1, 2, 2) + cell(stage_1, 2, 3)
+        for c, n in ((0, W), (W, W), (2 * W, HALF), (2 * W + HALF, HALF)):
             tensor += [(stage_2, f, c, n, g, g + 1) for g in range(G) for f in range(2)]
             tensor += [(stage_2, f, c, n, 0, G) for f in range(2, R)]
 
         empty = [reader(job) for job in tensor if fills_bank(job)]
         k = empty.index(cell(weigh, 0, 1)[2])
         empty[k : k + 6] = empty[k + 2 : k + 6] + empty[k : k + 2]
+        k = empty.index(cell(weigh, 1, 2)[0])
+        empty[k : k + 8] = weave(empty[k : k + 4], empty[k + 4 : k + 8])
         freed = [job for job in empty if job in [takes(other)[1] for other in tensor]]
         last_copies = empty[-3::2]
-        helped = {3: cell(weigh, 0, 3)[3:], 4: []}
+        helped = {3: [], 4: []}
         scalar = [job for job in empty if job[0] in (copy_d, weigh, store) and job not in helped[3] + helped[4] + last_copies]
-        scalar = planes(1, 0) + scalar[:1] + planes(1, 1) + scalar[1:]
-        k = scalar.index(reader(blocks(0)[-1])) + 1
+        scalar = planes(1, 0) + planes(1, 1) + scalar
+        k = scalar.index(cell(weigh, 2, 3)[3]) + 1
         halves = [(interleave_wj, J - 1, G - 1, h * HALF, HALF) for h in range(2)]
-        scalar = scalar[: k + 2] + halves[1:] + scalar[k + 2 :]
+        scalar = scalar[:k] + halves[:1] + scalar[k : k + 4] + halves[1:] + scalar[k + 4 :]
 
         ws = [(weights, k) for k in range(4)]
-        vector = planes(0, 0) + finish(0)[:1] + planes(0, 1) + finish(0)[2:3] + finish(0)[1:2] + weave(singles(0)[:1] + finish(0)[3:] + singles(0)[1:2] + finish(1)[:1], ws) + singles(0)[2:] + finish(1)[1:2] + sorts(1)[1:] + finish(1)[2:]
+        vector = planes(0, 0) + finish(0)[:1] + planes(0, 1) + finish(0)[2:3] + finish(0)[1:2] + weave(singles(0)[:1] + finish(0)[3:] + singles(0)[1:2] + finish(1)[:1], ws) + singles(0)[2:] + finish(1)[1:]
         vector += weave(sorts(2), pairs(1)) + weave(sorts(3), [(interleave_wj, 0, 0, 0, HALF)])
         vector += pairs(2)[:1] + planes(2, 0) + pairs(2)[1:] + planes(2, 1) + pairs(3)[:1] + finish(2)[:2] + pairs(3)[1:] + finish(2)[2:]
         for i in (3, 4):
             vector += planes(i, 0) + planes(i, 1) + finish(i) + helped[i]
-        for j, c, n in ((0, 0, W), (1, 0, W), (2, 0, HALF), (2, HALF, HALF)):
-            interleave = [(interleave_wj, j, g, c, n) for g in range(G)]
-            if j == 0:
-                interleave[0] = (interleave_wj, 0, 0, HALF, HALF)
-            quantize = [(quantize_wj, j, g, c, n) for g in range(G)]
-            vector += [job for job in interleave[:1] + weave(interleave[1:], quantize) if job not in scalar]
+        def il(j, g, c=0, n=W):
+            return [(interleave_wj, j, g, c, n)]
+
+        def q(j, g, c=0, n=W):
+            return [(quantize_wj, j, g, c, n)]
+
+        vector += directs(1, 3) + il(0, 1, 384, 128) + il(0, 0, HALF, HALF) + q(1, 3) + q(0, 1) + il(0, 2) + q(0, 0) + il(0, 3) + q(0, 2) + il(1, 0) + q(0, 3) + il(1, 1) + q(1, 0) + il(1, 2) + q(1, 1) + il(2, 0, 0, HALF) + q(1, 2) + il(2, 1, 0, HALF) + q(2, 0, 0, HALF) + il(2, 2, 0, HALF) + q(2, 1, 0, HALF) + q(2, 2, 0, HALF) + q(2, 3, 0, HALF) + il(2, 0, HALF, HALF) + il(2, 1, HALF, HALF) + q(2, 0, HALF, HALF) + il(2, 2, HALF, HALF) + q(2, 1, HALF, HALF) + q(2, 2, HALF, HALF) + q(2, 3, HALF, HALF)
+        gpsimd = il(0, 1, 0, 384)
+        gate = {(0, 1): (quantize_basis, 4, 0)}
         vector += last_copies
 
-        lists = {"tensor": tensor, "scalar": scalar, "vector": vector}
+        lists = {"tensor": tensor, "scalar": scalar, "vector": vector, "gpsimd": gpsimd}
         position = {engine: 0 for engine in lists}
         written = set()
         taken = {name: [] for name in DEPTH}

@@ -84,7 +84,10 @@ def tile_robust_information_block_s13_kernel(
 
         row_scale = keep.tile([P, S, T], F32, name="row_scale")
         nc.scalar.dma_start(out=row_scale[:], in_=basis_scale.rearrange("(s p t) o -> p s (t o)", p=P, t=T))
-        nc.scalar.dma_start(out=r_rows[:G, :], in_=r.rearrange("(g e) -> g e", g=G))
+        def load_r(queue):
+            queue.dma_start(out=r_rows[:G, :], in_=r.rearrange("(g e) -> g e", g=G))
+
+
         table = keep.tile([P, 1], F32, name="table")
         nc.scalar.activation(out=table[:], in_=zeros[:, 0:1], func=COPY)
 
@@ -107,8 +110,9 @@ def tile_robust_information_block_s13_kernel(
             d_raw[g, t] = staged("rows", [P, n, L], BF16)
             nc.sync.dma_start(out=d_raw[g, t][:], in_=d_rows[g][:, t : t + n, :])
 
-        for s in range(S):
-            load_codes(0, 1, s)
+        load_codes(0, 1, 0)
+        load_r(nc.sync)
+        load_codes(0, 1, 1)
         for t in range(T):
             load_d(0, t, 1)
         for g in range(1, G):
@@ -496,9 +500,9 @@ def tile_robust_information_block_s13_kernel(
 
         d0 = group(transpose_d, 0)
         w = [(warm, k) for k in range(WARM_ON_ZEROS, WARM_ON_ZEROS + 4)]
-        tensor = [(warm, k) for k in range(WARM_ON_ZEROS)] + w[:3] + d0[:2] + [(turn_r,)] + w[3:] + d0[2:]
+        tensor = [(warm, k) for k in range(WARM_ON_ZEROS)] + [(turn_r,)] + w[:3] + d0[:2] + w[3:] + d0[2:]
         tensor += half_cell(0, 0, 0)[:2] + group(transpose_d, 1)[:2] + half_cell(0, 0, 0)[2:]
-        tensor += group(transpose_d, 1)[2:] + half_cell(0, 0, 1)
+        tensor += half_cell(0, 0, 1) + group(transpose_d, 1)[2:]
         tensor += group(transpose_d, 2) + cell(stage_1, 0, 1) + group(transpose_d, 3) + cell(stage_1, 0, 2) + cell(stage_1, 0, 3)
         for h in range(2):
             tensor += half_cell(1, 0, h) + half_cell(1, 1, h)
@@ -516,14 +520,14 @@ def tile_robust_information_block_s13_kernel(
         last_copies = empty[-3::2]
         helped = {3: [], 4: []}
         scalar = [job for job in empty if job[0] in (copy_d, weigh, store) and job not in helped[3] + helped[4] + last_copies]
-        scalar = planes(1, 0) + planes(1, 1) + scalar
+        scalar = planes(1, 0) + planes(0, 1)[3:] + planes(1, 1)[:3] + scalar[:2] + planes(1, 1)[3:] + scalar[2:]
         k = scalar.index(cell(weigh, 2, 3)[3]) + 1
         halves = [(interleave_wj, J - 1, G - 1, h * HALF, HALF) for h in range(2)]
         scalar = scalar[:k] + halves[:1] + scalar[k : k + 4] + halves[1:] + scalar[k + 4 :]
 
         ws = [(weights, k) for k in range(4)]
-        vector = planes(0, 0) + finish(0)[:1] + planes(0, 1) + finish(0)[2:3] + finish(0)[1:2] + weave(singles(0)[:1] + finish(0)[3:] + singles(0)[1:2] + finish(1)[:1], ws) + singles(0)[2:] + finish(1)[1:]
-        vector += weave(sorts(2), pairs(1)) + weave(sorts(3), [(interleave_wj, 0, 0, 0, HALF)])
+        vector = planes(0, 0) + ws[:1] + finish(0)[:1] + ws[1:2] + planes(0, 1)[:3] + ws[2:3] + finish(0)[2:3] + ws[3:] + finish(0)[1:2] + singles(0)[:1] + finish(0)[3:] + singles(0)[1:2] + finish(1)[:1] + singles(0)[2:3] + finish(1)[1:2] + singles(0)[3:] + finish(1)[2:] + sorts(1)[1:]
+        vector += weave(sorts(2), pairs(1)[:1]) + [(interleave_wj, 0, 0, 0, HALF)] + weave(sorts(3), pairs(1)[1:])
         vector += pairs(2)[:1] + planes(2, 0) + pairs(2)[1:] + planes(2, 1) + pairs(3)[:1] + finish(2)[:2] + pairs(3)[1:] + finish(2)[2:]
         for i in (3, 4):
             vector += planes(i, 0) + planes(i, 1) + finish(i) + helped[i]

@@ -27,12 +27,12 @@ J = A // W
 R = F // P
 
 HALF = W // 2
-GATED = {(0, 1): "interleaved"}
-ASIDE = ((0, 0), (2, 3))
-PAIRED = ()
-DI = 2
-PASSES = [(0, 1, 2, 3), (3, 0, 1, 2), (0, 1, 2, 3)]
+QUARTER = W // T
 BANKS = 8
+
+DIRECT = (1, 3)
+BESIDE, BESIDE_COLUMNS = (0, 1), 3 * QUARTER
+PASSES = [(0, 1, 2, 3), (3, 0, 1, 2), (0, 1, 2, 3)]
 
 PIECES = [(0, HALF), (HALF, HALF), (W, HALF), (W + HALF, HALF), (2 * W, W)]
 DEPTH = {
@@ -42,13 +42,11 @@ DEPTH = {
     "d_grouped": 3,
     "wj_plane": 8,
     "wj": 3,
-    "wj_chain": 1,
     "wj_aside": 1,
     "rows": 10,
 }
 MOVING_WORDS, MOVING_SCALES, STATIONARY_WORDS, STATIONARY_SCALES = 0, 64, 128, 192
-ZW = (0, 0)
-WARM_ON_ZEROS = len(ZW)
+WARM_ON_ZEROS, WARM_ON_PLANES = 2, 4
 
 
 def tile_robust_information_block_s13_kernel(
@@ -73,21 +71,18 @@ def tile_robust_information_block_s13_kernel(
         def bank():
             return psum.tile([P, W], F32, name=made["next_bank"])
 
-        r_rows = keep.tile([P, P * T], BF16, name="r_rows")
-        nc.gpsimd.memset(r_rows[:].bitcast(I32), 0)
-        ident = keep.tile([P, P], F32, name="ident")
-        make_identity(nc, ident[:])
         zeros = keep.tile([P, W], BF16, name="zeros")
         nc.vector.memset(zeros[:], 0.0)
+        r_rows = keep.tile([P, P * T], BF16, name="r_rows")
+        nc.vector.memset(r_rows[: P - G, :].bitcast(I32), 0)
+        ident = keep.tile([P, P], F32, name="ident")
+        make_identity(nc, ident[:])
         ja_scale = placed("ja_scale", G * F, U8, 1, STATIONARY_SCALES)
         nc.vector.memset(ja_scale[:].bitcast(I32), 0)
 
         row_scale = keep.tile([P, S, T], F32, name="row_scale")
         nc.scalar.dma_start(out=row_scale[:], in_=basis_scale.rearrange("(s p t) o -> p s (t o)", p=P, t=T))
-        def load_r(queue):
-            queue.dma_start(out=r_rows[:G, :], in_=r.rearrange("(g e) -> g e", g=G))
-
-
+        nc.scalar.dma_start(out=r_rows[P - G :, :], in_=r.rearrange("(g e) -> g e", g=G))
         table = keep.tile([P, 1], F32, name="table")
         nc.scalar.activation(out=table[:], in_=zeros[:, 0:1], func=COPY)
 
@@ -96,23 +91,22 @@ def tile_robust_information_block_s13_kernel(
         codes = {}
         d_raw = {}
 
-        def load_codes(first, last, s, t0=0, t1=T):
+        def load_codes(first, last, s):
             c0 = PIECES[first][0]
             c1 = PIECES[last][0] + PIECES[last][1]
-            tile = keep.tile([P, t1 - t0, c1 - c0], U8, name="codes_%d_%d_%d" % (first, s, t0))
-            nc.sync.dma_start(out=tile[:], in_=code_rows[s][:, t0:t1, c0:c1])
+            tile = keep.tile([P, T, c1 - c0], U8, name="codes_%d_%d" % (first, s))
+            nc.sync.dma_start(out=tile[:], in_=code_rows[s][:, :, c0:c1])
             for i in range(first, last + 1):
                 c, n = PIECES[i]
-                for t in range(t0, t1):
-                    codes[i, s, t] = tile[:, t - t0, c - c0 : c - c0 + n]
+                for t in range(T):
+                    codes[i, s, t] = tile[:, t, c - c0 : c - c0 + n]
 
         def load_d(g, t, n):
             d_raw[g, t] = staged("rows", [P, n, L], BF16)
             nc.sync.dma_start(out=d_raw[g, t][:], in_=d_rows[g][:, t : t + n, :])
 
-        load_codes(0, 1, 0)
-        load_r(nc.sync)
-        load_codes(0, 1, 1)
+        for s in range(S):
+            load_codes(0, 1, s)
         for t in range(T):
             load_d(0, t, 1)
         for g in range(1, G):
@@ -176,7 +170,7 @@ def tile_robust_information_block_s13_kernel(
             if step == 0:
                 nc.vector.tensor_copy(
                     out=residual[:].bitcast(F32).rearrange("p (g u) -> p g u", u=2),
-                    in_=made["r_bank"][:, : 2 * P].rearrange("p (u k) -> p k u", u=2)[:, :G, :],
+                    in_=made["r_bank"][:, : 2 * P].rearrange("p (u k) -> p k u", u=2)[:, P - G :, :],
                 )
             elif step == 1:
                 nc.vector.tensor_tensor(out=square[:], in0=residual[:], in1=residual[:], op=MULT)
@@ -287,20 +281,9 @@ def tile_robust_information_block_s13_kernel(
             if ("wj", j, g) not in made:
                 made["wj", j, g] = staged(wj_name(j, g), [P, W, T], BF16)
             nc.vector.tensor_tensor(
-                out=made["wj", j, g][:, c : c + n, :].rearrange("p (c i) t -> p c t i", i=DI),
-                in0=made["whole_bank", g, 0, j * W + c][:].rearrange("p (t c i) -> p c t i", t=T, i=DI),
-                in1=weight[:, g * T : (g + 1) * T].unsqueeze(1).unsqueeze(3).to_broadcast([P, n // DI, T, DI]),
-                op=MULT,
-            )
-
-        def pairwise(engine, g, t, c, n):
-            j = c // W
-            if ("wj_plane", j, g) not in made:
-                made["wj_plane", j, g] = staged("wj_plane", [P, 2, W, 2], BF16)
-            nc.vector.tensor_tensor(
-                out=made["wj_plane", j, g][:, t // 2, c % W : c % W + n, :].rearrange("p (c i) e -> p c e i", i=DI),
-                in0=made["whole_bank", g, t - 1, c][:].rearrange("p (e c i) -> p c e i", e=2, i=DI),
-                in1=weight[:, g * T + t - 1 : g * T + t + 1].unsqueeze(1).unsqueeze(3).to_broadcast([P, n // DI, 2, DI]),
+                out=made["wj", j, g][:, c : c + n, :].rearrange("p (c i) t -> p c t i", i=2),
+                in0=made["whole_bank", g, 0, j * W + c][:].rearrange("p (t c i) -> p c t i", t=T, i=2),
+                in1=weight[:, g * T : (g + 1) * T].unsqueeze(1).unsqueeze(3).to_broadcast([P, n // 2, T, 2]),
                 op=MULT,
             )
 
@@ -308,21 +291,14 @@ def tile_robust_information_block_s13_kernel(
             return [job for job in vector + scalar + gpsimd if job[0] in (interleave_wj, direct) and job[1:3] == (j, g)]
 
         def wj_name(j, g):
-            if (j, g) in GATED:
-                return GATED[j, g]
-            return "wj_aside" if (j, g) in ASIDE else "wj"
+            if (j, g) == BESIDE:
+                return "interleaved"
+            return "wj_aside" if (j, g) in ((0, 0), (J - 1, G - 1)) else "wj"
 
         def interleave_wj(engine, j, g, c, n):
             if ("wj", j, g) not in made:
                 made["wj", j, g] = staged(wj_name(j, g), [P, W, T], BF16)
-            if (j, g) in PAIRED:
-                words = made["wj_plane", j, g][:].rearrange("p u n e -> p u (n e)").bitcast(F32)
-                nc.vector.tensor_copy(
-                    out=made["wj", j, g][:, c : c + n, :].bitcast(F32).rearrange("p (c i) u -> p c u i", i=2),
-                    in_=words[:, :, c : c + n].rearrange("p u (c i) -> p c u i", i=2),
-                )
-            else:
-                interleave_on(engine, made["wj", j, g][:, c : c + n, :], made["wj_plane", j, g][:, :, c : c + n])
+            interleave_on(engine, made["wj", j, g][:, c : c + n, :], made["wj_plane", j, g][:, :, c : c + n])
 
         def quantize_wj(engine, j, g, c, n):
             nc.vector.quantize_mx(
@@ -361,7 +337,7 @@ def tile_robust_information_block_s13_kernel(
 
         def warm(engine, k):
             if k < WARM_ON_ZEROS:
-                source = zeros[:]
+                source = zeros[:].bitcast(F32)
             else:
                 source = made["plane", 0, 0][:].rearrange("p t n -> p (t n)")[:, :W]
             nc.tensor.matmul(out=bank()[:, : source.shape[1]], lhsT=source[:, :P], rhs=source, start=True, stop=True)
@@ -387,13 +363,13 @@ def tile_robust_information_block_s13_kernel(
                 g, t, c, n = index
                 pieces = [i for i in range(len(PIECES)) if PIECES[i][0] < c + n and c < PIECES[i][0] + PIECES[i][1]]
                 return [quantiser_of(g, t)] + [(quantize_basis, i, s) for i in pieces for s in range(S)]
-            if kind in (weigh, pairwise):
+            if kind == weigh:
                 g, t, c, n = index
                 return [(stage_1, g, t if n == W else t | 1, c, n), (weights, 3)]
             if kind == interleave_wj:
                 j, g = index[:2]
-                before = [gate[j, g]] if (j, g) in gate else []
-                return before + [other for other in vector + scalar if other[:2] in ((weigh, g), (pairwise, g)) and other[3] // W == j]
+                before = [(quantize_basis, len(PIECES) - 1, 0)] if (j, g) == BESIDE else []
+                return before + [other for other in scalar if other[:2] == (weigh, g) and other[3] // W == j]
             if kind == direct:
                 j, g, c, n = index
                 return [(stage_1, g, T - 1, j * W + c, n)]
@@ -423,7 +399,7 @@ def tile_robust_information_block_s13_kernel(
                 g, t, c, n = index
                 last = t | (W // n - 1)
                 return ("bank", (stage_1, g, last, c)), reader((stage_1, g, last, c, n))
-            if kind in (weigh, pairwise):
+            if kind == weigh:
                 j, g = index[2] // W, index[0]
                 return ("wj_plane", (j, g)), interleavers(j, g)[-1]
             if kind in (interleave_wj, direct):
@@ -445,13 +421,10 @@ def tile_robust_information_block_s13_kernel(
             return [(stage_1, g, t, j * W + h * HALF, HALF) for t in range(T)]
 
         def quarters(j, g):
-            return [(stage_1, g, t, j * W + c, W // T) for c in range(0, W, W // T) for t in range(T)]
+            return [(stage_1, g, t, j * W + c, QUARTER) for c in range(0, W, QUARTER) for t in range(T)]
 
         def directs(j, g):
-            return [(direct, j, g, c, W // T) for c in range(0, W, W // T)]
-
-        def pairwises(j, g):
-            return [(pairwise, g, t, j * W + h * HALF, HALF) for h in range(2) for t in (1, 3)]
+            return [(direct, j, g, c, QUARTER) for c in range(0, W, QUARTER)]
 
         def group(kind, g):
             return [(kind, g, t) for t in range(T)]
@@ -485,61 +458,66 @@ def tile_robust_information_block_s13_kernel(
                 return (store,) + job[1:4]
             if job[0] in (warm, turn_r):
                 return takes(job)[1]
-            if job[0] == stage_1 and job[4] == W // T:
+            if job[0] == stage_1 and job[4] == QUARTER:
                 return (direct, job[3] // W, job[1], job[3] % W, job[4])
-            if job[0] == stage_1 and (job[3] // W, job[1]) in PAIRED:
-                return (pairwise,) + job[1:]
             return (copy_d if job[0] == transpose_d else weigh,) + job[1:]
 
         def fills_bank(job):
-            if job[0] == stage_1 and job[4] == W // T:
+            if job[0] == stage_1 and job[4] == QUARTER:
                 return job[2] == T - 1
-            if job[0] == stage_1 and (job[3] // W, job[1]) in PAIRED:
-                return job[2] % 2 == 1
             return job[0] != stage_2 or job[5] == G
 
-        d0 = group(transpose_d, 0)
-        w = [(warm, k) for k in range(WARM_ON_ZEROS, WARM_ON_ZEROS + 4)]
-        tensor = [(warm, k) for k in range(WARM_ON_ZEROS)] + [(turn_r,)] + w[:3] + d0[:2] + w[3:] + d0[2:]
-        tensor += half_cell(0, 0, 0)[:2] + group(transpose_d, 1)[:2] + half_cell(0, 0, 0)[2:]
-        tensor += half_cell(0, 0, 1) + group(transpose_d, 1)[2:]
-        tensor += group(transpose_d, 2) + cell(stage_1, 0, 1) + group(transpose_d, 3) + cell(stage_1, 0, 2) + cell(stage_1, 0, 3)
+        warm_ups = [(warm, k) for k in range(WARM_ON_ZEROS + WARM_ON_PLANES)]
+        tensor = warm_ups[:-2] + [(turn_r,)] + warm_ups[-2:-1]
+        tensor += group(transpose_d, 0)[:2] + warm_ups[-1:] + group(transpose_d, 0)[2:]
+        tensor += half_cell(0, 0, 0)[:2] + group(transpose_d, 1)[:2] + half_cell(0, 0, 0)[2:] + half_cell(0, 0, 1)
+        tensor += group(transpose_d, 1)[2:] + group(transpose_d, 2)[:2] + cell(stage_1, 0, 1)[:2]
+        tensor += group(transpose_d, 2)[2:] + cell(stage_1, 0, 1)[2:]
+        tensor += group(transpose_d, 3) + cell(stage_1, 0, 2) + cell(stage_1, 0, 3)
         for h in range(2):
             tensor += half_cell(1, 0, h) + half_cell(1, 1, h)
-        tensor += cell(stage_1, 1, 2) + quarters(1, 3) + cell(stage_1, 2, 0) + cell(stage_1, 2, 1) + cell(stage_1, 2, 2) + cell(stage_1, 2, 3)
+        tensor += cell(stage_1, 1, 2) + quarters(*DIRECT)
+        for g in range(G):
+            tensor += cell(stage_1, 2, g)
         for c, n in ((0, W), (W, W), (2 * W, HALF), (2 * W + HALF, HALF)):
             tensor += [(stage_2, f, c, n, g, g + 1) for g in range(G) for f in range(2)]
             tensor += [(stage_2, f, c, n, 0, G) for f in range(2, R)]
+        tensor[-1:] = [(stage_2, R - 1, c, QUARTER, 0, G) for c in (A - HALF, A - QUARTER)]
 
         empty = [reader(job) for job in tensor if fills_bank(job)]
-        k = empty.index(cell(weigh, 0, 1)[2])
-        empty[k : k + 6] = empty[k + 2 : k + 6] + empty[k : k + 2]
+        for pair, ahead in ((cell(weigh, 0, 1)[:2], 2), (cell(weigh, 0, 1)[2:], T)):
+            k = empty.index(pair[0])
+            empty[k : k + 2 + ahead] = empty[k + 2 : k + 2 + ahead] + pair
         k = empty.index(cell(weigh, 1, 2)[0])
-        empty[k : k + 8] = weave(empty[k : k + 4], empty[k + 4 : k + 8])
+        empty[k : k + 2 * T] = weave(empty[k : k + T], empty[k + T : k + 2 * T])
         freed = [job for job in empty if job in [takes(other)[1] for other in tensor]]
+
         last_copies = empty[-3::2]
-        helped = {3: [], 4: []}
-        scalar = [job for job in empty if job[0] in (copy_d, weigh, store) and job not in helped[3] + helped[4] + last_copies]
-        scalar = planes(1, 0) + planes(0, 1)[3:] + planes(1, 1)[:3] + scalar[:2] + planes(1, 1)[3:] + scalar[2:]
-        k = scalar.index(cell(weigh, 2, 3)[3]) + 1
+        scalar = [job for job in empty if job[0] in (copy_d, weigh, store) and job not in last_copies]
+        scalar = planes(1, 0)[:3] + planes(0, 1)[2:] + planes(1, 1)[:3] + scalar[:2] + planes(1, 1)[3:] + scalar[2:]
+        k = scalar.index(cell(weigh, J - 1, G - 1)[-1]) + 1
         halves = [(interleave_wj, J - 1, G - 1, h * HALF, HALF) for h in range(2)]
-        scalar = scalar[:k] + halves[:1] + scalar[k : k + 4] + halves[1:] + scalar[k + 4 :]
+        scalar = scalar[:k] + halves[:1] + scalar[k : k + R] + halves[1:] + scalar[k + R :]
 
-        ws = [(weights, k) for k in range(4)]
-        vector = planes(0, 0) + ws[:1] + finish(0)[:1] + ws[1:2] + planes(0, 1)[:3] + ws[2:3] + finish(0)[2:3] + ws[3:] + finish(0)[1:2] + singles(0)[:1] + finish(0)[3:] + singles(0)[1:2] + finish(1)[:1] + singles(0)[2:3] + finish(1)[1:2] + singles(0)[3:] + finish(1)[2:] + sorts(1)[1:]
-        vector += weave(sorts(2), pairs(1)[:1]) + [(interleave_wj, 0, 0, 0, HALF)] + weave(sorts(3), pairs(1)[1:])
-        vector += pairs(2)[:1] + planes(2, 0) + pairs(2)[1:] + planes(2, 1) + pairs(3)[:1] + finish(2)[:2] + pairs(3)[1:] + finish(2)[2:]
+        steps = [(weights, k) for k in range(4)]
+        vector = planes(0, 0) + planes(1, 0)[3:] + finish(0)[:1] + steps[:1] + planes(0, 1)[:2]
+        vector += weave(steps[1:], [finish(0)[2], finish(0)[1]])
+        vector += weave(singles(0), [finish(0)[3], finish(1)[0], finish(1)[1]]) + finish(1)[2:]
+        vector += sorts(1)[1:] + pairs(1)[:1] + sorts(2)[:1] + [(interleave_wj, 0, 0, 0, HALF)] + sorts(2)[1:]
+        vector += weave(pairs(1)[1:] + pairs(2)[:1], sorts(3))
+        vector += planes(2, 0) + pairs(2)[1:] + planes(2, 1) + pairs(3)[:1] + finish(2)[:2] + pairs(3)[1:] + finish(2)[2:]
         for i in (3, 4):
-            vector += planes(i, 0) + planes(i, 1) + finish(i) + helped[i]
-        def il(j, g, c=0, n=W):
-            return [(interleave_wj, j, g, c, n)]
-
-        def q(j, g, c=0, n=W):
-            return [(quantize_wj, j, g, c, n)]
-
-        vector += directs(1, 3) + il(0, 1, 384, 128) + il(0, 0, HALF, HALF) + q(1, 3) + q(0, 1) + il(0, 2) + q(0, 0) + il(0, 3) + q(0, 2) + il(1, 0) + q(0, 3) + il(1, 1) + q(1, 0) + il(1, 2) + q(1, 1) + il(2, 0, 0, HALF) + q(1, 2) + il(2, 1, 0, HALF) + q(2, 0, 0, HALF) + il(2, 2, 0, HALF) + q(2, 1, 0, HALF) + q(2, 2, 0, HALF) + q(2, 3, 0, HALF) + il(2, 0, HALF, HALF) + il(2, 1, HALF, HALF) + q(2, 0, HALF, HALF) + il(2, 2, HALF, HALF) + q(2, 1, HALF, HALF) + q(2, 2, HALF, HALF) + q(2, 3, HALF, HALF)
-        gpsimd = il(0, 1, 0, 384)
-        gate = {(0, 1): (quantize_basis, 4, 0)}
+            vector += planes(i, 0) + planes(i, 1) + finish(i)
+        gpsimd = [(interleave_wj,) + BESIDE + (0, BESIDE_COLUMNS)]
+        vector += directs(*DIRECT) + [(interleave_wj,) + BESIDE + (BESIDE_COLUMNS, W - BESIDE_COLUMNS)]
+        vector += [(interleave_wj, 0, 0, HALF, HALF), (quantize_wj,) + DIRECT + (0, W), (quantize_wj,) + BESIDE + (0, W)]
+        parts = [(0, 2, 0, W), (0, 3, 0, W)] + [(1, g, 0, W) for g in range(3)] + [(2, g, 0, HALF) for g in range(G)]
+        vector += weave(
+            [(interleave_wj,) + part for part in parts[:-1]], [(quantize_wj,) + part for part in [(0, 0, 0, W)] + parts]
+        )
+        parts = [(2, g, HALF, HALF) for g in range(G)]
+        interleave = [(interleave_wj,) + part for part in parts[:-1]]
+        vector += interleave[:1] + weave(interleave[1:], [(quantize_wj,) + part for part in parts])
         vector += last_copies
 
         lists = {"tensor": tensor, "scalar": scalar, "vector": vector, "gpsimd": gpsimd}

@@ -30,9 +30,8 @@ HALF = W // 2
 QUARTER = W // T
 BANKS = 8
 
-DIRECT = (1, 3)
-BESIDE, BESIDE_COLUMNS = (0, 1), 3 * QUARTER
-PASSES = [(0, 1, 2, 3), (3, 0, 1, 2), (0, 1, 2, 3)]
+STEPPED = (J - 1, G - 1)
+SHARED = (J - 1, G - 2)
 
 PIECES = [(0, HALF), (HALF, HALF), (W, HALF), (W + HALF, HALF), (2 * W, W)]
 DEPTH = {
@@ -135,8 +134,6 @@ def tile_robust_information_block_s13_kernel(
         def copy_on(engine, dst, src):
             if engine == "vector":
                 nc.vector.tensor_copy(out=dst, in_=src)
-            elif engine == "gpsimd":
-                nc.gpsimd.tensor_scalar(out=dst, in0=src, scalar1=1.0, scalar2=0.0, op0=MULT, op1=ADD)
             else:
                 nc.scalar.copy(out=dst, in_=src)
 
@@ -147,9 +144,6 @@ def tile_robust_information_block_s13_kernel(
                 nc.scalar.activation(out=dst, in_=src, func=COPY, scale=scale)
 
         def interleave_on(engine, dst, src):
-            if engine == "gpsimd":
-                copy_on(engine, dst, src.rearrange("p t n -> p n t"))
-                return
             copy_on(
                 engine,
                 dst.rearrange("p (c i) t -> p c t i", i=2),
@@ -194,10 +188,7 @@ def tile_robust_information_block_s13_kernel(
             made["interleaved", i, s] = staged("interleaved", [P, PIECES[i][1], T], BF16)
             if in_pairs(i):
                 words = made["plane", i, s][:].rearrange("p u n e -> p u (n e)").bitcast(F32)
-                nc.vector.tensor_copy(
-                    out=made["interleaved", i, s][:].bitcast(F32).rearrange("p (c i) u -> p c u i", i=2),
-                    in_=words.rearrange("p u (c i) -> p c u i", i=2),
-                )
+                interleave_on(engine, made["interleaved", i, s][:].bitcast(F32), words)
             else:
                 interleave_on(engine, made["interleaved", i, s][:], made["plane", i, s][:])
 
@@ -249,12 +240,12 @@ def tile_robust_information_block_s13_kernel(
                 in_=made["d_grouped", g, t][:].rearrange("p m c -> p (m c)"),
             )
 
-        def stage_1(engine, g, t, c, n):
-            if t % (W // n) == 0:
-                made["whole_bank", g, t, c] = bank()
+        def passes_1(g, t, c, n, passes):
+            if ("jb_bank", g, t, c) not in made:
+                whole = bank()
                 for k in range(W // n):
-                    made["jb_bank", g, t + k, c] = made["whole_bank", g, t, c][:, k * n : (k + 1) * n]
-            for s in range(S):
+                    made["jb_bank", g, t + k, c] = whole[:, k * n : (k + 1) * n]
+            for s in passes:
                 stationary = slice((t * S + s) * P, (t * S + s + 1) * P)
                 nc.tensor.matmul_mx(
                     out=made["jb_bank", g, t, c],
@@ -266,39 +257,38 @@ def tile_robust_information_block_s13_kernel(
                     stop=(s == S - 1),
                 )
 
+        def open_1(engine, g, t, c, n):
+            passes_1(g, t, c, n, [0])
+
+        def stage_1(engine, g, t, c, n):
+            passes_1(g, t, c, n, range(1 if (open_1, g, t, c, n) in tensor else 0, S))
+
         def weigh(engine, g, t, c, n):
             j = c // W
             if ("wj_plane", j, g) not in made:
-                made["wj_plane", j, g] = staged("wj_plane", [P, T, W], BF16)
+                made["wj_plane", j, g] = staged("wj_plane", [P, 2, W, 2] if (j, g) == STEPPED else [P, T, W], BF16)
+            tile, columns = made["wj_plane", j, g], slice(c % W, c % W + n)
             scale_on(
                 engine,
-                made["wj_plane", j, g][:, t, c % W : c % W + n],
+                tile[:, t // 2, columns, t % 2] if (j, g) == STEPPED else tile[:, t, columns],
                 made["jb_bank", g, t, c],
                 weight[:, g * T + t : g * T + t + 1],
             )
 
-        def direct(engine, j, g, c, n):
-            if ("wj", j, g) not in made:
-                made["wj", j, g] = staged(wj_name(j, g), [P, W, T], BF16)
-            nc.vector.tensor_tensor(
-                out=made["wj", j, g][:, c : c + n, :].rearrange("p (c i) t -> p c t i", i=2),
-                in0=made["whole_bank", g, 0, j * W + c][:].rearrange("p (t c i) -> p c t i", t=T, i=2),
-                in1=weight[:, g * T : (g + 1) * T].unsqueeze(1).unsqueeze(3).to_broadcast([P, n // 2, T, 2]),
-                op=MULT,
-            )
-
         def interleavers(j, g):
-            return [job for job in vector + scalar + gpsimd if job[0] in (interleave_wj, direct) and job[1:3] == (j, g)]
+            return [job for job in vector + scalar if job[:3] == (interleave_wj, j, g)]
 
         def wj_name(j, g):
-            if (j, g) == BESIDE:
-                return "interleaved"
-            return "wj_aside" if (j, g) in ((0, 0), (J - 1, G - 1)) else "wj"
+            return "wj_aside" if (j, g) in ((0, 0), SHARED) else "wj"
 
         def interleave_wj(engine, j, g, c, n):
             if ("wj", j, g) not in made:
                 made["wj", j, g] = staged(wj_name(j, g), [P, W, T], BF16)
-            interleave_on(engine, made["wj", j, g][:, c : c + n, :], made["wj_plane", j, g][:, :, c : c + n])
+            if (j, g) == STEPPED:
+                words = made["wj_plane", j, g][:].rearrange("p u n e -> p u (n e)").bitcast(F32)
+                interleave_on(engine, made["wj", j, g][:, c : c + n, :].bitcast(F32), words[:, :, c : c + n])
+            else:
+                interleave_on(engine, made["wj", j, g][:, c : c + n, :], made["wj_plane", j, g][:, :, c : c + n])
 
         def quantize_wj(engine, j, g, c, n):
             nc.vector.quantize_mx(
@@ -317,8 +307,7 @@ def tile_robust_information_block_s13_kernel(
             j = c // W
             if first == 0:
                 made["h_bank", f, c] = bank()
-            for k in range(first, last):
-                g = PASSES[j][k]
+            for g in range(first, last):
                 moving = slice(g * W + c % W, g * W + c % W + n)
                 nc.tensor.matmul_mx(
                     out=made["h_bank", f, c][:, :n],
@@ -326,8 +315,8 @@ def tile_robust_information_block_s13_kernel(
                     lhsT_scale=ja_scale[:, g * F + f * P : g * F + (f + 1) * P],
                     rhs=wj_q[j][:, moving].bitcast(FP8X4),
                     rhs_scale=wj_s[j][:, moving],
-                    start=(k == 0),
-                    stop=(k == G - 1),
+                    start=(g == 0),
+                    stop=(g == G - 1),
                 )
 
         def store(engine, f, c, n):
@@ -359,25 +348,22 @@ def tile_robust_information_block_s13_kernel(
             if kind == quantize_d:
                 g, t, n = index
                 return [(copy_d, g, t + k) for k in range(n)]
-            if kind == stage_1:
+            if kind in (stage_1, open_1):
                 g, t, c, n = index
                 pieces = [i for i in range(len(PIECES)) if PIECES[i][0] < c + n and c < PIECES[i][0] + PIECES[i][1]]
-                return [quantiser_of(g, t)] + [(quantize_basis, i, s) for i in pieces for s in range(S)]
+                passes = range(S if kind == stage_1 else 1)
+                return [quantiser_of(g, t)] + [(quantize_basis, i, s) for i in pieces for s in passes]
             if kind == weigh:
                 g, t, c, n = index
                 return [(stage_1, g, t if n == W else t | 1, c, n), (weights, 3)]
             if kind == interleave_wj:
                 j, g = index[:2]
-                before = [(quantize_basis, len(PIECES) - 1, 0)] if (j, g) == BESIDE else []
-                return before + [other for other in scalar if other[:2] == (weigh, g) and other[3] // W == j]
-            if kind == direct:
-                j, g, c, n = index
-                return [(stage_1, g, T - 1, j * W + c, n)]
+                return [other for other in vector + scalar if other[:2] == (weigh, g) and other[3] // W == j]
             if kind == quantize_wj:
                 return [other for other in interleavers(*index[:2]) if overlap(other, *index[2:])]
             if kind == stage_2:
                 f, c, n, first, last = index
-                return [q for g in PASSES[c // W][first:last] for q in quantisers(c // W, g) if overlap(q, c % W, n)]
+                return [q for g in range(first, last) for q in quantisers(c // W, g) if overlap(q, c % W, n)]
             if kind == store:
                 return [other for other in tensor if other[:4] == (stage_2,) + index]
             return []
@@ -385,8 +371,7 @@ def tile_robust_information_block_s13_kernel(
         def takes(job):
             kind, index = job[0], job[1:]
             if kind == widen:
-                last_reader = [job for job in tensor if job[0] == warm][-1] if index[:2] == (0, 0) else (interleave_basis,) + index[:2]
-                return ("plane", index[:2]), last_reader
+                return ("plane", index[:2]), warm_ups[-1] if index[:2] == (0, 0) else (interleave_basis,) + index[:2]
             if kind == interleave_basis:
                 return ("interleaved", index), (quantize_basis,) + index
             if kind == sort_words:
@@ -395,14 +380,14 @@ def tile_robust_information_block_s13_kernel(
                 return ("bank", job), (copy_d,) + index
             if kind == copy_d:
                 return ("d_grouped", quantiser_of(*index)), quantiser_of(*index)
-            if kind == stage_1:
+            if kind in (stage_1, open_1):
                 g, t, c, n = index
                 last = t | (W // n - 1)
-                return ("bank", (stage_1, g, last, c)), reader((stage_1, g, last, c, n))
+                return ("bank", (stage_1, g, last, c)), (weigh, g, last, c, n)
             if kind == weigh:
                 j, g = index[2] // W, index[0]
                 return ("wj_plane", (j, g)), interleavers(j, g)[-1]
-            if kind in (interleave_wj, direct):
+            if kind == interleave_wj:
                 return (wj_name(*index[:2]), index[:2]), quantisers(*index[:2])[-1]
             if kind == stage_2:
                 return ("bank", job[:4]), (store,) + index[:3]
@@ -419,12 +404,6 @@ def tile_robust_information_block_s13_kernel(
 
         def half_cell(j, g, h):
             return [(stage_1, g, t, j * W + h * HALF, HALF) for t in range(T)]
-
-        def quarters(j, g):
-            return [(stage_1, g, t, j * W + c, QUARTER) for c in range(0, W, QUARTER) for t in range(T)]
-
-        def directs(j, g):
-            return [(direct, j, g, c, QUARTER) for c in range(0, W, QUARTER)]
 
         def group(kind, g):
             return [(kind, g, t) for t in range(T)]
@@ -458,14 +437,10 @@ def tile_robust_information_block_s13_kernel(
                 return (store,) + job[1:4]
             if job[0] in (warm, turn_r):
                 return takes(job)[1]
-            if job[0] == stage_1 and job[4] == QUARTER:
-                return (direct, job[3] // W, job[1], job[3] % W, job[4])
             return (copy_d if job[0] == transpose_d else weigh,) + job[1:]
 
         def fills_bank(job):
-            if job[0] == stage_1 and job[4] == QUARTER:
-                return job[2] == T - 1
-            return job[0] != stage_2 or job[5] == G
+            return job[0] != open_1 and (job[0] != stage_2 or job[5] == G)
 
         warm_ups = [(warm, k) for k in range(WARM_ON_ZEROS + WARM_ON_PLANES)]
         tensor = warm_ups[:-2] + [(turn_r,)] + warm_ups[-2:-1]
@@ -474,12 +449,14 @@ def tile_robust_information_block_s13_kernel(
         tensor += group(transpose_d, 1)[2:] + group(transpose_d, 2)[:2] + cell(stage_1, 0, 1)[:2]
         tensor += group(transpose_d, 2)[2:] + cell(stage_1, 0, 1)[2:]
         tensor += group(transpose_d, 3) + cell(stage_1, 0, 2) + cell(stage_1, 0, 3)
-        for h in range(2):
-            tensor += half_cell(1, 0, h) + half_cell(1, 1, h)
-        tensor += cell(stage_1, 1, 2) + quarters(*DIRECT)
-        for g in range(G):
+        tensor += half_cell(1, 0, 0) + half_cell(1, 1, 0) + [(open_1, 0, t, W + HALF, HALF) for t in (0, 2)]
+        tensor += half_cell(1, 0, 1) + half_cell(1, 1, 1)
+        tensor += cell(stage_1, 1, 2) + cell(stage_1, 1, 3)
+        for g in range(G - 1):
             tensor += cell(stage_1, 2, g)
-        for c, n in ((0, W), (W, W), (2 * W, HALF), (2 * W + HALF, HALF)):
+        tensor += blocks(0)[:1] + cell(stage_1, *STEPPED)[:2] + blocks(0)[1:2] + cell(stage_1, *STEPPED)[2:]
+        tensor += blocks(0)[2:]
+        for c, n in ((W, W), (2 * W, HALF), (2 * W + HALF, HALF)):
             tensor += [(stage_2, f, c, n, g, g + 1) for g in range(G) for f in range(2)]
             tensor += [(stage_2, f, c, n, 0, G) for f in range(2, R)]
         tensor[-1:] = [(stage_2, R - 1, c, QUARTER, 0, G) for c in (A - HALF, A - QUARTER)]
@@ -488,39 +465,34 @@ def tile_robust_information_block_s13_kernel(
         for pair, ahead in ((cell(weigh, 0, 1)[:2], 2), (cell(weigh, 0, 1)[2:], T)):
             k = empty.index(pair[0])
             empty[k : k + 2 + ahead] = empty[k + 2 : k + 2 + ahead] + pair
-        k = empty.index(cell(weigh, 1, 2)[0])
-        empty[k : k + 2 * T] = weave(empty[k : k + T], empty[k + T : k + 2 * T])
         freed = [job for job in empty if job in [takes(other)[1] for other in tensor]]
 
-        last_copies = empty[-3::2]
-        scalar = [job for job in empty if job[0] in (copy_d, weigh, store) and job not in last_copies]
+        last_copies = empty[-4::2]
+        helped = cell(weigh, 0, 3)[3:]
+        scalar = [job for job in empty if job[0] in (copy_d, weigh, store) and job not in last_copies + helped]
         scalar = planes(1, 0)[:3] + planes(0, 1)[2:] + planes(1, 1)[:3] + scalar[:2] + planes(1, 1)[3:] + scalar[2:]
-        k = scalar.index(cell(weigh, J - 1, G - 1)[-1]) + 1
-        halves = [(interleave_wj, J - 1, G - 1, h * HALF, HALF) for h in range(2)]
-        scalar = scalar[:k] + halves[:1] + scalar[k : k + R] + halves[1:] + scalar[k + R :]
+        k = scalar.index(reader(blocks(1)[-1]))
+        scalar[k:k] = [(interleave_wj,) + SHARED + (HALF, HALF)]
 
         steps = [(weights, k) for k in range(4)]
         vector = planes(0, 0) + planes(1, 0)[3:] + finish(0)[:1] + steps[:1] + planes(0, 1)[:2]
         vector += weave(steps[1:], [finish(0)[2], finish(0)[1]])
         vector += weave(singles(0), [finish(0)[3], finish(1)[0], finish(1)[1]]) + finish(1)[2:]
-        vector += sorts(1)[1:] + pairs(1)[:1] + sorts(2)[:1] + [(interleave_wj, 0, 0, 0, HALF)] + sorts(2)[1:]
+        vector += sorts(1)[1:] + pairs(1)[:1]
+        vector += weave(sorts(2), [(interleave_wj, 0, 0, 0, HALF), (interleave_wj, 0, 0, HALF, QUARTER)])
         vector += weave(pairs(1)[1:] + pairs(2)[:1], sorts(3))
-        vector += planes(2, 0) + pairs(2)[1:] + planes(2, 1) + pairs(3)[:1] + finish(2)[:2] + pairs(3)[1:] + finish(2)[2:]
-        for i in (3, 4):
-            vector += planes(i, 0) + planes(i, 1) + finish(i)
-        gpsimd = [(interleave_wj,) + BESIDE + (0, BESIDE_COLUMNS)]
-        vector += directs(*DIRECT) + [(interleave_wj,) + BESIDE + (BESIDE_COLUMNS, W - BESIDE_COLUMNS)]
-        vector += [(interleave_wj, 0, 0, HALF, HALF), (quantize_wj,) + DIRECT + (0, W), (quantize_wj,) + BESIDE + (0, W)]
-        parts = [(0, 2, 0, W), (0, 3, 0, W)] + [(1, g, 0, W) for g in range(3)] + [(2, g, 0, HALF) for g in range(G)]
-        vector += weave(
-            [(interleave_wj,) + part for part in parts[:-1]], [(quantize_wj,) + part for part in [(0, 0, 0, W)] + parts]
-        )
-        parts = [(2, g, HALF, HALF) for g in range(G)]
-        interleave = [(interleave_wj,) + part for part in parts[:-1]]
-        vector += interleave[:1] + weave(interleave[1:], [(quantize_wj,) + part for part in parts])
+        vector += planes(2, 0) + pairs(2)[1:] + planes(2, 1) + pairs(3)[:1]
+        vector += finish(2)[:2] + pairs(3)[1:] + finish(2)[2:]
+        vector += planes(3, 0) + planes(3, 1) + finish(3) + helped + planes(4, 0) + planes(4, 1) + finish(4)
+        for j, c, n in ((0, 0, W), (1, 0, W), (2, 0, HALF), (2, HALF, HALF)):
+            interleave = [(interleave_wj, j, g, c, n) for g in range(G)]
+            if j == 0:
+                interleave[0] = (interleave_wj, 0, 0, W - QUARTER, QUARTER)
+            quantize = [(quantize_wj, j, g, c, n) for g in range(G)]
+            vector += [job for job in interleave[:1] + weave(interleave[1:], quantize) if job not in scalar]
         vector += last_copies
 
-        lists = {"tensor": tensor, "scalar": scalar, "vector": vector, "gpsimd": gpsimd}
+        lists = {"tensor": tensor, "scalar": scalar, "vector": vector}
         position = {engine: 0 for engine in lists}
         written = set()
         taken = {name: [] for name in DEPTH}

@@ -45,7 +45,7 @@ DEPTH = {
     "rows": 10,
 }
 MOVING_WORDS, MOVING_SCALES, STATIONARY_WORDS, STATIONARY_SCALES = 0, 64, 128, 192
-WARM_ON_ZEROS, WARM_ON_PLANES = 2, 4
+WARM_ON_ZEROS, WARM_ON_PLANES = 3, 3
 
 
 def tile_robust_information_block_s13_kernel(
@@ -325,11 +325,8 @@ def tile_robust_information_block_s13_kernel(
             nc.sync.dma_start(out=out[f * P : (f + 1) * P, c : c + n], in_=h[:])
 
         def warm(engine, k):
-            if k < WARM_ON_ZEROS:
-                source = zeros[:].bitcast(F32)
-            else:
-                source = made["plane", 0, 0][:].rearrange("p t n -> p (t n)")[:, :W]
-            nc.tensor.matmul(out=bank()[:, : source.shape[1]], lhsT=source[:, :P], rhs=source, start=True, stop=True)
+            source = zeros[:] if k < WARM_ON_ZEROS else made["plane", 0, 0][:].rearrange("p t n -> p (t n)")[:, :W]
+            nc.tensor.matmul(out=bank()[:], lhsT=source[:, :P], rhs=source, start=True, stop=True)
 
         def needs(job):
             kind, index = job[0], job[1:]

@@ -44,7 +44,7 @@ DEPTH = {
     "wj_aside": 1,
     "rows": 10,
 }
-MOVING_WORDS, MOVING_SCALES, STATIONARY_WORDS, STATIONARY_SCALES = 0, 64, 128, 192
+MOVING_WORDS, MOVING_SCALES, STATIONARY_WORDS, STATIONARY_SCALES = 0, 128, 64, 0
 WARM_ON_ZEROS, WARM_ON_PLANES = 3, 3
 
 

from contextlib import ExitStack

import concourse.mybir as mybir
from concourse.masks import make_identity

E, L, A, F = 2048, 1024, 1536, 512
FLOPS = 2 * E * L * A + 2 * E * A * F

F32 = mybir.dt.float32
BF16 = mybir.dt.bfloat16
I32 = mybir.dt.int32
U32 = mybir.dt.uint32
U8 = mybir.dt.uint8
FP8 = mybir.dt.float8_e4m3fn
FP8X4 = mybir.dt.float8_e4m3fn_x4
FP4X4 = mybir.dt.float4_e2m1fn_x4
MULT = mybir.AluOpType.mult
ADD = mybir.AluOpType.add
COPY = mybir.ActivationFunctionType.Copy

P = 128
T = 4
S = L // (P * T)
G = E // (P * T)
W = 512
J = A // W
R = F // P

HALF = W // 2
QUARTER = W // T
BANKS = 8

STEPPED = (J - 1, G - 1)
SHARED = (J - 1, G - 2)

PIECES = [(0, HALF), (HALF, HALF), (W, HALF), (W + HALF, HALF), (2 * W, W)]
DEPTH = {
    "plane": 4,
    "interleaved": 2,
    "sorted_d": 4,
    "d_grouped": 3,
    "wj_plane": 8,
    "wj": 3,
    "wj_aside": 1,
    "rows": 10,
}
MOVING_WORDS, MOVING_SCALES, STATIONARY_WORDS, STATIONARY_SCALES = 0, 128, 64, 0
WARM_ON_ZEROS, WARM_ON_PLANES = 3, 3


def tile_robust_information_block_s13_kernel(
    tc, d, basis_bytes, basis_scale, r, ja_words, ja_scales, out
):
    nc = tc.nc
    with ExitStack() as ctx:
        keep = ctx.enter_context(tc.tile_pool(name="keep", bufs=1))
        stage = ctx.enter_context(tc.tile_pool(name="stage", bufs=1))
        psum = ctx.enter_context(tc.psum_pool(name="psum", bufs=1))
        ctx.enter_context(tc.manual_schedule())

        def staged(name, shape, dtype):
            return stage.tile(shape, dtype, name=name, bufs=DEPTH[name], align_bytes=64)

        def placed(name, columns, dtype, size, start):
            skip = start // size
            return keep.tile([P, skip + columns], dtype, name=name, align_bytes=256)[:, skip:]

        held = {}

        def bank():
            return psum.tile([P, W], F32, name=made["next_bank"])

        zeros = keep.tile([P, W], BF16, name="zeros")
        nc.vector.memset(zeros[:], 0.0)
        r_rows = keep.tile([P, P * T], BF16, name="r_rows")
        nc.vector.memset(r_rows[: P - G, :].bitcast(I32), 0)
        ident = keep.tile([P, P], F32, name="ident")
        make_identity(nc, ident[:])
        ja_scale = placed("ja_scale", G * F, U8, 1, STATIONARY_SCALES)
        nc.vector.memset(ja_scale[:].bitcast(I32), 0)

        row_scale = keep.tile([P, S, T], F32, name="row_scale")
        nc.scalar.dma_start(out=row_scale[:], in_=basis_scale.rearrange("(s p t) o -> p s (t o)", p=P, t=T))
        nc.scalar.dma_start(out=r_rows[P - G :, :], in_=r.rearrange("(g e) -> g e", g=G))
        table = keep.tile([P, 1], F32, name="table")
        nc.scalar.activation(out=table[:], in_=zeros[:, 0:1], func=COPY)

        code_rows = basis_bytes.rearrange("(s p t) n -> s p t n", p=P, t=T)
        d_rows = d.rearrange("(g p t) k -> g p t k", p=P, t=T)
        codes = {}
        d_raw = {}

        def load_codes(first, last, s):
            c0 = PIECES[first][0]
            c1 = PIECES[last][0] + PIECES[last][1]
            tile = keep.tile([P, T, c1 - c0], U8, name="codes_%d_%d" % (first, s))
            nc.sync.dma_start(out=tile[:], in_=code_rows[s][:, :, c0:c1])
            for i in range(first, last + 1):
                c, n = PIECES[i]
                for t in range(T):
                    codes[i, s, t] = tile[:, t, c - c0 : c - c0 + n]

        def load_d(g, t, n):
            d_raw[g, t] = staged("rows", [P, n, L], BF16)
            nc.sync.dma_start(out=d_raw[g, t][:], in_=d_rows[g][:, t : t + n, :])

        for s in range(S):
            load_codes(0, 1, s)
        for t in range(T):
            load_d(0, t, 1)
        for g in range(1, G):
            load_d(g, 0, 2)
            load_d(g, 2, 2)
        for first, last in ((2, 3), (4, 4)):
            for s in range(S):
                load_codes(first, last, s)
        ja = placed("ja", G * 2 * F, U8, 1, STATIONARY_WORDS).rearrange("p (g n) -> p g n", g=G)
        nc.sync.dma_start(out=ja[:], in_=ja_words.rearrange("g p n -> p g n"))
        for q in range(4):
            nc.sync.dma_start(
                out=ja_scale[32 * q : 32 * q + 4, :].rearrange("p (g n) -> p g n", g=G).bitcast(I32),
                in_=ja_scales[:, 4 * q : 4 * q + 4, :].rearrange("g q n -> q g n").bitcast(I32),
            )

        basis_q = [placed("basis_q_%d" % s, A, U32, 4, MOVING_WORDS) for s in range(S)]
        basis_s = [placed("basis_s_%d" % s, A, U8, 1, MOVING_SCALES) for s in range(S)]
        d_q = [placed("d_q_%d" % g, T * S * P, U32, 4, STATIONARY_WORDS) for g in range(G)]
        d_s = [placed("d_s_%d" % g, T * S * P, U8, 1, STATIONARY_SCALES) for g in range(G)]
        wj_q = [placed("wj_q_%d" % j, G * W, U32, 4, MOVING_WORDS) for j in range(J)]
        wj_s = [placed("wj_s_%d" % j, G * W, U8, 1, MOVING_SCALES) for j in range(J)]

        made = {}

        def copy_on(engine, dst, src):
            if engine == "vector":
                nc.vector.tensor_copy(out=dst, in_=src)
            else:
                nc.scalar.copy(out=dst, in_=src)

        def scale_on(engine, dst, src, scale):
            if engine == "vector":
                nc.vector.tensor_scalar(out=dst, in0=src, scalar1=scale, scalar2=None, op0=MULT)
            else:
                nc.scalar.activation(out=dst, in_=src, func=COPY, scale=scale)

        def interleave_on(engine, dst, src):
            copy_on(
                engine,
                dst.rearrange("p (c i) t -> p c t i", i=2),
                src.rearrange("p t (c i) -> p c t i", i=2),
            )

        residual = keep.tile([P, G * T], BF16, name="residual")
        square = keep.tile([P, G * T], F32, name="square")
        denominator = keep.tile([P, G * T], F32, name="denominator")
        weight = keep.tile([P, G * T], F32, name="weight")

        def turn_r(engine):
            made["r_bank"] = bank()
            for u in range(2):
                nc.tensor.transpose(made["r_bank"][:, u * P : (u + 1) * P], r_rows[:].bitcast(F32)[:, u::2], ident[:])

        def weights(engine, step):
            if step == 0:
                nc.vector.tensor_copy(
                    out=residual[:].bitcast(F32).rearrange("p (g u) -> p g u", u=2),
                    in_=made["r_bank"][:, : 2 * P].rearrange("p (u k) -> p k u", u=2)[:, P - G :, :],
                )
            elif step == 1:
                nc.vector.tensor_tensor(out=square[:], in0=residual[:], in1=residual[:], op=MULT)
            elif step == 2:
                nc.vector.tensor_scalar(out=denominator[:], in0=square[:], scalar1=1.0, scalar2=None, op0=ADD)
            else:
                nc.vector.reciprocal(out=weight[:], in_=denominator[:])

        def in_pairs(i):
            return PIECES[i][0] >= W

        def widen(engine, i, s, t):
            n = PIECES[i][1]
            if ("plane", i, s) not in made:
                made["plane", i, s] = staged("plane", [P, 2, n, 2] if in_pairs(i) else [P, T, n], BF16)
            tile = made["plane", i, s]
            dst = tile[:, t // 2, :, t % 2] if in_pairs(i) else tile[:, t, :]
            scale_on(engine, dst, codes[i, s, t].bitcast(FP8), row_scale[:, s, t : t + 1])

        def interleave_basis(engine, i, s):
            made["interleaved", i, s] = staged("interleaved", [P, PIECES[i][1], T], BF16)
            if in_pairs(i):
                words = made["plane", i, s][:].rearrange("p u n e -> p u (n e)").bitcast(F32)
                interleave_on(engine, made["interleaved", i, s][:].bitcast(F32), words)
            else:
                interleave_on(engine, made["interleaved", i, s][:], made["plane", i, s][:])

        def quantize_basis(engine, i, s):
            c, n = PIECES[i]
            nc.vector.quantize_mx(
                out=basis_q[s][:, c : c + n].bitcast(FP8X4),
                scales=basis_s[s][:, c : c + n],
                in_=made["interleaved", i, s][:].rearrange("p n t -> p (n t)"),
            )

        def sort_words(engine, g, t):
            made["sorted_d", g, t] = staged("sorted_d", [P, 2, L], BF16)
            nc.vector.tensor_copy(
                out=made["sorted_d", g, t][:].bitcast(F32).rearrange("p m (s u q) -> p (m s) u q", s=S, u=2),
                in_=d_raw[g, t][:].bitcast(F32).rearrange("p m (s q u) -> p (m s) u q", s=S, u=2),
            )

        def transpose_d(engine, g, t):
            made["d_bank", g, t] = bank()
            first = t if (g, t) in d_raw else t - 1
            for s in range(S):
                for u in range(2):
                    o = (2 * s + u) * P
                    if ("sorted_d", g, first) in made:
                        words = made["sorted_d", g, first][:, t - first, :].bitcast(F32)[:, o : o + P]
                    else:
                        words = d_raw[g, first][:, t - first, :].bitcast(F32)[:, 2 * P * s + u : 2 * P * (s + 1) : 2]
                    nc.tensor.transpose(made["d_bank", g, t][:, o : o + P], words, ident[:])

        def quantiser_of(g, t):
            return [job for job in vector if job[:2] == (quantize_d, g) and job[2] <= t < job[2] + job[3]][0]

        def copy_d(engine, g, t):
            first, n = quantiser_of(g, t)[2:]
            if t == first:
                made["d_grouped", g, first] = staged("d_grouped", [P, n, S * P * T], BF16)
            copy_on(
                engine,
                made["d_grouped", g, first][:, t - first, :].bitcast(F32).rearrange("p (s e u) -> p s e u", s=S, u=2),
                made["d_bank", g, t][:].rearrange("p (s u e) -> p s e u", s=S, u=2),
            )

        def quantize_d(engine, g, t, n):
            columns = slice(t * S * P, (t + n) * S * P)
            nc.vector.quantize_mx(
                out=d_q[g][:, columns].bitcast(FP8X4),
                scales=d_s[g][:, columns],
                in_=made["d_grouped", g, t][:].rearrange("p m c -> p (m c)"),
            )

        def passes_1(g, t, c, n, passes):
            if ("jb_bank", g, t, c) not in made:
                whole = bank()
                for k in range(W // n):
                    made["jb_bank", g, t + k, c] = whole[:, k * n : (k + 1) * n]
            for s in passes:
                stationary = slice((t * S + s) * P, (t * S + s + 1) * P)
                nc.tensor.matmul_mx(
                    out=made["jb_bank", g, t, c],
                    lhsT=d_q[g][:, stationary].bitcast(FP8X4),
                    lhsT_scale=d_s[g][:, stationary],
                    rhs=basis_q[s][:, c : c + n].bitcast(FP8X4),
                    rhs_scale=basis_s[s][:, c : c + n],
                    start=(s == 0),
                    stop=(s == S - 1),
                )

        def open_1(engine, g, t, c, n):
            passes_1(g, t, c, n, [0])

        def stage_1(engine, g, t, c, n):
            passes_1(g, t, c, n, range(1 if (open_1, g, t, c, n) in tensor else 0, S))

        def weigh(engine, g, t, c, n):
            j = c // W
            if ("wj_plane", j, g) not in made:
                made["wj_plane", j, g] = staged("wj_plane", [P, 2, W, 2] if (j, g) == STEPPED else [P, T, W], BF16)
            tile, columns = made["wj_plane", j, g], slice(c % W, c % W + n)
            scale_on(
                engine,
                tile[:, t // 2, columns, t % 2] if (j, g) == STEPPED else tile[:, t, columns],
                made["jb_bank", g, t, c],
                weight[:, g * T + t : g * T + t + 1],
            )

        def interleavers(j, g):
            return [job for job in vector + scalar if job[:3] == (interleave_wj, j, g)]

        def wj_name(j, g):
            return "wj_aside" if (j, g) in ((0, 0), SHARED) else "wj"

        def interleave_wj(engine, j, g, c, n):
            if ("wj", j, g) not in made:
                made["wj", j, g] = staged(wj_name(j, g), [P, W, T], BF16)
            if (j, g) == STEPPED:
                words = made["wj_plane", j, g][:].rearrange("p u n e -> p u (n e)").bitcast(F32)
                interleave_on(engine, made["wj", j, g][:, c : c + n, :].bitcast(F32), words[:, :, c : c + n])
            else:
                interleave_on(engine, made["wj", j, g][:, c : c + n, :], made["wj_plane", j, g][:, :, c : c + n])

        def quantize_wj(engine, j, g, c, n):
            nc.vector.quantize_mx(
                out=wj_q[j][:, g * W + c : g * W + c + n].bitcast(FP8X4),
                scales=wj_s[j][:, g * W + c : g * W + c + n],
                in_=made["wj", j, g][:, c : c + n, :].rearrange("p n t -> p (n t)"),
            )

        def quantisers(j, g):
            return [job for job in vector if job[:3] == (quantize_wj, j, g)]

        def overlap(job, c, n):
            return job[3] < c + n and c < job[3] + job[4]

        def stage_2(engine, f, c, n, first, last):
            j = c // W
            if first == 0:
                made["h_bank", f, c] = bank()
            for g in range(first, last):
                moving = slice(g * W + c % W, g * W + c % W + n)
                nc.tensor.matmul_mx(
                    out=made["h_bank", f, c][:, :n],
                    lhsT=ja[:, g, 2 * P * f : 2 * P * (f + 1)].bitcast(FP4X4),
                    lhsT_scale=ja_scale[:, g * F + f * P : g * F + (f + 1) * P],
                    rhs=wj_q[j][:, moving].bitcast(FP8X4),
                    rhs_scale=wj_s[j][:, moving],
                    start=(g == 0),
                    stop=(g == G - 1),
                )

        def store(engine, f, c, n):
            h = staged("rows", [P, n], F32)
            copy_on(engine, h[:], made["h_bank", f, c][:, :n])
            nc.sync.dma_start(out=out[f * P : (f + 1) * P, c : c + n], in_=h[:])

        def warm(engine, k):
            source = zeros[:] if k < WARM_ON_ZEROS else made["plane", 0, 0][:].rearrange("p t n -> p (t n)")[:, :W]
            nc.tensor.matmul(out=bank()[:], lhsT=source[:, :P], rhs=source, start=True, stop=True)

        def needs(job):
            kind, index = job[0], job[1:]
            if kind == warm:
                return [(widen, 0, 0, t) for t in range(W // HALF)] if index[0] >= WARM_ON_ZEROS else []
            if kind == weights:
                return [(turn_r,)] + [(weights, k) for k in range(index[0])]
            if kind == interleave_basis:
                return [(widen,) + index + (t,) for t in range(T)]
            if kind == quantize_basis:
                return [(interleave_basis,) + index]
            if kind == transpose_d:
                return [other for other in vector if other == (sort_words, index[0], index[1] // 2 * 2)]
            if kind == copy_d:
                return [(transpose_d,) + index]
            if kind == quantize_d:
                g, t, n = index
                return [(copy_d, g, t + k) for k in range(n)]
            if kind in (stage_1, open_1):
                g, t, c, n = index
                pieces = [i for i in range(len(PIECES)) if PIECES[i][0] < c + n and c < PIECES[i][0] + PIECES[i][1]]
                passes = range(S if kind == stage_1 else 1)
                return [quantiser_of(g, t)] + [(quantize_basis, i, s) for i in pieces for s in passes]
            if kind == weigh:
                g, t, c, n = index
                return [(stage_1, g, t if n == W else t | 1, c, n), (weights, 3)]
            if kind == interleave_wj:
                j, g = index[:2]
                return [other for other in vector + scalar if other[:2] == (weigh, g) and other[3] // W == j]
            if kind == quantize_wj:
                return [other for other in interleavers(*index[:2]) if overlap(other, *index[2:])]
            if kind == stage_2:
                f, c, n, first, last = index
                return [q for g in range(first, last) for q in quantisers(c // W, g) if overlap(q, c % W, n)]
            if kind == store:
                return [other for other in tensor if other[:4] == (stage_2,) + index]
            return []

        def takes(job):
            kind, index = job[0], job[1:]
            if kind == widen:
                return ("plane", index[:2]), warm_ups[-1] if index[:2] == (0, 0) else (interleave_basis,) + index[:2]
            if kind == interleave_basis:
                return ("interleaved", index), (quantize_basis,) + index
            if kind == sort_words:
                return ("sorted_d", index), (transpose_d, index[0], index[1] + 1)
            if kind == transpose_d:
                return ("bank", job), (copy_d,) + index
            if kind == copy_d:
                return ("d_grouped", quantiser_of(*index)), quantiser_of(*index)
            if kind in (stage_1, open_1):
                g, t, c, n = index
                last = t | (W // n - 1)
                return ("bank", (stage_1, g, last, c)), (weigh, g, last, c, n)
            if kind == weigh:
                j, g = index[2] // W, index[0]
                return ("wj_plane", (j, g)), interleavers(j, g)[-1]
            if kind == interleave_wj:
                return (wj_name(*index[:2]), index[:2]), quantisers(*index[:2])[-1]
            if kind == stage_2:
                return ("bank", job[:4]), (store,) + index[:3]
            if kind == store:
                return ("rows", index), job
            if kind == turn_r:
                return ("bank", job), (weights, 0)
            if kind == warm:
                return ("bank", job), job
            return None

        def cell(kind, j, g):
            return [(kind, g, t, j * W, W) for t in range(T)]

        def half_cell(j, g, h):
            return [(stage_1, g, t, j * W + h * HALF, HALF) for t in range(T)]

        def group(kind, g):
            return [(kind, g, t) for t in range(T)]

        def singles(g):
            return [(quantize_d, g, t, 1) for t in range(T)]

        def pairs(g):
            return [(quantize_d, g, t, 2) for t in (0, 2)]

        def sorts(g):
            return [(sort_words, g, t) for t in (0, 2)]

        def planes(i, s):
            return [(widen, i, s, t) for t in range(T)]

        def finish(i):
            return [(interleave_basis, i, s) for s in range(S)] + [(quantize_basis, i, s) for s in range(S)]

        def weave(first, second):
            jobs = []
            for k in range(max(len(first), len(second))):
                jobs += first[k : k + 1] + second[k : k + 1]
            return jobs

        def blocks(j):
            return [(stage_2, f, j * W, W, 0, G) for f in range(R)]

        def reader(job):
            if job[0] == stage_2:
                return (store,) + job[1:4]
            if job[0] in (warm, turn_r):
                return takes(job)[1]
            return (copy_d if job[0] == transpose_d else weigh,) + job[1:]

        def fills_bank(job):
            return job[0] != open_1 and (job[0] != stage_2 or job[5] == G)

        warm_ups = [(warm, k) for k in range(WARM_ON_ZEROS + WARM_ON_PLANES)]
        tensor = warm_ups[:-2] + [(turn_r,)] + warm_ups[-2:-1]
        tensor += group(transpose_d, 0)[:2] + warm_ups[-1:] + group(transpose_d, 0)[2:]
        tensor += half_cell(0, 0, 0)[:2] + group(transpose_d, 1)[:2] + half_cell(0, 0, 0)[2:] + half_cell(0, 0, 1)
        tensor += group(transpose_d, 1)[2:] + group(transpose_d, 2)[:2] + cell(stage_1, 0, 1)[:2]
        tensor += group(transpose_d, 2)[2:] + cell(stage_1, 0, 1)[2:]
        tensor += group(transpose_d, 3) + cell(stage_1, 0, 2) + cell(stage_1, 0, 3)
        tensor += half_cell(1, 0, 0) + half_cell(1, 1, 0) + [(open_1, 0, t, W + HALF, HALF) for t in (0, 2)]
        tensor += half_cell(1, 0, 1) + half_cell(1, 1, 1)
        tensor += cell(stage_1, 1, 2) + cell(stage_1, 1, 3)
        for g in range(G - 1):
            tensor += cell(stage_1, 2, g)
        tensor += blocks(0)[:1] + cell(stage_1, *STEPPED)[:2] + blocks(0)[1:2] + cell(stage_1, *STEPPED)[2:]
        tensor += blocks(0)[2:]
        for c, n in ((W, W), (2 * W, HALF), (2 * W + HALF, HALF)):
            tensor += [(stage_2, f, c, n, g, g + 1) for g in range(G) for f in range(2)]
            tensor += [(stage_2, f, c, n, 0, G) for f in range(2, R)]
        tensor[-1:] = [(stage_2, R - 1, c, QUARTER, 0, G) for c in (A - HALF, A - QUARTER)]

        empty = [reader(job) for job in tensor if fills_bank(job)]
        for pair, ahead in ((cell(weigh, 0, 1)[:2], 2), (cell(weigh, 0, 1)[2:], T)):
            k = empty.index(pair[0])
            empty[k : k + 2 + ahead] = empty[k + 2 : k + 2 + ahead] + pair
        freed = [job for job in empty if job in [takes(other)[1] for other in tensor]]

        last_copies = empty[-4::2]
        helped = cell(weigh, 0, 3)[3:]
        scalar = [job for job in empty if job[0] in (copy_d, weigh, store) and job not in last_copies + helped]
        scalar = planes(1, 0)[:3] + planes(0, 1)[2:] + planes(1, 1)[:3] + scalar[:2] + planes(1, 1)[3:] + scalar[2:]
        k = scalar.index(reader(blocks(1)[-1]))
        scalar[k:k] = [(interleave_wj,) + SHARED + (HALF, HALF)]

        steps = [(weights, k) for k in range(4)]
        vector = planes(0, 0) + planes(1, 0)[3:] + finish(0)[:1] + steps[:1] + planes(0, 1)[:2]
        vector += weave(steps[1:], [finish(0)[2], finish(0)[1]])
        vector += weave(singles(0), [finish(0)[3], finish(1)[0], finish(1)[1]]) + finish(1)[2:]
        vector += sorts(1)[1:] + pairs(1)[:1]
        vector += weave(sorts(2), [(interleave_wj, 0, 0, 0, HALF), (interleave_wj, 0, 0, HALF, QUARTER)])
        vector += weave(pairs(1)[1:] + pairs(2)[:1], sorts(3))
        vector += planes(2, 0) + pairs(2)[1:] + planes(2, 1) + pairs(3)[:1]
        vector += finish(2)[:2] + pairs(3)[1:] + finish(2)[2:]
        vector += planes(3, 0) + planes(3, 1) + finish(3) + helped + planes(4, 0) + planes(4, 1) + finish(4)
        for j, c, n in ((0, 0, W), (1, 0, W), (2, 0, HALF), (2, HALF, HALF)):
            interleave = [(interleave_wj, j, g, c, n) for g in range(G)]
            if j == 0:
                interleave[0] = (interleave_wj, 0, 0, W - QUARTER, QUARTER)
            quantize = [(quantize_wj, j, g, c, n) for g in range(G)]
            vector += [job for job in interleave[:1] + weave(interleave[1:], quantize) if job not in scalar]
        vector += last_copies

        lists = {"tensor": tensor, "scalar": scalar, "vector": vector}
        position = {engine: 0 for engine in lists}
        written = set()
        taken = {name: [] for name in DEPTH}
        taken["rows"] = [(key, (transpose_d, key[0], key[1] + d_raw[key].shape[1] - 1)) for key in d_raw]
        while any(position[engine] < len(lists[engine]) for engine in lists):
            before = len(written)
            for engine in lists:
                if position[engine] == len(lists[engine]):
                    continue
                job = lists[engine][position[engine]]
                if not all(other in written for other in needs(job)):
                    continue
                take = takes(job)
                if take is not None:
                    (name, index), last_reader = take
                    if name == "bank":
                        if last_reader not in held:
                            n = len(held) - BANKS
                            if n >= 0 and freed[n] not in written:
                                continue
                            made["next_bank"] = held[freed[n]] if n >= 0 else "bank_%d" % len(held)
                            held[last_reader] = made["next_bank"]
                    elif index not in [entry[0] for entry in taken[name]]:
                        if len(taken[name]) >= DEPTH[name] and taken[name][-DEPTH[name]][1] not in written:
                            continue
                        taken[name].append((index, last_reader))
                job[0](engine, *job[1:])
                written.add(job)
                position[engine] += 1
            assert len(written) > before
